import numpy as np
import ml_dtypes


def mxq(x, axis, fmt="e4m3"):
    dtype, down = {"e4m3": (ml_dtypes.float8_e4m3fn, 7), "e5m2": (ml_dtypes.float8_e5m2, 14)}[fmt]
    v = np.moveaxis(np.asarray(x, np.float32).astype(ml_dtypes.bfloat16).astype(np.float64), axis, -1)
    blocks = v.reshape(v.shape[:-1] + (-1, 32))
    amax = np.abs(blocks).max(-1, keepdims=True)
    byte = np.maximum(np.where(amax > 0, np.frexp(amax)[1] - 1 + 127, 0) - down, 1)
    scale = np.exp2(byte - 127.0)
    codes = (blocks / scale).astype(np.float32).astype(dtype).astype(np.float64)
    return np.moveaxis((codes * scale).reshape(v.shape), -1, axis)


WIDE = False


def mx_kscale(k):
    if not WIDE:
        return np.ones(k)
    levels = np.array([10, -10, 5, -5, 0])
    if k % 512:
        return np.exp2(np.random.permutation(np.resize(levels, k // 32))).repeat(32)
    a = np.empty((k // 512, 16))
    for p in range(k // 512):
        a[p, :8] = np.random.permutation(np.resize(levels, 8))
        for g in range(8):
            far = levels[np.abs(levels - a[p, g]) >= 10]
            a[p, g + 8] = far[np.random.randint(len(far))]
    return np.exp2(a.ravel()).repeat(32)


BF16 = ml_dtypes.bfloat16


def bf(x):
    return np.asarray(x, np.float32).astype(BF16)


def f64(x):
    return np.asarray(x).astype(np.float64)


M, N, D, R, F, H = 3, 1024, 512, 4, 512, 1024
RF = R * F


def draw0():
    s = mx_kscale(D)
    t = mx_kscale(F)
    return {
        "x": bf(np.random.standard_normal((M, N, D)) * s),
        "w": bf(np.random.standard_normal((M, D, RF)) / np.sqrt(D) / s[:, None]),
        "b": bf(0.5 * np.random.standard_normal((M, RF))),
        "omega": bf((0.5 + 0.1 * np.random.standard_normal((R, F))) * t[None, :]),
        "wo": bf(np.random.standard_normal((F, H)) / np.sqrt(F) / t[:, None]),
        "bo": bf(0.3 * np.random.standard_normal(H)),
    }


def project_modalities(x, w, b):
    h = mxq(x, 2, "e4m3") @ mxq(w, 1, "e4m3")
    return h + b[:, None, :]


def fuse_ranks(h, omega):
    p = h[0] * h[1] * h[2]
    p = p.reshape(p.shape[0], omega.shape[0], omega.shape[1])
    return np.sum(omega[None, :, :] * p, axis=1)


def core(x, w, b, omega, wo, bo):
    h = project_modalities(f64(x), f64(w), f64(b))
    z = fuse_ranks(h, f64(omega))
    y = (mxq(z, 1, "e4m3") @ mxq(f64(wo), 0, "e4m3")) + f64(bo)[None, :]
    return y


def e4m3fn_bytes(y):
    return np.clip(np.asarray(y, np.float64), -448.0, 448.0).astype(np.float32).astype(ml_dtypes.float8_e4m3fn).view(np.uint8)


def e4m3fn_values(b):
    return np.asarray(b, np.uint8).view(ml_dtypes.float8_e4m3fn).astype(np.float64)


def setup_inputs():
    d = draw0()
    x0 = np.asarray(d['w']).astype(np.float64)
    s = (np.max(np.abs(x0), axis=(0, 2), keepdims=True) / 448.0).astype(np.float32)
    out = {}
    for k, v in d.items():
        if k == 'w':
            out['w_bytes'] = e4m3fn_bytes(x0 / s.astype(np.float64))
            out['w_scale'] = s
        else:
            out[k] = v
    return out


def reference(x, w_bytes, w_scale, b, omega, wo, bo):
    return core(x, e4m3fn_values(w_bytes) * w_scale.astype(np.float64), b, omega, wo, bo)

@@ -1,0 +1,420 @@
+from contextlib import ExitStack
+
+import concourse.mybir as mybir
+from concourse.masks import make_identity
+
+F32 = mybir.dt.float32
+BF16 = mybir.dt.bfloat16
+U32 = mybir.dt.uint32
+U8 = mybir.dt.uint8
+FP8 = mybir.dt.float8_e4m3fn
+FP8X4 = mybir.dt.float8_e4m3fn_x4
+ACT = mybir.ActivationFunctionType
+ALU = mybir.AluOpType
+
+M, N, D, R, F, H = 3, 1024, 512, 4, 512, 1024
+FLOPS = 2 * M * N * D * R * F + 2 * N * F * H
+
+P = 128
+HALF = 512
+
+
+def tile_lowranktrimodalfusion_kernel(tc, x, w_bytes, w_scale, b, omega, wo, bo, out):
+    nc = tc.nc
+    with ExitStack() as ctx:
+        keep = ctx.enter_context(tc.tile_pool(name="keep", bufs=1))
+        stage = ctx.enter_context(tc.tile_pool(name="stage", bufs=3))
+        psum = ctx.enter_context(tc.psum_pool(name="psum", bufs=1))
+        ctx.enter_context(tc.manual_schedule())
+
+        ws = keep.tile([P, 4], F32, name="ws")
+        vec = keep.tile([P, F], BF16, name="vec")
+        nc.gpsimd.memset(vec[:], 0.0)
+        ident = keep.tile([P, P], F32, name="ident")
+        make_identity(nc, ident[:])
+
+        nc.scalar.dma_start(out=ws[:], in_=w_scale.rearrange("a (p j) o -> p (a j o)", j=4))
+        nc.scalar.dma_start(out=vec[0:12, :], in_=b.rearrange("m (r f) -> (m r) f", r=R))
+        nc.scalar.dma_start(out=vec[12:16, :], in_=omega)
+
+        w_first, w_rest, xr = [], [], {}
+        for m in range(M):
+            t0 = keep.tile([P, 4, F], U8, name="w_first%d" % m)
+            w_first.append(t0)
+            t1 = keep.tile([P, 4, 3 * F], U8, name="w_rest%d" % m)
+            w_rest.append(t1)
+            for half in range(2):
+                t2 = keep.tile([P, 4, D], BF16, name="xr%d%d" % (m, half))
+                xr[m, half] = t2
+        wo_raw = keep.tile([P, 4, H], BF16, name="wo_raw")
+        bo_sb = keep.tile([P, H], BF16, name="bo_sb")
+
+        def load_x(m, half):
+            src = x[m].rearrange("(p a) k -> p a k", a=8)
+            nc.sync.dma_start(out=xr[m, half][:], in_=src[:, 4 * half : 4 * half + 4, :])
+
+        for m in range(M):
+            src = w_bytes[m].rearrange("(p j) n -> p j n", j=4)
+            nc.sync.dma_start(out=w_first[m][:], in_=src[:, :, 0:F])
+            load_x(m, 0)
+        for m in range(M):
+            src = w_bytes[m].rearrange("(p j) n -> p j n", j=4)
+            nc.sync.dma_start(out=w_rest[m][:], in_=src[:, :, F:])
+        for m in range(M):
+            load_x(m, 1)
+        wo_rows = wo.rearrange("(g t i) n -> t g i n", t=4, i=4)
+        for t in range(4):
+            nc.sync.dma_start(out=wo_raw[:, t, :], in_=wo_rows[t])
+        nc.sync.dma_start(out=bo_sb[:], in_=bo.partition_broadcast(P))
+
+        xc, xs, wc, wsc = {}, {}, {}, {}
+        for m in range(M):
+            for half in range(2):
+                c = keep.tile([P, HALF], U32, name="xc%d%d" % (m, half), align_bytes=64)
+                s = keep.tile([P, HALF], U8, name="xs%d%d" % (m, half), align_bytes=64)
+                xc[m, half], xs[m, half] = c, s
+            for r in range(R):
+                c = keep.tile([P, F], U32, name="wc%d%d" % (m, r), align_bytes=64)
+                s = keep.tile([P, F], U8, name="wsc%d%d" % (m, r), align_bytes=64)
+                wc[m, r], wsc[m, r] = c, s
+        woc = keep.tile([P, H], U32, name="woc", align_bytes=64)
+        wos = keep.tile([P, H], U8, name="wos", align_bytes=64)
+        wog = keep.tile([P, H, 4], BF16, name="wog", align_bytes=64)
+        zacc = {}
+        for t in range(4):
+            z = keep.tile([P, HALF], F32, name="zacc%d" % t)
+            zacc[1, t] = z
+        zb, zg, zc, zs = {}, {}, {}, {}
+        for half in range(2):
+            t0 = keep.tile([P, 4, HALF], BF16, name="zb%d" % half)
+            t1 = keep.tile([P, HALF, 4], BF16, name="zg%d" % half, align_bytes=64)
+            t2 = keep.tile([P, HALF], U32, name="zc%d" % half, align_bytes=64)
+            t3 = keep.tile([P, HALF], U8, name="zs%d" % half, align_bytes=64)
+            zb[half], zg[half], zc[half], zs[half] = t0, t1, t2, t3
+
+        xt_of, xg_of = {}, {}
+
+        def x_turn(m, half, pair):
+            if pair == 0:
+                g = stage.tile([P, HALF, 4], BF16, name="xg", align_bytes=64)
+                xg_of[m, half] = g
+            xt = psum.tile([P, 2, 2, P], F32, name="aux" if half else ("h%d" if pair == 0 else "z%d") % m)
+            words = xr[m, half][:].rearrange("p a k -> p (a k)").bitcast(F32)
+            for i in range(2):
+                a = 2 * pair + i
+                for u in range(2):
+                    nc.tensor.transpose(xt[:, i, u, :], words[:, a * 256 + u : (a + 1) * 256 : 2], ident[:])
+            xt_of[m, half, pair] = xt
+
+        def x_out(m, half, pair, on_scalar):
+            dst = xg_of[m, half][:].rearrange("p n j -> p (n j)").bitcast(F32)
+            dst = dst[:, pair * 512 : (pair + 1) * 512].rearrange("p (a r u) -> p a r u", a=2, u=2)
+            src = xt_of[m, half, pair][:].rearrange("p a u r -> p a r u")
+            if on_scalar:
+                nc.scalar.copy(out=dst, in_=src)
+            else:
+                nc.vector.tensor_copy(out=dst, in_=src)
+
+        def x_quant(m, half):
+            nc.vector.quantize_mx(
+                out=xc[m, half][:].bitcast(FP8X4),
+                scales=xs[m, half][:],
+                in_=xg_of[m, half][:].rearrange("p n j -> p (n j)"),
+            )
+
+        wb_of, wg_of = {}, {}
+
+        def w_widen(m, r, j, on_scalar=True):
+            if j == 0:
+                t0 = stage.tile([P, 4, F], BF16, name="wb")
+                wb_of[m, r] = t0
+            src = w_first[m][:, j, :] if r == 0 else w_rest[m][:, j, (r - 1) * F : r * F]
+            if on_scalar:
+                nc.scalar.activation(
+                    out=wb_of[m, r][:, j, :], in_=src.bitcast(FP8), func=ACT.Copy, scale=ws[:, j : j + 1]
+                )
+            else:
+                nc.vector.tensor_scalar(
+                    out=wb_of[m, r][:, j, :], in0=src.bitcast(FP8), scalar1=ws[:, j : j + 1], scalar2=None, op0=ALU.mult
+                )
+
+        def w_weave(m, r, part):
+            if part == 0:
+                t0 = stage.tile([P, F, 4], BF16, name="wg", align_bytes=64)
+                wg_of[m, r] = t0
+            dst = wg_of[m, r][:].rearrange("p (t g i) j -> p g t j i", t=4, i=4)
+            src = wb_of[m, r][:].rearrange("p j (g t i) -> p g t j i", t=4, i=4)
+            gs = slice(part * 16, part * 16 + 16)
+            nc.vector.tensor_copy(out=dst[:, gs], in_=src[:, gs])
+
+        def w_quant(m, r):
+            nc.vector.quantize_mx(
+                out=wc[m, r][:].bitcast(FP8X4),
+                scales=wsc[m, r][:],
+                in_=wg_of[m, r][:].rearrange("p n j -> p (n j)"),
+            )
+
+        def wo_weave(part):
+            cs = slice(part * 512, part * 512 + 512)
+            dst = wog[:, cs, :].rearrange("p (c i) t -> p c t i", i=4)
+            src = wo_raw[:, :, cs].rearrange("p t (c i) -> p c t i", i=4)
+            nc.vector.tensor_copy(out=dst, in_=src)
+
+        def wo_quant(part):
+            cs = slice(part * 512, part * 512 + 512)
+            nc.vector.quantize_mx(
+                out=woc[:, cs].bitcast(FP8X4),
+                scales=wos[:, cs],
+                in_=wog[:, cs, :].rearrange("p n j -> p (n j)"),
+            )
+
+        ident_bf = keep.tile([P, P], BF16, name="ident_bf")
+        vecp = keep.tile([P, 4, P], BF16, name="vecp")
+        cols = keep.tile([P, 4, 16], F32, name="cols")
+        ob0 = keep.tile([P, 4, 4], F32, name="ob0")
+
+        def columns_a():
+            nc.vector.tensor_copy(out=ident_bf[:], in_=ident[:])
+            nc.vector.tensor_copy(
+                out=vecp[:].rearrange("p t (g i) -> p t g i", i=4),
+                in_=vec[:].rearrange("p (g t i) -> p t g i", t=4, i=4),
+            )
+
+        def columns_b():
+            vt = psum.tile([P, 4, P], BF16, name="aux")
+            for t in range(4):
+                nc.tensor.transpose(vt[:, t, :], vecp[:, t, :], ident_bf[:])
+            nc.vector.tensor_copy(out=cols[:], in_=vt[:, :, 0:16])
+
+        def columns_c():
+            nc.vector.tensor_tensor(out=ob0[:], in0=cols[:, :, 12:16], in1=cols[:, :, 0:4], op=ALU.mult)
+
+        units = [(0, r, t, 0, 512, "v") for r in range(R) for t in range(4)]
+        units += [(1, r, t, 0, 512, "g" if t % 2 else "v") for r in range(R - 1) for t in range(4)]
+        units += [(1, R - 1, t, c, 256, "v") for c in (0, 256) for t in range(4)]
+        zps = {}
+        hps, a_of, b_of, ab_of, pr_of = {}, {}, {}, {}, {}
+
+        def mm(u, m):
+            half, r, t, c0, w, mode = units[u]
+            h = psum.tile([P, 512], F32, name=("z%d" if u >= 21 and u % 2 else "h%d") % m)
+            hps[u, m] = h
+            nc.tensor.matmul_mx(
+                out=h[:, 0:w],
+                lhsT=wc[m, r][:, t * P : (t + 1) * P].bitcast(FP8X4),
+                lhsT_scale=wsc[m, r][:, t * P : (t + 1) * P],
+                rhs=xc[m, half][:, c0 : c0 + w].bitcast(FP8X4),
+                rhs_scale=xs[m, half][:, c0 : c0 + w],
+                start=True,
+                stop=True,
+            )
+
+        def first_factor(u):
+            half, r, t, c0, w, mode = units[u]
+            a = stage.tile([P, 512], F32, name="a")
+            a_of[u] = a
+            nc.scalar.activation(
+                out=a[:, 0:w],
+                in_=hps[u, 0][:, 0:w],
+                func=ACT.Identity,
+                scale=cols[:, t, 12 + r : 13 + r],
+                bias=ob0[:, t, r : r + 1],
+            )
+
+        def second_on_scalar(u):
+            half, r, t, c0, w, mode = units[u]
+            bb = stage.tile([P, 512], F32, name="bb")
+            b_of[u] = bb
+            nc.scalar.activation(
+                out=bb[:, 0:w], in_=hps[u, 1][:, 0:w], func=ACT.Identity, bias=cols[:, t, 4 + r : 5 + r]
+            )
+
+        def product_on_gpsimd(u):
+            half, r, t, c0, w, mode = units[u]
+            ab = stage.tile([P, 512], F32, name="ab")
+            ab_of[u] = ab
+            nc.gpsimd.tensor_tensor(out=ab[:, 0:w], in0=a_of[u][:, 0:w], in1=b_of[u][:, 0:w], op=ALU.mult)
+
+        def second_factor(u):
+            half, r, t, c0, w, mode = units[u]
+            ab = stage.tile([P, 512], F32, name="ab")
+            ab_of[u] = ab
+            nc.vector.scalar_tensor_tensor(
+                out=ab[:, 0:w], in0=hps[u, 1][:, 0:w], scalar=cols[:, t, 4 + r : 5 + r], in1=a_of[u][:, 0:w],
+                op0=ALU.add, op1=ALU.mult,
+            )
+
+        def third_factor(u):
+            half, r, t, c0, w, mode = units[u]
+            if half == 1 and r == 0:
+                dst = zacc[half, t][:, c0 : c0 + w]
+            else:
+                pr = stage.tile([P, 512], F32, name="pr")
+                pr_of[u] = pr
+                dst = pr[:, 0:w]
+            nc.vector.scalar_tensor_tensor(
+                out=dst, in0=hps[u, 2][:, 0:w], scalar=cols[:, t, 8 + r : 9 + r], in1=ab_of[u][:, 0:w],
+                op0=ALU.add, op1=ALU.mult,
+            )
+
+        def rank_sum(u, eng):
+            half, r, t, c0, w, mode = units[u]
+            if half == 0:
+                if r == 0:
+                    z_bank = psum.tile([P, 512], F32, name="z%d" % t)
+                    zps[t] = z_bank
+                nc.tensor.matmul(zps[t][:], lhsT=ident[:], rhs=pr_of[u][:], start=r == 0, stop=r == R - 1)
+                return
+            if r == 0:
+                return
+            z = zacc[half, t][:, c0 : c0 + w]
+            dst = z if r < R - 1 else zb[half][:, t, c0 : c0 + w]
+            eng.tensor_tensor(out=dst, in0=z, in1=pr_of[u][:, 0:w], op=ALU.add)
+
+        def z_out(t):
+            nc.scalar.copy(out=zb[0][:, t, :], in_=zps[t][:])
+
+        def z_weave(half, c0, w):
+            dst = zg[half][:, c0 : c0 + w, :].rearrange("p (c i) t -> p c t i", i=4)
+            src = zb[half][:, :, c0 : c0 + w].rearrange("p t (c i) -> p c t i", i=4)
+            nc.vector.tensor_copy(out=dst, in_=src)
+
+        def z_quant(half, c0, w):
+            nc.vector.quantize_mx(
+                out=zc[half][:, c0 : c0 + w].bitcast(FP8X4),
+                scales=zs[half][:, c0 : c0 + w],
+                in_=zg[half][:, c0 : c0 + w, :].rearrange("p n j -> p (n j)"),
+            )
+
+        out_rows = out.rearrange("(p a) h -> p a h", a=8)
+        osb_of, y_of = {}, {}
+
+        def out_mm(half, a, hh):
+            y = psum.tile([P, 512], F32, name="aux" if hh else "z3")
+            hs = slice(hh * 512, hh * 512 + 512)
+            ts = slice(a * P, (a + 1) * P)
+            nc.tensor.matmul_mx(
+                out=y[:],
+                lhsT=zc[half][:, ts].bitcast(FP8X4),
+                lhsT_scale=zs[half][:, ts],
+                rhs=woc[:, hs].bitcast(FP8X4),
+                rhs_scale=wos[:, hs],
+                start=True,
+                stop=True,
+            )
+            y_of[half, a, hh] = y
+
+        def out_tile(half, a, hh):
+            y = y_of[half, a, hh]
+            if hh == 0:
+                o = stage.tile([P, H], F32, name="o")
+                osb_of[half, a] = o
+            hs = slice(hh * 512, hh * 512 + 512)
+            nc.vector.tensor_tensor(out=osb_of[half, a][:, hs], in0=y[:], in1=bo_sb[:, hs], op=ALU.add)
+            if hh == 1:
+                nc.sync.dma_start(out=out_rows[:, 4 * half + a, :], in_=osb_of[half, a][:])
+
+        v_tasks, s_tasks, t_tasks = {}, {}, {}
+
+        def at(table, step, fn, *args):
+            table.setdefault(step, []).append((fn, args))
+
+        def go(tasks):
+            for fn, args in tasks:
+                fn(*args)
+
+        for m in range(M):
+            x_turn(m, 0, 0)
+            x_turn(m, 0, 1)
+        for j in range(4):
+            w_widen(0, 0, j)
+        x_out(0, 0, 0, False)
+        x_out(0, 0, 1, False)
+        x_out(1, 0, 0, False)
+        x_quant(0, 0)
+        w_weave(0, 0, 0)
+        w_weave(0, 0, 1)
+        for j in range(4):
+            w_widen(1, 0, j)
+        x_out(1, 0, 1, False)
+        w_quant(0, 0)
+        x_out(2, 0, 0, True)
+        columns_a()
+        columns_b()
+        x_quant(1, 0)
+        w_weave(1, 0, 0)
+        w_weave(1, 0, 1)
+        columns_c()
+        x_out(2, 0, 1, True)
+        for j in range(4):
+            w_widen(2, 0, j)
+        w_quant(1, 0)
+        x_quant(2, 0)
+        w_weave(2, 0, 0)
+        w_weave(2, 0, 1)
+        w_quant(2, 0)
+
+        for r in range(1, R):
+            base = 4 * r - 8
+            for i in range(12):
+                at(s_tasks, max(base + i // 3, -2), w_widen, i // 4, r, i % 4)
+            seq = []
+            for m in range(M):
+                seq += [(w_weave, m, r, 0), (w_weave, m, r, 1)]
+                if m:
+                    seq.insert(len(seq) - 1, (w_quant, m - 1, r))
+            seq.append((w_quant, M - 1, r))
+            for i, task in enumerate(seq):
+                at(v_tasks, max(base + 2 + i * 4 // 9, -1), *task)
+        for m in range(M):
+            for pair in range(2):
+                at(t_tasks, 7 + 2 * m + pair, x_turn, m, 1, pair)
+                at(s_tasks, 8 + 2 * m + pair, x_out, m, 1, pair, True)
+            at(v_tasks, 10 + 2 * m - (m == 2), x_quant, m, 1)
+        for t in range(4):
+            at(s_tasks, 16 + t // 2, z_out, t)
+        for part in range(2):
+            at(v_tasks, 14 + 2 * part, wo_weave, part)
+            at(v_tasks, 15 + 2 * part, wo_quant, part)
+        at(v_tasks, 18, z_weave, 0, 0, 512)
+        at(v_tasks, 19, z_quant, 0, 0, 512)
+        for a in range(4):
+            for hh in range(2):
+                at(t_tasks, 19 + 2 * a + hh, out_mm, 0, a, hh)
+                at(v_tasks, 20 + 2 * a + hh, out_tile, 0, a, hh)
+        last = len(units) - 1
+        at(v_tasks, last - 2, z_weave, 1, 0, 256)
+        at(v_tasks, last - 1, z_quant, 1, 0, 256)
+        for a in range(2):
+            for hh in range(2):
+                at(t_tasks, last - 1 + a, out_mm, 1, a, hh)
+                at(v_tasks, last + a, out_tile, 1, a, hh)
+        at(v_tasks, last + 1, z_weave, 1, 256, 256)
+        at(v_tasks, last + 1, z_quant, 1, 256, 256)
+        for a in range(2, 4):
+            for hh in range(2):
+                at(t_tasks, last + 2 + 2 * a + hh, out_mm, 1, a, hh)
+                at(v_tasks, last + 3 + 2 * a + hh, out_tile, 1, a, hh)
+
+        mm(0, 0)
+        for s in range(-2, last + 14):
+            if 0 <= s + 2 <= last:
+                first_factor(s + 2)
+                mm(s + 2, 1)
+                if units[s + 2][5] == "g":
+                    second_on_scalar(s + 2)
+            if 0 <= s + 1 <= last:
+                if units[s + 1][5] == "g":
+                    product_on_gpsimd(s + 1)
+                else:
+                    second_factor(s + 1)
+                mm(s + 1, 2)
+            if s + 3 <= last:
+                mm(s + 3, 0)
+            if 0 <= s <= last:
+                third_factor(s)
+            go(s_tasks.get(s, []))
+            go(v_tasks.get(s, []))
+            go(t_tasks.get(s, []))
+            if 0 <= s <= last:
+                rank_sum(s, nc.vector if s > last - 2 else nc.gpsimd)

@@ -17,6 +17,8 @@ FLOPS = 2 * M * N * D * R * F + 2 * N * F * H
 
 P = 128
 HALF = 512
+TILES = F // P
+G_RANKS = 4
 
 
 def tile_lowranktrimodalfusion_kernel(tc, x, w_bytes, w_scale, b, omega, wo, bo, out):
@@ -28,393 +30,368 @@ def tile_lowranktrimodalfusion_kernel(tc, x, w_bytes, w_scale, b, omega, wo, bo,
         ctx.enter_context(tc.manual_schedule())
 
         ws = keep.tile([P, 4], F32, name="ws")
-        vec = keep.tile([P, F], BF16, name="vec")
-        nc.gpsimd.memset(vec[:], 0.0)
+        vec = keep.tile([P, P], BF16, name="vec")
         ident = keep.tile([P, P], F32, name="ident")
+        nc.gpsimd.memset(vec[64:128, :], 0.0)
         make_identity(nc, ident[:])
 
-        nc.scalar.dma_start(out=ws[:], in_=w_scale.rearrange("a (p j) o -> p (a j o)", j=4))
-        nc.scalar.dma_start(out=vec[0:12, :], in_=b.rearrange("m (r f) -> (m r) f", r=R))
-        nc.scalar.dma_start(out=vec[12:16, :], in_=omega)
-
-        w_first, w_rest, xr = [], [], {}
+        w_raw, xr = {}, {}
+        for c in range(TILES):
+            for m in range(M):
+                t0 = keep.tile([P, 4, R, P], U8, name="w_raw%d%d" % (c, m))
+                w_raw[c, m] = t0
         for m in range(M):
-            t0 = keep.tile([P, 4, F], U8, name="w_first%d" % m)
-            w_first.append(t0)
-            t1 = keep.tile([P, 4, 3 * F], U8, name="w_rest%d" % m)
-            w_rest.append(t1)
             for half in range(2):
-                t2 = keep.tile([P, 4, D], BF16, name="xr%d%d" % (m, half))
-                xr[m, half] = t2
+                t1 = keep.tile([P, 4, D], BF16, name="xr%d%d" % (m, half))
+                xr[m, half] = t1
         wo_raw = keep.tile([P, 4, H], BF16, name="wo_raw")
         bo_sb = keep.tile([P, H], BF16, name="bo_sb")
+
+        def load_w(c, m):
+            src = w_bytes[m].rearrange("(p j) (r f) -> p (j r) f", j=4, r=R)
+            nc.sync.dma_start(
+                out=w_raw[c, m][:].rearrange("p j r f -> p (j r) f"), in_=src[:, :, c * P : (c + 1) * P]
+            )
 
         def load_x(m, half):
             src = x[m].rearrange("(p a) k -> p a k", a=8)
             nc.sync.dma_start(out=xr[m, half][:], in_=src[:, 4 * half : 4 * half + 4, :])
 
-        for m in range(M):
-            src = w_bytes[m].rearrange("(p j) n -> p j n", j=4)
-            nc.sync.dma_start(out=w_first[m][:], in_=src[:, :, 0:F])
-            load_x(m, 0)
-        for m in range(M):
-            src = w_bytes[m].rearrange("(p j) n -> p j n", j=4)
-            nc.sync.dma_start(out=w_rest[m][:], in_=src[:, :, F:])
+        nc.scalar.dma_start(out=ws[:], in_=w_scale.rearrange("a (p j) o -> p (a j o)", j=4))
+        nc.scalar.dma_start(out=vec[48:64, :], in_=omega.rearrange("r (c f) -> (r c) f", f=P))
+        nc.scalar.dma_start(out=vec[0:48, :], in_=b.rearrange("m (q f) -> (m q) f", f=P))
+        load_w(0, 0)
+        load_x(0, 0)
+        load_w(0, 1)
+        load_x(1, 0)
+        load_w(0, 2)
+        load_x(2, 0)
+        load_w(1, 0)
         for m in range(M):
             load_x(m, 1)
-        wo_rows = wo.rearrange("(g t i) n -> t g i n", t=4, i=4)
-        for t in range(4):
-            nc.sync.dma_start(out=wo_raw[:, t, :], in_=wo_rows[t])
+        load_w(1, 1)
+        load_w(1, 2)
+        for c in range(2, TILES):
+            for m in range(M):
+                load_w(c, m)
+        nc.sync.dma_start(out=wo_raw[:], in_=wo.rearrange("(p j) n -> p j n", j=4))
         nc.sync.dma_start(out=bo_sb[:], in_=bo.partition_broadcast(P))
 
-        xc, xs, wc, wsc = {}, {}, {}, {}
-        for m in range(M):
-            for half in range(2):
-                c = keep.tile([P, HALF], U32, name="xc%d%d" % (m, half), align_bytes=64)
-                s = keep.tile([P, HALF], U8, name="xs%d%d" % (m, half), align_bytes=64)
-                xc[m, half], xs[m, half] = c, s
-            for r in range(R):
-                c = keep.tile([P, F], U32, name="wc%d%d" % (m, r), align_bytes=64)
-                s = keep.tile([P, F], U8, name="wsc%d%d" % (m, r), align_bytes=64)
-                wc[m, r], wsc[m, r] = c, s
-        woc = keep.tile([P, H], U32, name="woc", align_bytes=64)
-        wos = keep.tile([P, H], U8, name="wos", align_bytes=64)
-        wog = keep.tile([P, H, 4], BF16, name="wog", align_bytes=64)
-        zacc = {}
-        for t in range(4):
-            z = keep.tile([P, HALF], F32, name="zacc%d" % t)
-            zacc[1, t] = z
-        zb, zg, zc, zs = {}, {}, {}, {}
-        for half in range(2):
-            t0 = keep.tile([P, 4, HALF], BF16, name="zb%d" % half)
-            t1 = keep.tile([P, HALF, 4], BF16, name="zg%d" % half, align_bytes=64)
-            t2 = keep.tile([P, HALF], U32, name="zc%d" % half, align_bytes=64)
-            t3 = keep.tile([P, HALF], U8, name="zs%d" % half, align_bytes=64)
-            zb[half], zg[half], zc[half], zs[half] = t0, t1, t2, t3
+        def codes(name, width):
+            c = keep.tile([P, width], U32, name=name + "c", align_bytes=64)
+            s = keep.tile([P, width], U8, name=name + "s", align_bytes=64)
+            return c, s
 
-        xt_of, xg_of = {}, {}
+        def quantize(dst, src):
+            nc.vector.quantize_mx(
+                out=dst[0][:].bitcast(FP8X4), scales=dst[1][:], in_=src[:].rearrange("p n j -> p (n j)")
+            )
 
-        def x_turn(m, half, pair):
+        def matmul(bank, lhs, lcols, rhs, rcols):
+            nc.tensor.matmul_mx(
+                out=bank,
+                lhsT=lhs[0][:, lcols].bitcast(FP8X4),
+                lhsT_scale=lhs[1][:, lcols],
+                rhs=rhs[0][:, rcols].bitcast(FP8X4),
+                rhs_scale=rhs[1][:, rcols],
+                start=True,
+                stop=True,
+            )
+
+        xq = {(m, half): codes("x%d%d" % (m, half), HALF) for m in range(M) for half in range(2)}
+        wq = {(c, m): codes("w%d%d" % (c, m), R * P) for c in range(TILES) for m in range(M)}
+        woq = [codes("wo%d" % part, 512) for part in range(2)]
+        zq = [codes("z%d" % half, HALF) for half in range(2)]
+
+        turned, grouped = {}, {}
+
+        def turn(key, rows, pair, bank, step):
             if pair == 0:
-                g = stage.tile([P, HALF, 4], BF16, name="xg", align_bytes=64)
-                xg_of[m, half] = g
-            xt = psum.tile([P, 2, 2, P], F32, name="aux" if half else ("h%d" if pair == 0 else "z%d") % m)
-            words = xr[m, half][:].rearrange("p a k -> p (a k)").bitcast(F32)
+                g = stage.tile([P, HALF, 4], BF16, name="grouped", align_bytes=64, bufs=4)
+                grouped[key] = g
+            t = psum.tile([P, 2, 2, P], F32, name=bank)
+            words = rows[:].rearrange("p a k -> p (a k)").bitcast(F32)
             for i in range(2):
-                a = 2 * pair + i
+                base = (2 * pair + i) * 256
                 for u in range(2):
-                    nc.tensor.transpose(xt[:, i, u, :], words[:, a * 256 + u : (a + 1) * 256 : 2], ident[:])
-            xt_of[m, half, pair] = xt
+                    src = words[:, base + u : base + 256 : 2] if step == 2 else words[:, base + u * P : base + (u + 1) * P]
+                    nc.tensor.transpose(t[:, i, u, :], src, ident[:])
+            turned[key, pair] = t
 
-        def x_out(m, half, pair, on_scalar):
-            dst = xg_of[m, half][:].rearrange("p n j -> p (n j)").bitcast(F32)
+        def turn_out(key, pair, on_scalar):
+            dst = grouped[key][:].rearrange("p n j -> p (n j)").bitcast(F32)
             dst = dst[:, pair * 512 : (pair + 1) * 512].rearrange("p (a r u) -> p a r u", a=2, u=2)
-            src = xt_of[m, half, pair][:].rearrange("p a u r -> p a r u")
+            src = turned[key, pair][:].rearrange("p a u r -> p a r u")
             if on_scalar:
                 nc.scalar.copy(out=dst, in_=src)
             else:
                 nc.vector.tensor_copy(out=dst, in_=src)
 
+        def x_turn(m, half, pair, bank):
+            turn((m, half), xr[m, half], pair, bank, 2)
+
         def x_quant(m, half):
-            nc.vector.quantize_mx(
-                out=xc[m, half][:].bitcast(FP8X4),
-                scales=xs[m, half][:],
-                in_=xg_of[m, half][:].rearrange("p n j -> p (n j)"),
-            )
+            quantize(xq[m, half], grouped[m, half])
 
-        wb_of, wg_of = {}, {}
+        planes, woven = {}, {}
 
-        def w_widen(m, r, j, on_scalar=True):
-            if j == 0:
-                t0 = stage.tile([P, 4, F], BF16, name="wb")
-                wb_of[m, r] = t0
-            src = w_first[m][:, j, :] if r == 0 else w_rest[m][:, j, (r - 1) * F : r * F]
+        def w_widen(c, m, j, on_scalar):
+            if (c, m) not in planes:
+                t0 = stage.tile([P, 4, R * P], BF16, name="planes", bufs=5)
+                planes[c, m] = t0
+            src = w_raw[c, m][:, j].rearrange("p r f -> p (r f)").bitcast(FP8)
             if on_scalar:
-                nc.scalar.activation(
-                    out=wb_of[m, r][:, j, :], in_=src.bitcast(FP8), func=ACT.Copy, scale=ws[:, j : j + 1]
-                )
+                nc.scalar.activation(out=planes[c, m][:, j, :], in_=src, func=ACT.Copy, scale=ws[:, j : j + 1])
             else:
                 nc.vector.tensor_scalar(
-                    out=wb_of[m, r][:, j, :], in0=src.bitcast(FP8), scalar1=ws[:, j : j + 1], scalar2=None, op0=ALU.mult
+                    out=planes[c, m][:, j, :], in0=src, scalar1=ws[:, j : j + 1], scalar2=None, op0=ALU.mult
                 )
 
-        def w_weave(m, r, part):
-            if part == 0:
-                t0 = stage.tile([P, F, 4], BF16, name="wg", align_bytes=64)
-                wg_of[m, r] = t0
-            dst = wg_of[m, r][:].rearrange("p (t g i) j -> p g t j i", t=4, i=4)
-            src = wb_of[m, r][:].rearrange("p j (g t i) -> p g t j i", t=4, i=4)
-            gs = slice(part * 16, part * 16 + 16)
-            nc.vector.tensor_copy(out=dst[:, gs], in_=src[:, gs])
+        def weave(key, src, cols, on_gpsimd):
+            if key not in woven:
+                t0 = stage.tile([P, 512, 4], BF16, name="woven", align_bytes=64, bufs=1)
+                woven[key] = t0
+            dst = woven[key][:, cols, :] if cols.start < 512 else woven[key][:, cols.start - 512 : cols.stop - 512, :]
+            if on_gpsimd:
+                nc.gpsimd.tensor_scalar(
+                    out=dst, in0=src[:, :, cols].rearrange("p j n -> p n j"), scalar1=1.0, scalar2=0.0,
+                    op0=ALU.mult, op1=ALU.add,
+                )
+            else:
+                nc.vector.tensor_copy(
+                    out=dst.rearrange("p (c i) j -> p c j i", i=4),
+                    in_=src[:, :, cols].rearrange("p j (c i) -> p c j i", i=4),
+                )
 
-        def w_quant(m, r):
-            nc.vector.quantize_mx(
-                out=wc[m, r][:].bitcast(FP8X4),
-                scales=wsc[m, r][:],
-                in_=wg_of[m, r][:].rearrange("p n j -> p (n j)"),
-            )
+        def w_weave(c, m, r0, r1, on_gpsimd):
+            weave((c, m), planes[c, m], slice(r0 * P, r1 * P), on_gpsimd)
+
+        def w_quant(c, m):
+            quantize(wq[c, m], woven[c, m])
 
         def wo_weave(part):
-            cs = slice(part * 512, part * 512 + 512)
-            dst = wog[:, cs, :].rearrange("p (c i) t -> p c t i", i=4)
-            src = wo_raw[:, :, cs].rearrange("p t (c i) -> p c t i", i=4)
-            nc.vector.tensor_copy(out=dst, in_=src)
+            weave(part, wo_raw, slice(part * 512, part * 512 + 512), True)
 
         def wo_quant(part):
-            cs = slice(part * 512, part * 512 + 512)
-            nc.vector.quantize_mx(
-                out=woc[:, cs].bitcast(FP8X4),
-                scales=wos[:, cs],
-                in_=wog[:, cs, :].rearrange("p n j -> p (n j)"),
-            )
+            quantize(woq[part], woven[part])
 
-        ident_bf = keep.tile([P, P], BF16, name="ident_bf")
-        vecp = keep.tile([P, 4, P], BF16, name="vecp")
-        cols = keep.tile([P, 4, 16], F32, name="cols")
-        ob0 = keep.tile([P, 4, 4], F32, name="ob0")
+        vec32 = keep.tile([P, P], F32, name="vec32")
+        cols = keep.tile([P, 64], F32, name="cols")
+        ob0 = keep.tile([P, 16], F32, name="ob0")
 
         def columns_a():
-            nc.vector.tensor_copy(out=ident_bf[:], in_=ident[:])
-            nc.vector.tensor_copy(
-                out=vecp[:].rearrange("p t (g i) -> p t g i", i=4),
-                in_=vec[:].rearrange("p (g t i) -> p t g i", t=4, i=4),
-            )
+            nc.vector.tensor_copy(out=vec32[:], in_=vec[:])
 
         def columns_b():
-            vt = psum.tile([P, 4, P], BF16, name="aux")
-            for t in range(4):
-                nc.tensor.transpose(vt[:, t, :], vecp[:, t, :], ident_bf[:])
-            nc.vector.tensor_copy(out=cols[:], in_=vt[:, :, 0:16])
+            vt = psum.tile([P, P], F32, name="aux")
+            nc.tensor.transpose(vt[:], vec32[:], ident[:])
+            nc.vector.tensor_copy(out=cols[:], in_=vt[:, 0:64])
 
         def columns_c():
-            nc.vector.tensor_tensor(out=ob0[:], in0=cols[:, :, 12:16], in1=cols[:, :, 0:4], op=ALU.mult)
+            nc.vector.tensor_tensor(out=ob0[:], in0=cols[:, 48:64], in1=cols[:, 0:16], op=ALU.mult)
 
-        units = [(0, r, t, 0, 512, "v") for r in range(R) for t in range(4)]
-        units += [(1, r, t, 0, 512, "g" if t % 2 else "v") for r in range(R - 1) for t in range(4)]
-        units += [(1, R - 1, t, c, 256, "v") for c in (0, 256) for t in range(4)]
-        zps = {}
-        hps, a_of, b_of, ab_of, pr_of = {}, {}, {}, {}, {}
+        def bias(m, r, c):
+            q = 16 * m + 4 * r + c
+            return cols[:, q : q + 1]
+
+        slots = [(c, h) for c in range(4) for h in range(2)]
+        units = [(c, half, r) for c, half in slots for r in range(R)]
+        last = len(units) - 1
+        by_gpsimd = ()
+        hps, a_of, b_of, ab_of, pr_of, zps = {}, {}, {}, {}, {}, {}
+        ztok = {}
+        for half in range(2):
+            t0 = keep.tile([P, 4, F], BF16, name="ztok%d" % half)
+            ztok[half] = t0
 
         def mm(u, m):
-            half, r, t, c0, w, mode = units[u]
-            h = psum.tile([P, 512], F32, name=("z%d" if u >= 21 and u % 2 else "h%d") % m)
+            c, half, r = units[u]
+            h = psum.tile([P, HALF], F32, name="h%d%d" % (m, u % 2))
             hps[u, m] = h
-            nc.tensor.matmul_mx(
-                out=h[:, 0:w],
-                lhsT=wc[m, r][:, t * P : (t + 1) * P].bitcast(FP8X4),
-                lhsT_scale=wsc[m, r][:, t * P : (t + 1) * P],
-                rhs=xc[m, half][:, c0 : c0 + w].bitcast(FP8X4),
-                rhs_scale=xs[m, half][:, c0 : c0 + w],
-                start=True,
-                stop=True,
-            )
+            matmul(h[:], wq[c, m], slice(r * P, (r + 1) * P), xq[m, half], slice(0, HALF))
 
         def first_factor(u):
-            half, r, t, c0, w, mode = units[u]
-            a = stage.tile([P, 512], F32, name="a")
+            c, half, r = units[u]
+            a = stage.tile([P, HALF], F32, name="a", bufs=4)
             a_of[u] = a
             nc.scalar.activation(
-                out=a[:, 0:w],
-                in_=hps[u, 0][:, 0:w],
-                func=ACT.Identity,
-                scale=cols[:, t, 12 + r : 13 + r],
-                bias=ob0[:, t, r : r + 1],
+                out=a[:], in_=hps[u, 0][:], func=ACT.Identity, scale=bias(3, r, c),
+                bias=ob0[:, 4 * r + c : 4 * r + c + 1],
             )
 
         def second_on_scalar(u):
-            half, r, t, c0, w, mode = units[u]
-            bb = stage.tile([P, 512], F32, name="bb")
+            c, half, r = units[u]
+            bb = stage.tile([P, HALF], F32, name="bb", bufs=2)
             b_of[u] = bb
-            nc.scalar.activation(
-                out=bb[:, 0:w], in_=hps[u, 1][:, 0:w], func=ACT.Identity, bias=cols[:, t, 4 + r : 5 + r]
-            )
-
-        def product_on_gpsimd(u):
-            half, r, t, c0, w, mode = units[u]
-            ab = stage.tile([P, 512], F32, name="ab")
-            ab_of[u] = ab
-            nc.gpsimd.tensor_tensor(out=ab[:, 0:w], in0=a_of[u][:, 0:w], in1=b_of[u][:, 0:w], op=ALU.mult)
+            nc.scalar.activation(out=bb[:], in_=hps[u, 1][:], func=ACT.Identity, bias=bias(1, r, c))
 
         def second_factor(u):
-            half, r, t, c0, w, mode = units[u]
-            ab = stage.tile([P, 512], F32, name="ab")
+            c, half, r = units[u]
+            ab = stage.tile([P, HALF], F32, name="ab")
             ab_of[u] = ab
-            nc.vector.scalar_tensor_tensor(
-                out=ab[:, 0:w], in0=hps[u, 1][:, 0:w], scalar=cols[:, t, 4 + r : 5 + r], in1=a_of[u][:, 0:w],
-                op0=ALU.add, op1=ALU.mult,
-            )
+            if u in by_gpsimd:
+                nc.gpsimd.tensor_tensor(out=ab[:], in0=a_of[u][:], in1=b_of[u][:], op=ALU.mult)
+            else:
+                nc.vector.scalar_tensor_tensor(
+                    out=ab[:], in0=hps[u, 1][:], scalar=bias(1, r, c), in1=a_of[u][:], op0=ALU.add, op1=ALU.mult
+                )
 
         def third_factor(u):
-            half, r, t, c0, w, mode = units[u]
-            if half == 1 and r == 0:
-                dst = zacc[half, t][:, c0 : c0 + w]
-            else:
-                pr = stage.tile([P, 512], F32, name="pr")
-                pr_of[u] = pr
-                dst = pr[:, 0:w]
+            c, half, r = units[u]
+            pr = stage.tile([P, HALF], F32, name="pr", bufs=5)
+            pr_of[u] = pr
             nc.vector.scalar_tensor_tensor(
-                out=dst, in0=hps[u, 2][:, 0:w], scalar=cols[:, t, 8 + r : 9 + r], in1=ab_of[u][:, 0:w],
-                op0=ALU.add, op1=ALU.mult,
+                out=pr[:], in0=hps[u, 2][:], scalar=bias(2, r, c), in1=ab_of[u][:], op0=ALU.add, op1=ALU.mult
             )
 
-        def rank_sum(u, eng):
-            half, r, t, c0, w, mode = units[u]
-            if half == 0:
-                if r == 0:
-                    z_bank = psum.tile([P, 512], F32, name="z%d" % t)
-                    zps[t] = z_bank
-                nc.tensor.matmul(zps[t][:], lhsT=ident[:], rhs=pr_of[u][:], start=r == 0, stop=r == R - 1)
-                return
+        def rank_sum(u):
+            c, half, r = units[u]
             if r == 0:
-                return
-            z = zacc[half, t][:, c0 : c0 + w]
-            dst = z if r < R - 1 else zb[half][:, t, c0 : c0 + w]
-            eng.tensor_tensor(out=dst, in0=z, in1=pr_of[u][:, 0:w], op=ALU.add)
+                z = psum.tile([P, 4, P], F32, name="z")
+                zps[c, half] = z
+            for a in range(4):
+                nc.tensor.matmul(
+                    zps[c, half][:, a, :], lhsT=pr_of[u][:, a * P : (a + 1) * P], rhs=ident[:], is_transpose=True,
+                    start=r == 0 and a == 0, stop=r == R - 1 and a == 3,
+                )
 
-        def z_out(t):
-            nc.scalar.copy(out=zb[0][:, t, :], in_=zps[t][:])
-
-        def z_weave(half, c0, w):
-            dst = zg[half][:, c0 : c0 + w, :].rearrange("p (c i) t -> p c t i", i=4)
-            src = zb[half][:, :, c0 : c0 + w].rearrange("p t (c i) -> p c t i", i=4)
-            nc.vector.tensor_copy(out=dst, in_=src)
-
-        def z_quant(half, c0, w):
-            nc.vector.quantize_mx(
-                out=zc[half][:, c0 : c0 + w].bitcast(FP8X4),
-                scales=zs[half][:, c0 : c0 + w],
-                in_=zg[half][:, c0 : c0 + w, :].rearrange("p n j -> p (n j)"),
+        def z_out(c, half):
+            dst = ztok[half][:].rearrange("p a (u q) -> p a u q", u=2)[:, :, :, 64 * c : 64 * c + 64]
+            nc.scalar.copy(
+                out=dst.rearrange("p a u (q e) -> p a u q e", e=2),
+                in_=zps[c, half][:].rearrange("p a (q u e) -> p a u q e", u=2, e=2),
             )
+
+        def z_turn(half, pair, bank):
+            turn(half, ztok[half], pair, bank, 1)
+
+        def z_quant(half):
+            quantize(zq[half], grouped[half])
 
         out_rows = out.rearrange("(p a) h -> p a h", a=8)
-        osb_of, y_of = {}, {}
+        y_of = {}
+        by_scalar = ()
 
-        def out_mm(half, a, hh):
-            y = psum.tile([P, 512], F32, name="aux" if hh else "z3")
-            hs = slice(hh * 512, hh * 512 + 512)
-            ts = slice(a * P, (a + 1) * P)
-            nc.tensor.matmul_mx(
-                out=y[:],
-                lhsT=zc[half][:, ts].bitcast(FP8X4),
-                lhsT_scale=zs[half][:, ts],
-                rhs=woc[:, hs].bitcast(FP8X4),
-                rhs_scale=wos[:, hs],
-                start=True,
-                stop=True,
-            )
-            y_of[half, a, hh] = y
+        def out_mm(half, a, part, bank):
+            y = psum.tile([P, 512], F32, name=bank)
+            matmul(y[:], zq[half], slice(a * P, (a + 1) * P), woq[part], slice(0, 512))
+            y_of[half, a, part] = y
 
-        def out_tile(half, a, hh):
-            y = y_of[half, a, hh]
-            if hh == 0:
-                o = stage.tile([P, H], F32, name="o")
-                osb_of[half, a] = o
-            hs = slice(hh * 512, hh * 512 + 512)
-            nc.vector.tensor_tensor(out=osb_of[half, a][:, hs], in0=y[:], in1=bo_sb[:, hs], op=ALU.add)
-            if hh == 1:
-                nc.sync.dma_start(out=out_rows[:, 4 * half + a, :], in_=osb_of[half, a][:])
+        def out_tile(half, a, part):
+            hs = slice(part * 512, part * 512 + 512)
+            o = stage.tile([P, 512], F32, name="o", bufs=12)
+            if (half, a, part) in by_scalar:
+                y = stage.tile([P, 512], F32, name="bb", bufs=2)
+                nc.scalar.copy(out=y[:], in_=y_of[half, a, part][:])
+                nc.gpsimd.tensor_tensor(out=o[:], in0=y[:], in1=bo_sb[:, hs], op=ALU.add)
+            else:
+                nc.vector.tensor_tensor(out=o[:], in0=y_of[half, a, part][:], in1=bo_sb[:, hs], op=ALU.add)
+            nc.sync.dma_start(out=out_rows[:, 4 * half + a, hs], in_=o[:])
 
-        v_tasks, s_tasks, t_tasks = {}, {}, {}
+        tasks = {}
 
-        def at(table, step, fn, *args):
-            table.setdefault(step, []).append((fn, args))
+        def at(step, fn, *args):
+            tasks.setdefault(step, []).append((fn, args))
 
-        def go(tasks):
-            for fn, args in tasks:
-                fn(*args)
-
-        for m in range(M):
-            x_turn(m, 0, 0)
-            x_turn(m, 0, 1)
+        banks = ["h00", "h01", "h10", "h11", "h20", "h21"]
         for j in range(4):
-            w_widen(0, 0, j)
-        x_out(0, 0, 0, False)
-        x_out(0, 0, 1, False)
-        x_out(1, 0, 0, False)
-        x_quant(0, 0)
-        w_weave(0, 0, 0)
-        w_weave(0, 0, 1)
-        for j in range(4):
-            w_widen(1, 0, j)
-        x_out(1, 0, 1, False)
-        w_quant(0, 0)
-        x_out(2, 0, 0, True)
+            w_widen(0, 0, j, False)
         columns_a()
         columns_b()
-        x_quant(1, 0)
-        w_weave(1, 0, 0)
-        w_weave(1, 0, 1)
-        columns_c()
-        x_out(2, 0, 1, True)
-        for j in range(4):
-            w_widen(2, 0, j)
-        w_quant(1, 0)
-        x_quant(2, 0)
-        w_weave(2, 0, 0)
-        w_weave(2, 0, 1)
-        w_quant(2, 0)
-
-        for r in range(1, R):
-            base = 4 * r - 8
-            for i in range(12):
-                at(s_tasks, max(base + i // 3, -2), w_widen, i // 4, r, i % 4)
-            seq = []
-            for m in range(M):
-                seq += [(w_weave, m, r, 0), (w_weave, m, r, 1)]
-                if m:
-                    seq.insert(len(seq) - 1, (w_quant, m - 1, r))
-            seq.append((w_quant, M - 1, r))
-            for i, task in enumerate(seq):
-                at(v_tasks, max(base + 2 + i * 4 // 9, -1), *task)
         for m in range(M):
             for pair in range(2):
-                at(t_tasks, 7 + 2 * m + pair, x_turn, m, 1, pair)
-                at(s_tasks, 8 + 2 * m + pair, x_out, m, 1, pair, True)
-            at(v_tasks, 10 + 2 * m - (m == 2), x_quant, m, 1)
-        for t in range(4):
-            at(s_tasks, 16 + t // 2, z_out, t)
-        for part in range(2):
-            at(v_tasks, 14 + 2 * part, wo_weave, part)
-            at(v_tasks, 15 + 2 * part, wo_quant, part)
-        at(v_tasks, 18, z_weave, 0, 0, 512)
-        at(v_tasks, 19, z_quant, 0, 0, 512)
-        for a in range(4):
-            for hh in range(2):
-                at(t_tasks, 19 + 2 * a + hh, out_mm, 0, a, hh)
-                at(v_tasks, 20 + 2 * a + hh, out_tile, 0, a, hh)
-        last = len(units) - 1
-        at(v_tasks, last - 2, z_weave, 1, 0, 256)
-        at(v_tasks, last - 1, z_quant, 1, 0, 256)
-        for a in range(2):
-            for hh in range(2):
-                at(t_tasks, last - 1 + a, out_mm, 1, a, hh)
-                at(v_tasks, last + a, out_tile, 1, a, hh)
-        at(v_tasks, last + 1, z_weave, 1, 256, 256)
-        at(v_tasks, last + 1, z_quant, 1, 256, 256)
-        for a in range(2, 4):
-            for hh in range(2):
-                at(t_tasks, last + 2 + 2 * a + hh, out_mm, 1, a, hh)
-                at(v_tasks, last + 3 + 2 * a + hh, out_tile, 1, a, hh)
+                x_turn(m, 0, pair, banks[2 * m + pair])
+        w_weave(0, 0, 0, R, False)
+        columns_c()
+        w_quant(0, 0)
+        for m in range(1, M):
+            for j in range(4):
+                w_widen(0, m, j, True)
+        for pair in range(2):
+            turn_out((0, 0), pair, False)
+        turn_out((1, 0), 0, False)
+        x_quant(0, 0)
+        turn_out((1, 0), 1, False)
+        w_weave(0, 1, 0, R, False)
+        x_quant(1, 0)
+        w_quant(0, 1)
+        w_weave(0, 2, 0, R, True)
+        for pair in range(2):
+            turn_out((2, 0), pair, False)
+        for j in range(4):
+            w_widen(1, 0, j, True)
+        x_turn(0, 1, 0, "aux")
+        x_turn(0, 1, 1, "z")
+        for pair in range(2):
+            turn_out((0, 1), pair, False)
+        x_turn(1, 1, 0, "h21")
+        x_turn(1, 1, 1, "h11")
+        x_quant(2, 0)
+        w_quant(0, 2)
+        w_weave(1, 0, 0, R, True)
+        x_quant(0, 1)
+        for pair in range(2):
+            turn_out((1, 1), pair, False)
+        x_turn(2, 1, 0, "aux")
+        x_turn(2, 1, 1, "z")
 
-        mm(0, 0)
-        for s in range(-2, last + 14):
+        pieces = [(c, m) for c in range(1, TILES) for m in range(M)]
+        due = [8 * i // 3 for i in range(len(pieces))]
+        planes_left = [(c, m, j) for c, m in pieces[1:] for j in range(4)]
+        for i, (c, m, j) in enumerate(planes_left):
+            at(-3 + 2 * i // 3, w_widen, c, m, j, True)
+        for pair in range(2):
+            at(-1 + pair, turn_out, (2, 1), pair, False)
+        at(due[0], x_quant, 1, 1)
+        at(due[1], x_quant, 2, 1)
+        for i, (c, m) in enumerate(pieces):
+            at(due[i], w_quant, c, m)
+            if i + 1 < len(pieces):
+                if G_RANKS < R:
+                    at(due[i], w_weave, *pieces[i + 1], G_RANKS, R, False)
+                at(due[i], w_weave, *pieces[i + 1], 0, G_RANKS, True)
+        at(due[-1], wo_weave, 0)
+        at(due[-1] + 3, wo_quant, 0)
+        at(due[-1] + 3, wo_weave, 1)
+        at(due[-1] + 6, wo_quant, 1)
+        for i, (c, half) in enumerate(slots):
+            at(4 * i + 6, z_out, c, half)
+        at(last - 1, z_turn, 0, 0, "aux")
+        at(last - 1, z_turn, 0, 1, "h00")
+        at(last - 1, turn_out, 0, 0, True)
+        at(last - 1, turn_out, 0, 1, True)
+        at(last + 1, z_quant, 0)
+        ring = ["h01", "h10", "h11", "h20", "h21"]
+        tiles = [(half, a, part) for half in range(2) for a in range(4) for part in range(2)]
+        for i, t in enumerate(tiles[:8]):
+            at(last + 2 + max(i - 4, 0), out_mm, *t, ring[i % 5])
+            at(last + 3 + i, out_tile, *t)
+        at(last + 3, z_turn, 1, 0, "aux")
+        at(last + 3, z_turn, 1, 1, "h00")
+        at(last + 4, turn_out, 1, 0, True)
+        at(last + 4, turn_out, 1, 1, True)
+        at(last + 8, z_quant, 1)
+        for i, t in enumerate(tiles[8:]):
+            at(last + 8 + i, out_mm, *t, ring[(i + 3) % 5])
+            at(last + 11 + i, out_tile, *t)
+
+        for s in range(-3, max(tasks) + 1):
             if 0 <= s + 2 <= last:
                 first_factor(s + 2)
-                mm(s + 2, 1)
-                if units[s + 2][5] == "g":
-                    second_on_scalar(s + 2)
+            if 0 <= s <= last:
+                second_factor(s)
             if 0 <= s + 1 <= last:
-                if units[s + 1][5] == "g":
-                    product_on_gpsimd(s + 1)
-                else:
-                    second_factor(s + 1)
-                mm(s + 1, 2)
-            if s + 3 <= last:
+                mm(s + 1, 1)
+                if s + 1 in by_gpsimd:
+                    second_on_scalar(s + 1)
+            if 0 <= s <= last:
+                mm(s, 2)
+            if 0 <= s - 1 <= last:
+                third_factor(s - 1)
+            if 0 <= s + 3 <= last:
                 mm(s + 3, 0)
-            if 0 <= s <= last:
-                third_factor(s)
-            go(s_tasks.get(s, []))
-            go(v_tasks.get(s, []))
-            go(t_tasks.get(s, []))
-            if 0 <= s <= last:
-                rank_sum(s, nc.vector if s > last - 2 else nc.gpsimd)
+            if 0 <= s - 2 <= last and s % 2:
+                rank_sum(s - 3)
+                rank_sum(s - 2)
+            for fn, args in tasks.get(s, []):
+                fn(*args)

@@ -18,7 +18,6 @@ FLOPS = 2 * M * N * D * R * F + 2 * N * F * H
 P = 128
 HALF = 512
 TILES = F // P
-G_RANKS = 4
 
 
 def tile_lowranktrimodalfusion_kernel(tc, x, w_bytes, w_scale, b, omega, wo, bo, out):
@@ -61,15 +60,16 @@ def tile_lowranktrimodalfusion_kernel(tc, x, w_bytes, w_scale, b, omega, wo, bo,
         nc.scalar.dma_start(out=vec[48:64, :], in_=omega.rearrange("r (c f) -> (r c) f", f=P))
         nc.scalar.dma_start(out=vec[0:48, :], in_=b.rearrange("m (q f) -> (m q) f", f=P))
         load_w(0, 0)
-        load_x(0, 0)
         load_w(0, 1)
-        load_x(1, 0)
+        load_x(0, 0)
         load_w(0, 2)
-        load_x(2, 0)
+        load_x(1, 0)
         load_w(1, 0)
-        for m in range(M):
-            load_x(m, 1)
+        load_x(2, 0)
+        load_x(0, 1)
         load_w(1, 1)
+        load_x(1, 1)
+        load_x(2, 1)
         load_w(1, 2)
         for c in range(2, TILES):
             for m in range(M):
@@ -101,7 +101,6 @@ def tile_lowranktrimodalfusion_kernel(tc, x, w_bytes, w_scale, b, omega, wo, bo,
         xq = {(m, half): codes("x%d%d" % (m, half), HALF) for m in range(M) for half in range(2)}
         wq = {(c, m): codes("w%d%d" % (c, m), R * P) for c in range(TILES) for m in range(M)}
         woq = [codes("wo%d" % part, 512) for part in range(2)]
-        zq = [codes("z%d" % half, HALF) for half in range(2)]
 
         turned, grouped = {}, {}
 
@@ -194,99 +193,114 @@ def tile_lowranktrimodalfusion_kernel(tc, x, w_bytes, w_scale, b, omega, wo, bo,
             q = 16 * m + 4 * r + c
             return cols[:, q : q + 1]
 
-        slots = [(c, h) for c in range(4) for h in range(2)]
-        units = [(c, half, r) for c, half in slots for r in range(R)]
+        groups = [(c, half, 0, 4) for c in range(TILES) for half in range(2)][:-1]
+        groups += [(TILES - 1, 1, a0, 2) for a0 in (0, 2)]
+        units = [(g, r) for g in groups for r in range(R)]
         last = len(units) - 1
-        by_gpsimd = ()
-        hps, a_of, b_of, ab_of, pr_of, zps = {}, {}, {}, {}, {}, {}
+        wide = 8 * TILES - R
+        hps, a_of, ab_of, pr_of, zps = {}, {}, {}, {}, {}
         ztok = {}
         for half in range(2):
             t0 = keep.tile([P, 4, F], BF16, name="ztok%d" % half)
             ztok[half] = t0
 
         def mm(u, m):
-            c, half, r = units[u]
-            h = psum.tile([P, HALF], F32, name="h%d%d" % (m, u % 2))
-            hps[u, m] = h
-            matmul(h[:], wq[c, m], slice(r * P, (r + 1) * P), xq[m, half], slice(0, HALF))
+            (c, half, a0, na), r = units[u]
+            if u < wide or m == 0:
+                h = psum.tile([P, na * P], F32, name="h%d%d" % (m, u % 2))
+                hps[u, m] = h[:]
+            elif m == 1:
+                h = psum.tile([P, 2, na * P], F32, name=("h10", "h11", "h20", "h21")[u % 4])
+                hps[u, 1], hps[u, 2] = h[:, 0, :], h[:, 1, :]
+            matmul(hps[u, m], wq[c, m], slice(r * P, (r + 1) * P), xq[m, half], slice(a0 * P, (a0 + na) * P))
 
         def first_factor(u):
-            c, half, r = units[u]
-            a = stage.tile([P, HALF], F32, name="a", bufs=4)
+            (c, half, a0, na), r = units[u]
+            a = stage.tile([P, na * P], F32, name="a", bufs=4)
             a_of[u] = a
             nc.scalar.activation(
-                out=a[:], in_=hps[u, 0][:], func=ACT.Identity, scale=bias(3, r, c),
+                out=a[:], in_=hps[u, 0], func=ACT.Identity, scale=bias(3, r, c),
                 bias=ob0[:, 4 * r + c : 4 * r + c + 1],
             )
 
-        def second_on_scalar(u):
-            c, half, r = units[u]
-            bb = stage.tile([P, HALF], F32, name="bb", bufs=2)
-            b_of[u] = bb
-            nc.scalar.activation(out=bb[:], in_=hps[u, 1][:], func=ACT.Identity, bias=bias(1, r, c))
-
         def second_factor(u):
-            c, half, r = units[u]
-            ab = stage.tile([P, HALF], F32, name="ab")
+            (c, half, a0, na), r = units[u]
+            ab = stage.tile([P, na * P], F32, name="ab")
             ab_of[u] = ab
-            if u in by_gpsimd:
-                nc.gpsimd.tensor_tensor(out=ab[:], in0=a_of[u][:], in1=b_of[u][:], op=ALU.mult)
-            else:
-                nc.vector.scalar_tensor_tensor(
-                    out=ab[:], in0=hps[u, 1][:], scalar=bias(1, r, c), in1=a_of[u][:], op0=ALU.add, op1=ALU.mult
-                )
+            nc.vector.scalar_tensor_tensor(
+                out=ab[:], in0=hps[u, 1], scalar=bias(1, r, c), in1=a_of[u][:], op0=ALU.add, op1=ALU.mult
+            )
 
         def third_factor(u):
-            c, half, r = units[u]
-            pr = stage.tile([P, HALF], F32, name="pr", bufs=5)
+            (c, half, a0, na), r = units[u]
+            pr = stage.tile([P, na * P], F32, name="pr", bufs=6)
             pr_of[u] = pr
             nc.vector.scalar_tensor_tensor(
-                out=pr[:], in0=hps[u, 2][:], scalar=bias(2, r, c), in1=ab_of[u][:], op0=ALU.add, op1=ALU.mult
+                out=pr[:], in0=hps[u, 2], scalar=bias(2, r, c), in1=ab_of[u][:], op0=ALU.add, op1=ALU.mult
             )
 
         def rank_sum(u):
-            c, half, r = units[u]
+            g, r = units[u]
+            na = g[3]
             if r == 0:
-                z = psum.tile([P, 4, P], F32, name="z")
-                zps[c, half] = z
-            for a in range(4):
+                z = psum.tile([P, na, P], F32, name="z")
+                zps[g] = z
+            for a in range(na):
                 nc.tensor.matmul(
-                    zps[c, half][:, a, :], lhsT=pr_of[u][:, a * P : (a + 1) * P], rhs=ident[:], is_transpose=True,
-                    start=r == 0 and a == 0, stop=r == R - 1 and a == 3,
+                    zps[g][:, a, :], lhsT=pr_of[u][:, a * P : (a + 1) * P], rhs=ident[:], is_transpose=True,
+                    start=r == 0 and a == 0, stop=r == R - 1 and a == na - 1,
                 )
 
-        def z_out(c, half):
-            dst = ztok[half][:].rearrange("p a (u q) -> p a u q", u=2)[:, :, :, 64 * c : 64 * c + 64]
+        def z_out(g):
+            c, half, a0, na = g
+            dst = ztok[half][:, a0 : a0 + na, :].rearrange("p a (u q) -> p a u q", u=2)[:, :, :, 64 * c : 64 * c + 64]
             nc.scalar.copy(
                 out=dst.rearrange("p a u (q e) -> p a u q e", e=2),
-                in_=zps[c, half][:].rearrange("p a (q u e) -> p a u q e", u=2, e=2),
+                in_=zps[g][:].rearrange("p a (q u e) -> p a u q e", u=2, e=2),
             )
 
-        def z_turn(half, pair, bank):
-            turn(half, ztok[half], pair, bank, 1)
+        zq = [codes("z%d" % q, 256) for q in range(4)]
+        z_turned, z_grouped = {}, {}
 
-        def z_quant(half):
-            quantize(zq[half], grouped[half])
+        def z_turn(q, bank):
+            t = psum.tile([P, 2, 2, P], F32, name=bank)
+            words = ztok[q // 2][:].rearrange("p a k -> p (a k)").bitcast(F32)
+            for i in range(4):
+                base = (4 * (q % 2) + i) * P
+                nc.tensor.transpose(t[:, i // 2, i % 2, :], words[:, base : base + P], ident[:])
+            z_turned[q] = t
+
+        def z_turn_out(q):
+            g = stage.tile([P, 256, 4], BF16, name="z_grouped", align_bytes=64, bufs=2)
+            z_grouped[q] = g
+            dst = g[:].rearrange("p n j -> p (n j)").bitcast(F32).rearrange("p (a r u) -> p a r u", a=2, u=2)
+            nc.scalar.copy(out=dst, in_=z_turned[q][:].rearrange("p a u r -> p a r u"))
+
+        def z_quant(q):
+            quantize(zq[q], z_grouped[q])
 
         out_rows = out.rearrange("(p a) h -> p a h", a=8)
-        y_of = {}
-        by_scalar = ()
+        y_of, o_of = {}, {}
 
-        def out_mm(half, a, part, bank):
+        def out_mm(q, i, bank):
             y = psum.tile([P, 512], F32, name=bank)
-            matmul(y[:], zq[half], slice(a * P, (a + 1) * P), woq[part], slice(0, 512))
-            y_of[half, a, part] = y
+            matmul(y[:], zq[q], slice(i % 2 * P, (i % 2 + 1) * P), woq[i // 2], slice(0, 512))
+            y_of[q, i] = y
 
-        def out_tile(half, a, part):
-            hs = slice(part * 512, part * 512 + 512)
-            o = stage.tile([P, 512], F32, name="o", bufs=12)
-            if (half, a, part) in by_scalar:
-                y = stage.tile([P, 512], F32, name="bb", bufs=2)
-                nc.scalar.copy(out=y[:], in_=y_of[half, a, part][:])
-                nc.gpsimd.tensor_tensor(out=o[:], in0=y[:], in1=bo_sb[:, hs], op=ALU.add)
+        def out_tile(q, i, on_vector):
+            hs = slice(i // 2 * 512, i // 2 * 512 + 512)
+            o = stage.tile([P, 512], F32, name="o", bufs=16)
+            if on_vector:
+                nc.vector.tensor_tensor(out=o[:], in0=y_of[q, i][:], in1=bo_sb[:, hs], op=ALU.add)
             else:
-                nc.vector.tensor_tensor(out=o[:], in0=y_of[half, a, part][:], in1=bo_sb[:, hs], op=ALU.add)
-            nc.sync.dma_start(out=out_rows[:, 4 * half + a, hs], in_=o[:])
+                y = stage.tile([P, 512], F32, name="y", bufs=3)
+                nc.scalar.copy(out=y[:], in_=y_of[q, i][:])
+                nc.gpsimd.tensor_tensor(out=o[:], in0=y[:], in1=bo_sb[:, hs], op=ALU.add)
+            o_of[q, i] = o
+
+        def store(q, i):
+            hs = slice(i // 2 * 512, i // 2 * 512 + 512)
+            nc.sync.dma_start(out=out_rows[:, 2 * q + i % 2, hs], in_=o_of[q, i][:])
 
         tasks = {}
 
@@ -296,84 +310,72 @@ def tile_lowranktrimodalfusion_kernel(tc, x, w_bytes, w_scale, b, omega, wo, bo,
         banks = ["h00", "h01", "h10", "h11", "h20", "h21"]
         for j in range(4):
             w_widen(0, 0, j, False)
+        w_weave(0, 0, 0, R, False)
         columns_a()
         columns_b()
         for m in range(M):
             for pair in range(2):
                 x_turn(m, 0, pair, banks[2 * m + pair])
-        w_weave(0, 0, 0, R, False)
-        columns_c()
         w_quant(0, 0)
-        for m in range(1, M):
+        for c, m in ((0, 1), (0, 2), (1, 0)):
             for j in range(4):
-                w_widen(0, m, j, True)
-        for pair in range(2):
-            turn_out((0, 0), pair, False)
-        turn_out((1, 0), 0, False)
-        x_quant(0, 0)
-        turn_out((1, 0), 1, False)
+                w_widen(c, m, j, True)
         w_weave(0, 1, 0, R, False)
-        x_quant(1, 0)
+        turn_out((0, 0), 0, False)
         w_quant(0, 1)
-        w_weave(0, 2, 0, R, True)
-        for pair in range(2):
-            turn_out((2, 0), pair, False)
-        for j in range(4):
-            w_widen(1, 0, j, True)
-        x_turn(0, 1, 0, "aux")
-        x_turn(0, 1, 1, "z")
-        for pair in range(2):
-            turn_out((0, 1), pair, False)
-        x_turn(1, 1, 0, "h21")
-        x_turn(1, 1, 1, "h11")
-        x_quant(2, 0)
+        turn_out((0, 0), 1, False)
+        columns_c()
+        w_weave(0, 2, 0, R, False)
+        x_quant(0, 0)
         w_quant(0, 2)
         w_weave(1, 0, 0, R, True)
+        x_turn(0, 1, 0, "aux")
+        x_turn(0, 1, 1, "z")
+        for key in ((1, 0), (2, 0), (0, 1)):
+            for pair in range(2):
+                turn_out(key, pair, False)
+        x_turn(1, 1, 0, "aux")
+        x_turn(1, 1, 1, "z")
+        x_turn(2, 1, 0, "h21")
+        x_quant(1, 0)
+        x_quant(2, 0)
         x_quant(0, 1)
-        for pair in range(2):
-            turn_out((1, 1), pair, False)
-        x_turn(2, 1, 0, "aux")
-        x_turn(2, 1, 1, "z")
-
         pieces = [(c, m) for c in range(1, TILES) for m in range(M)]
-        due = [8 * i // 3 for i in range(len(pieces))]
+        due = [3 * i - 2 for i in range(len(pieces))]
         planes_left = [(c, m, j) for c, m in pieces[1:] for j in range(4)]
-        for i, (c, m, j) in enumerate(planes_left):
-            at(-3 + 2 * i // 3, w_widen, c, m, j, True)
-        for pair in range(2):
-            at(-1 + pair, turn_out, (2, 1), pair, False)
-        at(due[0], x_quant, 1, 1)
-        at(due[1], x_quant, 2, 1)
+        for j in range(4):
+            w_widen(1, 1, j, True)
+        for i, (c, m, j) in enumerate(planes_left[4:]):
+            at(-2 + 21 * i // 28, w_widen, c, m, j, True)
         for i, (c, m) in enumerate(pieces):
+            if i == 1:
+                at(due[1], x_quant, 1, 1)
+                at(due[1], x_quant, 2, 1)
             at(due[i], w_quant, c, m)
             if i + 1 < len(pieces):
-                if G_RANKS < R:
-                    at(due[i], w_weave, *pieces[i + 1], G_RANKS, R, False)
-                at(due[i], w_weave, *pieces[i + 1], 0, G_RANKS, True)
+                at(due[i], w_weave, *pieces[i + 1], 0, R, True)
+        at(-2, turn_out, (1, 1), 0, False)
+        at(-2, x_turn, 2, 1, 1, "aux")
+        at(-1, turn_out, (1, 1), 1, False)
+        at(-1, turn_out, (2, 1), 0, False)
+        at(0, turn_out, (2, 1), 1, False)
         at(due[-1], wo_weave, 0)
         at(due[-1] + 3, wo_quant, 0)
         at(due[-1] + 3, wo_weave, 1)
-        at(due[-1] + 6, wo_quant, 1)
-        for i, (c, half) in enumerate(slots):
-            at(4 * i + 6, z_out, c, half)
-        at(last - 1, z_turn, 0, 0, "aux")
-        at(last - 1, z_turn, 0, 1, "h00")
-        at(last - 1, turn_out, 0, 0, True)
-        at(last - 1, turn_out, 0, 1, True)
-        at(last + 1, z_quant, 0)
-        ring = ["h01", "h10", "h11", "h20", "h21"]
-        tiles = [(half, a, part) for half in range(2) for a in range(4) for part in range(2)]
-        for i, t in enumerate(tiles[:8]):
-            at(last + 2 + max(i - 4, 0), out_mm, *t, ring[i % 5])
-            at(last + 3 + i, out_tile, *t)
-        at(last + 3, z_turn, 1, 0, "aux")
-        at(last + 3, z_turn, 1, 1, "h00")
-        at(last + 4, turn_out, 1, 0, True)
-        at(last + 4, turn_out, 1, 1, True)
-        at(last + 8, z_quant, 1)
-        for i, t in enumerate(tiles[8:]):
-            at(last + 8 + i, out_mm, *t, ring[(i + 3) % 5])
-            at(last + 11 + i, out_tile, *t)
+        at(due[-1] + 7, wo_quant, 1)
+        for i, g in enumerate(groups[:-1]):
+            at(4 * i + 6, z_out, g)
+        at(wide + 3, z_turn, 0, "aux")
+        at(wide + 4, z_turn_out, 0)
+        at(wide + 5, z_turn, 1, "aux")
+        at(wide + 6, z_quant, 0)
+        at(wide + 6, z_turn_out, 1)
+        at(last - 1, out_mm, 0, 0, "h00")
+        at(last, out_mm, 0, 1, "h01")
+        at(last, z_turn, 2, "aux")
+        at(last + 1, z_quant, 1)
+        at(last + 1, z_turn_out, 2)
+        at(last + 2, z_out, groups[-1])
 
         for s in range(-3, max(tasks) + 1):
             if 0 <= s + 2 <= last:
@@ -382,16 +384,40 @@ def tile_lowranktrimodalfusion_kernel(tc, x, w_bytes, w_scale, b, omega, wo, bo,
                 second_factor(s)
             if 0 <= s + 1 <= last:
                 mm(s + 1, 1)
-                if s + 1 in by_gpsimd:
-                    second_on_scalar(s + 1)
-            if 0 <= s <= last:
+                if s + 1 >= wide:
+                    mm(s + 1, 2)
+            if 0 <= s < wide:
                 mm(s, 2)
             if 0 <= s - 1 <= last:
                 third_factor(s - 1)
             if 0 <= s + 3 <= last:
                 mm(s + 3, 0)
-            if 0 <= s - 2 <= last and s % 2:
+            if 0 <= s - 2 < wide and s % 2:
                 rank_sum(s - 3)
                 rank_sum(s - 2)
+            if wide <= s - 2 <= last and s % 4 == 1:
+                for u in range(s - 5, s - 1):
+                    rank_sum(u)
             for fn, args in tasks.get(s, []):
                 fn(*args)
+
+        ring = ["h00", "h01", "h10", "h11", "h20", "h21"]
+        tiles = [(q, i) for q in range(4) for i in range(4)]
+        shared = ()
+        for k in range(2, 6):
+            out_mm(*tiles[k], ring[k])
+        for k, (q, i) in enumerate(tiles):
+            out_tile(q, i, k not in shared)
+            if k not in shared:
+                store(q, i)
+            if k - 3 in shared:
+                store(*tiles[k - 3])
+            if k == 0:
+                z_turn(3, "aux")
+                z_turn_out(3)
+            if k == 2:
+                z_quant(2)
+            if k == 5:
+                z_quant(3)
+            if k + 6 < 16:
+                out_mm(*tiles[k + 6], ring[k % 6])

@@ -59,21 +59,13 @@ def tile_lowranktrimodalfusion_kernel(tc, x, w_bytes, w_scale, b, omega, wo, bo,
         nc.scalar.dma_start(out=ws[:], in_=w_scale.rearrange("a (p j) o -> p (a j o)", j=4))
         nc.scalar.dma_start(out=vec[48:64, :], in_=omega.rearrange("r (c f) -> (r c) f", f=P))
         nc.scalar.dma_start(out=vec[0:48, :], in_=b.rearrange("m (q f) -> (m q) f", f=P))
+        order = [(c, m) for c in range(TILES) for m in range(M)]
         load_w(0, 0)
-        load_w(0, 1)
-        load_x(0, 0)
-        load_w(0, 2)
-        load_x(1, 0)
-        load_w(1, 0)
-        load_x(2, 0)
-        load_x(0, 1)
-        load_w(1, 1)
-        load_x(1, 1)
-        load_x(2, 1)
-        load_w(1, 2)
-        for c in range(2, TILES):
-            for m in range(M):
-                load_w(c, m)
+        for i in range(6):
+            load_w(*order[i + 1])
+            load_x(i % M, i // M)
+        for c, m in order[7:]:
+            load_w(c, m)
         nc.sync.dma_start(out=wo_raw[:], in_=wo.rearrange("(p j) n -> p j n", j=4))
         nc.sync.dma_start(out=bo_sb[:], in_=bo.partition_broadcast(P))
 
@@ -181,13 +173,16 @@ def tile_lowranktrimodalfusion_kernel(tc, x, w_bytes, w_scale, b, omega, wo, bo,
         def columns_a():
             nc.vector.tensor_copy(out=vec32[:], in_=vec[:])
 
+        vt = psum.tile([P, P], F32, name="aux")
+
         def columns_b():
-            vt = psum.tile([P, P], F32, name="aux")
             nc.tensor.transpose(vt[:], vec32[:], ident[:])
-            nc.vector.tensor_copy(out=cols[:], in_=vt[:, 0:64])
 
         def columns_c():
-            nc.vector.tensor_tensor(out=ob0[:], in0=cols[:, 48:64], in1=cols[:, 0:16], op=ALU.mult)
+            nc.vector.tensor_copy(out=cols[:], in_=vt[:, 0:64])
+
+        def columns_d():
+            nc.vector.tensor_tensor(out=ob0[:], in0=vt[:, 48:64], in1=cols[:, 0:16], op=ALU.mult)
 
         def bias(m, r, c):
             q = 16 * m + 4 * r + c
@@ -307,64 +302,76 @@ def tile_lowranktrimodalfusion_kernel(tc, x, w_bytes, w_scale, b, omega, wo, bo,
         def at(step, fn, *args):
             tasks.setdefault(step, []).append((fn, args))
 
-        banks = ["h00", "h01", "h10", "h11", "h20", "h21"]
         for j in range(4):
-            w_widen(0, 0, j, False)
+            w_widen(0, 0, j, j == 3)
         w_weave(0, 0, 0, R, False)
+        x_turn(0, 0, 0, "h00")
+        x_turn(0, 0, 1, "h01")
         columns_a()
-        columns_b()
-        for m in range(M):
-            for pair in range(2):
-                x_turn(m, 0, pair, banks[2 * m + pair])
         w_quant(0, 0)
-        for c, m in ((0, 1), (0, 2), (1, 0)):
+        columns_b()
+        x_turn(1, 0, 0, "h10")
+        x_turn(1, 0, 1, "h11")
+        for m in range(1, M):
             for j in range(4):
-                w_widen(c, m, j, True)
-        w_weave(0, 1, 0, R, False)
+                w_widen(0, m, j, True)
         turn_out((0, 0), 0, False)
-        w_quant(0, 1)
+        w_weave(0, 1, 0, R, False)
         turn_out((0, 0), 1, False)
         columns_c()
-        w_weave(0, 2, 0, R, False)
         x_quant(0, 0)
-        w_quant(0, 2)
-        w_weave(1, 0, 0, R, True)
-        x_turn(0, 1, 0, "aux")
-        x_turn(0, 1, 1, "z")
-        for key in ((1, 0), (2, 0), (0, 1)):
+        w_quant(0, 1)
+        w_weave(0, 2, 0, R, True)
+        x_turn(2, 0, 0, "h20")
+        x_turn(2, 0, 1, "h21")
+        mm(0, 0)
+        mm(1, 0)
+        for j in range(4):
+            w_widen(1, 0, j, True)
+        columns_d()
+        for key in ((1, 0), (2, 0)):
             for pair in range(2):
                 turn_out(key, pair, False)
-        x_turn(1, 1, 0, "aux")
-        x_turn(1, 1, 1, "z")
-        x_turn(2, 1, 0, "h21")
+        for u in range(2):
+            w_widen(1, 1, u, True)
+            first_factor(u)
+        x_turn(0, 1, 0, "aux")
+        x_turn(0, 1, 1, "z")
         x_quant(1, 0)
         x_quant(2, 0)
-        x_quant(0, 1)
+        w_quant(0, 2)
+        w_weave(1, 0, 0, R, True)
+        for pair in range(2):
+            turn_out((0, 1), pair, False)
+        for i, g in enumerate(groups[:-1]):
+            at(4 * i + 6, z_out, g)
         pieces = [(c, m) for c in range(1, TILES) for m in range(M)]
-        due = [3 * i - 2 for i in range(len(pieces))]
-        planes_left = [(c, m, j) for c, m in pieces[1:] for j in range(4)]
-        for j in range(4):
-            w_widen(1, 1, j, True)
-        for i, (c, m, j) in enumerate(planes_left[4:]):
-            at(-2 + 21 * i // 28, w_widen, c, m, j, True)
+        due = [0, 2] + [3 * i - 1 for i in range(2, len(pieces))]
+        on_vector = ()
+        planes_left = [(c, m, j) for c, m in pieces[1:] for j in range(4) if (c, m, j) not in on_vector][2:]
+        for i, (c, m, j) in enumerate(planes_left):
+            at(-1 + 22 * i // len(planes_left), w_widen, c, m, j, True)
+        at(-1, x_turn, 1, 1, 0, "aux")
+        at(-1, x_turn, 1, 1, 1, "z")
+        at(0, turn_out, (1, 1), 0, False)
+        at(0, turn_out, (1, 1), 1, True)
+        at(0, x_turn, 2, 1, 0, "aux")
+        at(1, x_turn, 2, 1, 1, "z")
+        at(1, turn_out, (2, 1), 0, False)
+        at(2, turn_out, (2, 1), 1, True)
+        at(due[0], x_quant, 0, 1)
+        at(due[1], x_quant, 1, 1)
+        at(due[1], x_quant, 2, 1)
         for i, (c, m) in enumerate(pieces):
-            if i == 1:
-                at(due[1], x_quant, 1, 1)
-                at(due[1], x_quant, 2, 1)
+            if i + 1 < len(pieces) and (*pieces[i + 1], 3) in on_vector:
+                at(due[i], w_widen, *pieces[i + 1], 3, False)
             at(due[i], w_quant, c, m)
             if i + 1 < len(pieces):
                 at(due[i], w_weave, *pieces[i + 1], 0, R, True)
-        at(-2, turn_out, (1, 1), 0, False)
-        at(-2, x_turn, 2, 1, 1, "aux")
-        at(-1, turn_out, (1, 1), 1, False)
-        at(-1, turn_out, (2, 1), 0, False)
-        at(0, turn_out, (2, 1), 1, False)
         at(due[-1], wo_weave, 0)
         at(due[-1] + 3, wo_quant, 0)
         at(due[-1] + 3, wo_weave, 1)
         at(due[-1] + 7, wo_quant, 1)
-        for i, g in enumerate(groups[:-1]):
-            at(4 * i + 6, z_out, g)
         at(wide + 3, z_turn, 0, "aux")
         at(wide + 4, z_turn_out, 0)
         at(wide + 5, z_turn, 1, "aux")
@@ -377,8 +384,8 @@ def tile_lowranktrimodalfusion_kernel(tc, x, w_bytes, w_scale, b, omega, wo, bo,
         at(last + 1, z_turn_out, 2)
         at(last + 2, z_out, groups[-1])
 
-        for s in range(-3, max(tasks) + 1):
-            if 0 <= s + 2 <= last:
+        for s in range(-1, max(tasks) + 1):
+            if 2 <= s + 2 <= last:
                 first_factor(s + 2)
             if 0 <= s <= last:
                 second_factor(s)

@@ -60,11 +60,10 @@ def tile_lowranktrimodalfusion_kernel(tc, x, w_bytes, w_scale, b, omega, wo, bo,
         nc.scalar.dma_start(out=vec[48:64, :], in_=omega.rearrange("r (c f) -> (r c) f", f=P))
         nc.scalar.dma_start(out=vec[0:48, :], in_=b.rearrange("m (q f) -> (m q) f", f=P))
         order = [(c, m) for c in range(TILES) for m in range(M)]
-        load_w(0, 0)
         for i in range(6):
-            load_w(*order[i + 1])
+            load_w(*order[i])
             load_x(i % M, i // M)
-        for c, m in order[7:]:
+        for c, m in order[6:]:
             load_w(c, m)
         nc.sync.dma_start(out=wo_raw[:], in_=wo.rearrange("(p j) n -> p j n", j=4))
         nc.sync.dma_start(out=bo_sb[:], in_=bo.partition_broadcast(P))
@@ -128,7 +127,7 @@ def tile_lowranktrimodalfusion_kernel(tc, x, w_bytes, w_scale, b, omega, wo, bo,
 
         def w_widen(c, m, j, on_scalar):
             if (c, m) not in planes:
-                t0 = stage.tile([P, 4, R * P], BF16, name="planes", bufs=5)
+                t0 = stage.tile([P, 4, R * P], BF16, name="planes", bufs=6)
                 planes[c, m] = t0
             src = w_raw[c, m][:, j].rearrange("p r f -> p (r f)").bitcast(FP8)
             if on_scalar:
@@ -246,12 +245,12 @@ def tile_lowranktrimodalfusion_kernel(tc, x, w_bytes, w_scale, b, omega, wo, bo,
                     start=r == 0 and a == 0, stop=r == R - 1 and a == na - 1,
                 )
 
-        def z_out(g):
-            c, half, a0, na = g
+        def z_out(g, a0, na):
+            c, half = g[:2]
             dst = ztok[half][:, a0 : a0 + na, :].rearrange("p a (u q) -> p a u q", u=2)[:, :, :, 64 * c : 64 * c + 64]
             nc.scalar.copy(
                 out=dst.rearrange("p a u (q e) -> p a u q e", e=2),
-                in_=zps[g][:].rearrange("p a (q u e) -> p a u q e", u=2, e=2),
+                in_=zps[g][:, a0 - g[2] : a0 - g[2] + na, :].rearrange("p a (q u e) -> p a u q e", u=2, e=2),
             )
 
         zq = [codes("z%d" % q, 256) for q in range(4)]
@@ -284,7 +283,7 @@ def tile_lowranktrimodalfusion_kernel(tc, x, w_bytes, w_scale, b, omega, wo, bo,
 
         def out_tile(q, i, on_vector):
             hs = slice(i // 2 * 512, i // 2 * 512 + 512)
-            o = stage.tile([P, 512], F32, name="o", bufs=16)
+            o = stage.tile([P, 512], F32, name="o", bufs=12)
             if on_vector:
                 nc.vector.tensor_tensor(out=o[:], in0=y_of[q, i][:], in1=bo_sb[:, hs], op=ALU.add)
             else:
@@ -302,55 +301,60 @@ def tile_lowranktrimodalfusion_kernel(tc, x, w_bytes, w_scale, b, omega, wo, bo,
         def at(step, fn, *args):
             tasks.setdefault(step, []).append((fn, args))
 
+        for i, g in enumerate(groups[:-3]):
+            at(4 * i + 6, z_out, g, 0, 4)
         for j in range(4):
-            w_widen(0, 0, j, j == 3)
+            w_widen(0, 0, j, j >= 3)
         w_weave(0, 0, 0, R, False)
         x_turn(0, 0, 0, "h00")
         x_turn(0, 0, 1, "h01")
         columns_a()
+        turn_out((0, 0), 0, True)
         w_quant(0, 0)
         columns_b()
         x_turn(1, 0, 0, "h10")
         x_turn(1, 0, 1, "h11")
+        turn_out((0, 0), 1, False)
         for m in range(1, M):
             for j in range(4):
-                w_widen(0, m, j, True)
-        turn_out((0, 0), 0, False)
-        w_weave(0, 1, 0, R, False)
-        turn_out((0, 0), 1, False)
+                w_widen(0, m, j, m == 2 or j >= 0)
         columns_c()
         x_quant(0, 0)
+        columns_d()
+        turn_out((1, 0), 0, False)
+        w_weave(0, 1, 0, R, False)
+        turn_out((1, 0), 1, False)
         w_quant(0, 1)
         w_weave(0, 2, 0, R, True)
-        x_turn(2, 0, 0, "h20")
-        x_turn(2, 0, 1, "h21")
+        x_quant(1, 0)
         mm(0, 0)
         mm(1, 0)
+        x_turn(2, 0, 0, "h20")
+        x_turn(2, 0, 1, "h21")
+        first_factor(0)
+        first_factor(1)
         for j in range(4):
             w_widen(1, 0, j, True)
-        columns_d()
-        for key in ((1, 0), (2, 0)):
-            for pair in range(2):
-                turn_out(key, pair, False)
+        mm(0, 1)
+        mm(1, 1)
+        for pair in range(2):
+            turn_out((2, 0), pair, False)
+            second_factor(pair)
         for u in range(2):
             w_widen(1, 1, u, True)
-            first_factor(u)
         x_turn(0, 1, 0, "aux")
         x_turn(0, 1, 1, "z")
-        x_quant(1, 0)
         x_quant(2, 0)
         w_quant(0, 2)
         w_weave(1, 0, 0, R, True)
         for pair in range(2):
             turn_out((0, 1), pair, False)
-        for i, g in enumerate(groups[:-1]):
-            at(4 * i + 6, z_out, g)
         pieces = [(c, m) for c in range(1, TILES) for m in range(M)]
         due = [0, 2] + [3 * i - 1 for i in range(2, len(pieces))]
         on_vector = ()
         planes_left = [(c, m, j) for c, m in pieces[1:] for j in range(4) if (c, m, j) not in on_vector][2:]
         for i, (c, m, j) in enumerate(planes_left):
-            at(-1 + 22 * i // len(planes_left), w_widen, c, m, j, True)
+            at(-1 + (i // 2 if i < 14 else 7 + (21 - 7) * (i - 14) // (len(planes_left) - 14)), w_widen, c, m, j, True)
         at(-1, x_turn, 1, 1, 0, "aux")
         at(-1, x_turn, 1, 1, 1, "z")
         at(0, turn_out, (1, 1), 0, False)
@@ -372,24 +376,28 @@ def tile_lowranktrimodalfusion_kernel(tc, x, w_bytes, w_scale, b, omega, wo, bo,
         at(due[-1] + 3, wo_quant, 0)
         at(due[-1] + 3, wo_weave, 1)
         at(due[-1] + 7, wo_quant, 1)
+        at(wide + 2, z_out, groups[-3], 0, 2)
+        at(wide + 2, z_out, groups[-3], 2, 2)
         at(wide + 3, z_turn, 0, "aux")
         at(wide + 4, z_turn_out, 0)
+        at(wide + 4, z_quant, 0)
         at(wide + 5, z_turn, 1, "aux")
-        at(wide + 6, z_quant, 0)
+        at(wide + 5, out_mm, 0, 0, "h00")
+        at(wide + 5, out_mm, 0, 1, "h01")
+        at(wide + 5, z_out, groups[-2], 0, 2)
         at(wide + 6, z_turn_out, 1)
-        at(last - 1, out_mm, 0, 0, "h00")
-        at(last, out_mm, 0, 1, "h01")
-        at(last, z_turn, 2, "aux")
+        at(wide + 6, out_tile, 0, 0, True)
+        at(wide + 6, store, 0, 0)
         at(last + 1, z_quant, 1)
-        at(last + 1, z_turn_out, 2)
-        at(last + 2, z_out, groups[-1])
+        at(last, z_turn, 2, "aux")
+        at(last, out_mm, 0, 2, "h10")
 
-        for s in range(-1, max(tasks) + 1):
+        for s in range(-1, last + 2):
             if 2 <= s + 2 <= last:
                 first_factor(s + 2)
-            if 0 <= s <= last:
+            if 2 <= s <= last:
                 second_factor(s)
-            if 0 <= s + 1 <= last:
+            if 2 <= s + 1 <= last:
                 mm(s + 1, 1)
                 if s + 1 >= wide:
                     mm(s + 1, 2)
@@ -402,29 +410,49 @@ def tile_lowranktrimodalfusion_kernel(tc, x, w_bytes, w_scale, b, omega, wo, bo,
             if 0 <= s - 2 < wide and s % 2:
                 rank_sum(s - 3)
                 rank_sum(s - 2)
-            if wide <= s - 2 <= last and s % 4 == 1:
+            if s == wide + 5:
                 for u in range(s - 5, s - 1):
                     rank_sum(u)
             for fn, args in tasks.get(s, []):
                 fn(*args)
 
-        ring = ["h00", "h01", "h10", "h11", "h20", "h21"]
-        tiles = [(q, i) for q in range(4) for i in range(4)]
-        shared = ()
-        for k in range(2, 6):
-            out_mm(*tiles[k], ring[k])
-        for k, (q, i) in enumerate(tiles):
-            out_tile(q, i, k not in shared)
-            if k not in shared:
+        def finish(q, i, on_vector=True):
+            out_tile(q, i, on_vector)
+            if on_vector:
                 store(q, i)
-            if k - 3 in shared:
-                store(*tiles[k - 3])
-            if k == 0:
-                z_turn(3, "aux")
-                z_turn_out(3)
-            if k == 2:
-                z_quant(2)
-            if k == 5:
-                z_quant(3)
-            if k + 6 < 16:
-                out_mm(*tiles[k + 6], ring[k % 6])
+
+        for u in range(last - 3, last + 1):
+            rank_sum(u)
+        z_turn_out(2)
+        for k, bank in enumerate(("h00", "h11", "h20", "h21")):
+            out_mm(k // 1 and 1, (k + 3) % 4, bank)
+        finish(0, 1)
+        z_out(groups[-1], 2, 2)
+        finish(0, 2)
+        z_quant(2)
+        finish(0, 3, False)
+        z_turn(3, "aux")
+        out_mm(1, 3, "h01")
+        out_mm(2, 0, "h10")
+        finish(1, 0)
+        finish(1, 1)
+        z_turn_out(3)
+        out_mm(2, 1, "h00")
+        out_mm(2, 2, "h11")
+        out_mm(2, 3, "h20")
+        finish(1, 2)
+        store(0, 3)
+        z_quant(3)
+        finish(1, 3, False)
+        finish(2, 1, False)
+        finish(2, 0)
+        for i, bank in enumerate(("h21", "aux", "h01", "h10")):
+            out_mm(3, i, bank)
+        finish(2, 2)
+        finish(3, 1, True)
+        finish(2, 3)
+        store(1, 3)
+        finish(3, 0)
+        finish(3, 2)
+        store(2, 1)
+        finish(3, 3)

@@ -91,7 +91,7 @@ def tile_lowranktrimodalfusion_kernel(tc, x, w_bytes, w_scale, b, omega, wo, bo,
 
         xq = {(m, half): codes("x%d%d" % (m, half), HALF) for m in range(M) for half in range(2)}
         wq = {(c, m): codes("w%d%d" % (c, m), R * P) for c in range(TILES) for m in range(M)}
-        woq = [codes("wo%d" % part, 512) for part in range(2)]
+        woq = codes("wo", H)
 
         turned, grouped = {}, {}
 
@@ -159,11 +159,16 @@ def tile_lowranktrimodalfusion_kernel(tc, x, w_bytes, w_scale, b, omega, wo, bo,
         def w_quant(c, m):
             quantize(wq[c, m], woven[c, m])
 
-        def wo_weave(part):
-            weave(part, wo_raw, slice(part * 512, part * 512 + 512), True)
+        def wo_weave():
+            wo_woven = stage.tile([P, H, 4], BF16, name="woven", align_bytes=64, bufs=1)
+            woven["wo"] = wo_woven
+            nc.gpsimd.tensor_scalar(
+                out=wo_woven[:], in0=wo_raw[:].rearrange("p j n -> p n j"), scalar1=1.0, scalar2=0.0,
+                op0=ALU.mult, op1=ALU.add,
+            )
 
-        def wo_quant(part):
-            quantize(woq[part], woven[part])
+        def wo_quant():
+            quantize(woq, woven["wo"])
 
         vec32 = keep.tile([P, P], F32, name="vec32")
         cols = keep.tile([P, 64], F32, name="cols")
@@ -278,7 +283,7 @@ def tile_lowranktrimodalfusion_kernel(tc, x, w_bytes, w_scale, b, omega, wo, bo,
 
         def out_mm(q, i, bank):
             y = psum.tile([P, 512], F32, name=bank)
-            matmul(y[:], zq[q], slice(i % 2 * P, (i % 2 + 1) * P), woq[i // 2], slice(0, 512))
+            matmul(y[:], zq[q], slice(i % 2 * P, (i % 2 + 1) * P), woq, slice(i // 2 * 512, i // 2 * 512 + 512))
             y_of[q, i] = y
 
         def out_tile(q, i, on_vector):
@@ -300,6 +305,11 @@ def tile_lowranktrimodalfusion_kernel(tc, x, w_bytes, w_scale, b, omega, wo, bo,
 
         def at(step, fn, *args):
             tasks.setdefault(step, []).append((fn, args))
+
+        halves = {}
+
+        def at_half(time, fn, *args):
+            (tasks if time % 2 else halves).setdefault(time // 2, []).append((fn, args))
 
         for i, g in enumerate(groups[:-3]):
             at(4 * i + 6, z_out, g, 0, 4)
@@ -344,38 +354,37 @@ def tile_lowranktrimodalfusion_kernel(tc, x, w_bytes, w_scale, b, omega, wo, bo,
             w_widen(1, 1, u, True)
         x_turn(0, 1, 0, "aux")
         x_turn(0, 1, 1, "z")
+        x_turn(1, 1, 0, "h21")
         x_quant(2, 0)
         w_quant(0, 2)
         w_weave(1, 0, 0, R, True)
         for pair in range(2):
             turn_out((0, 1), pair, False)
         pieces = [(c, m) for c in range(1, TILES) for m in range(M)]
-        due = [0, 2] + [3 * i - 1 for i in range(2, len(pieces))]
+        due = [3, 7, 13, 18, 24, 30, 36, 41, 47]
         on_vector = ()
+        at(-1, x_turn, 1, 1, 1, "aux")
+        at(-1, turn_out, (1, 1), 0, False)
+        at(0, turn_out, (1, 1), 1, False)
+        at(0, x_turn, 2, 1, 0, "z")
+        at(1, x_turn, 2, 1, 1, "aux")
+        at(2, turn_out, (2, 1), 0, False)
+        at(2, turn_out, (2, 1), 1, False)
         planes_left = [(c, m, j) for c, m in pieces[1:] for j in range(4) if (c, m, j) not in on_vector][2:]
         for i, (c, m, j) in enumerate(planes_left):
             at(-1 + (i // 2 if i < 14 else 7 + (21 - 7) * (i - 14) // (len(planes_left) - 14)), w_widen, c, m, j, True)
-        at(-1, x_turn, 1, 1, 0, "aux")
-        at(-1, x_turn, 1, 1, 1, "z")
-        at(0, turn_out, (1, 1), 0, False)
-        at(0, turn_out, (1, 1), 1, True)
-        at(0, x_turn, 2, 1, 0, "aux")
-        at(1, x_turn, 2, 1, 1, "z")
-        at(1, turn_out, (2, 1), 0, False)
-        at(2, turn_out, (2, 1), 1, True)
-        at(due[0], x_quant, 0, 1)
-        at(due[1], x_quant, 1, 1)
-        at(due[1], x_quant, 2, 1)
+        at(1, x_quant, 0, 1)
+        at(1, x_quant, 1, 1)
+        at(3, x_quant, 2, 1)
         for i, (c, m) in enumerate(pieces):
             if i + 1 < len(pieces) and (*pieces[i + 1], 3) in on_vector:
-                at(due[i], w_widen, *pieces[i + 1], 3, False)
-            at(due[i], w_quant, c, m)
+                at_half(due[i], w_widen, *pieces[i + 1], 3, False)
+            at_half(due[i], w_quant, c, m)
             if i + 1 < len(pieces):
-                at(due[i], w_weave, *pieces[i + 1], 0, R, True)
-        at(due[-1], wo_weave, 0)
-        at(due[-1] + 3, wo_quant, 0)
-        at(due[-1] + 3, wo_weave, 1)
-        at(due[-1] + 7, wo_quant, 1)
+                at_half(due[i], w_weave, *pieces[i + 1], 0, R, True)
+        at(1, mm, 4, 0)
+        at_half(due[-1], wo_weave)
+        at(wide + 1, wo_quant)
         at(wide + 2, z_out, groups[-3], 0, 2)
         at(wide + 2, z_out, groups[-3], 2, 2)
         at(wide + 3, z_turn, 0, "aux")
@@ -397,6 +406,8 @@ def tile_lowranktrimodalfusion_kernel(tc, x, w_bytes, w_scale, b, omega, wo, bo,
                 first_factor(s + 2)
             if 2 <= s <= last:
                 second_factor(s)
+            for fn, args in halves.get(s, []):
+                fn(*args)
             if 2 <= s + 1 <= last:
                 mm(s + 1, 1)
                 if s + 1 >= wide:
@@ -405,7 +416,7 @@ def tile_lowranktrimodalfusion_kernel(tc, x, w_bytes, w_scale, b, omega, wo, bo,
                 mm(s, 2)
             if 0 <= s - 1 <= last:
                 third_factor(s - 1)
-            if 0 <= s + 3 <= last:
+            if s + 3 <= last and s != 1:
                 mm(s + 3, 0)
             if 0 <= s - 2 < wide and s % 2:
                 rank_sum(s - 3)

@@ -368,7 +368,7 @@ def tile_lowranktrimodalfusion_kernel(tc, x, w_bytes, w_scale, b, omega, wo, bo,
         at(0, turn_out, (1, 1), 1, False)
         at(0, x_turn, 2, 1, 0, "z")
         at(1, x_turn, 2, 1, 1, "aux")
-        at(2, turn_out, (2, 1), 0, False)
+        at(2, turn_out, (2, 1), 0, True)
         at(2, turn_out, (2, 1), 1, False)
         planes_left = [(c, m, j) for c, m in pieces[1:] for j in range(4) if (c, m, j) not in on_vector][2:]
         for i, (c, m, j) in enumerate(planes_left):
@@ -384,24 +384,17 @@ def tile_lowranktrimodalfusion_kernel(tc, x, w_bytes, w_scale, b, omega, wo, bo,
                 at_half(due[i], w_weave, *pieces[i + 1], 0, R, True)
         at(1, mm, 4, 0)
         at_half(due[-1], wo_weave)
+        at(wide, rank_sum, wide - 2)
+        at(wide, rank_sum, wide - 1)
         at(wide + 1, wo_quant)
-        at(wide + 2, z_out, groups[-3], 0, 2)
+        at(wide + 1, z_out, groups[-3], 0, 2)
         at(wide + 2, z_out, groups[-3], 2, 2)
-        at(wide + 3, z_turn, 0, "aux")
-        at(wide + 4, z_turn_out, 0)
-        at(wide + 4, z_quant, 0)
-        at(wide + 5, z_turn, 1, "aux")
-        at(wide + 5, out_mm, 0, 0, "h00")
-        at(wide + 5, out_mm, 0, 1, "h01")
-        at(wide + 5, z_out, groups[-2], 0, 2)
-        at(wide + 6, z_turn_out, 1)
-        at(wide + 6, out_tile, 0, 0, True)
-        at(wide + 6, store, 0, 0)
-        at(last + 1, z_quant, 1)
-        at(last, z_turn, 2, "aux")
-        at(last, out_mm, 0, 2, "h10")
+        at(wide + 2, z_turn, 0, "aux")
+        at(wide + 2, z_turn_out, 0)
+        at_half(2 * wide + 8, z_quant, 0)
+        at(wide + 4, z_turn, 1, "aux")
 
-        for s in range(-1, last + 2):
+        for s in range(-1, wide + 5):
             if 2 <= s + 2 <= last:
                 first_factor(s + 2)
             if 2 <= s <= last:
@@ -418,12 +411,9 @@ def tile_lowranktrimodalfusion_kernel(tc, x, w_bytes, w_scale, b, omega, wo, bo,
                 third_factor(s - 1)
             if s + 3 <= last and s != 1:
                 mm(s + 3, 0)
-            if 0 <= s - 2 < wide and s % 2:
+            if 0 <= s - 2 < wide - 1 and s % 2:
                 rank_sum(s - 3)
                 rank_sum(s - 2)
-            if s == wide + 5:
-                for u in range(s - 5, s - 1):
-                    rank_sum(u)
             for fn, args in tasks.get(s, []):
                 fn(*args)
 
@@ -432,38 +422,64 @@ def tile_lowranktrimodalfusion_kernel(tc, x, w_bytes, w_scale, b, omega, wo, bo,
             if on_vector:
                 store(q, i)
 
-        for u in range(last - 3, last + 1):
+        first_factor(last)
+        z_turn_out(1)
+        out_mm(0, 0, "h00")
+        mm(last - 1, 1)
+        mm(last - 1, 2)
+        out_mm(0, 1, "h01")
+        mm(last, 1)
+        mm(last, 2)
+        second_factor(last - 2)
+        third_factor(last - 3)
+        out_mm(0, 2, "h10")
+        for u in range(wide, wide + R):
             rank_sum(u)
-        z_turn_out(2)
-        for k, bank in enumerate(("h00", "h11", "h20", "h21")):
-            out_mm(k // 1 and 1, (k + 3) % 4, bank)
-        finish(0, 1)
-        z_out(groups[-1], 2, 2)
+        finish(0, 1, False)
+        z_out(groups[-2], 0, 2)
+        finish(0, 0)
+        second_factor(last - 1)
+        z_quant(1)
         finish(0, 2)
-        z_quant(2)
-        finish(0, 3, False)
-        z_turn(3, "aux")
-        out_mm(1, 3, "h01")
-        out_mm(2, 0, "h10")
+        third_factor(last - 2)
+        store(0, 1)
+        out_mm(1, 0, "h00")
+        out_mm(1, 1, "h01")
+        out_mm(0, 3, "h11")
+        z_turn(2, "aux")
+        rank_sum(last - 3)
+        rank_sum(last - 2)
+        finish(1, 1, False)
+        z_turn_out(2)
+        second_factor(last)
+        third_factor(last - 1)
         finish(1, 0)
-        finish(1, 1)
-        z_turn_out(3)
-        out_mm(2, 1, "h00")
-        out_mm(2, 2, "h11")
-        out_mm(2, 3, "h20")
+        third_factor(last)
+        rank_sum(last - 1)
+        out_mm(1, 2, "h20")
+        rank_sum(last)
+        out_mm(1, 3, "h10")
+        z_out(groups[-1], 2, 2)
+        finish(0, 3)
+        store(1, 1)
+        z_quant(2)
         finish(1, 2)
-        store(0, 3)
-        z_quant(3)
-        finish(1, 3, False)
-        finish(2, 1, False)
+        out_mm(2, 0, "h11")
+        z_turn(3, "aux")
+        out_mm(2, 1, "h21")
+        out_mm(2, 2, "h00")
+        out_mm(2, 3, "h01")
+        finish(1, 3)
+        z_turn_out(3)
         finish(2, 0)
-        for i, bank in enumerate(("h21", "aux", "h01", "h10")):
+        finish(2, 3, False)
+        finish(2, 1)
+        z_quant(3)
+        for i, bank in enumerate(("h20", "h10", "aux", "h11")):
             out_mm(3, i, bank)
         finish(2, 2)
-        finish(3, 1, True)
-        finish(2, 3)
-        store(1, 3)
         finish(3, 0)
+        store(2, 3)
+        finish(3, 1)
         finish(3, 2)
-        store(2, 1)
         finish(3, 3)

@@ -16,8 +16,10 @@ M, N, D, R, F, H = 3, 1024, 512, 4, 512, 1024
 FLOPS = 2 * M * N * D * R * F + 2 * N * F * H
 
 P = 128
+PACK = 4
 HALF = 512
 TILES = F // P
+BANK = 512
 
 
 def tile_lowranktrimodalfusion_kernel(tc, x, w_bytes, w_scale, b, omega, wo, bo, out):
@@ -28,57 +30,58 @@ def tile_lowranktrimodalfusion_kernel(tc, x, w_bytes, w_scale, b, omega, wo, bo,
         psum = ctx.enter_context(tc.psum_pool(name="psum", bufs=1))
         ctx.enter_context(tc.manual_schedule())
 
-        ws = keep.tile([P, 4], F32, name="ws")
+        ws = keep.tile([P, PACK], F32, name="ws")
         vec = keep.tile([P, P], BF16, name="vec")
         ident = keep.tile([P, P], F32, name="ident")
         nc.gpsimd.memset(vec[64:128, :], 0.0)
         make_identity(nc, ident[:])
 
-        w_raw, xr = {}, {}
+        w_raw, x_raw = {}, {}
         for c in range(TILES):
             for m in range(M):
-                t0 = keep.tile([P, 4, R, P], U8, name="w_raw%d%d" % (c, m))
-                w_raw[c, m] = t0
+                t = keep.tile([P, PACK, R * P], U8, name="w_raw%d%d" % (c, m))
+                w_raw[c, m] = t
         for m in range(M):
             for half in range(2):
-                t1 = keep.tile([P, 4, D], BF16, name="xr%d%d" % (m, half))
-                xr[m, half] = t1
-        wo_raw = keep.tile([P, 4, H], BF16, name="wo_raw")
+                t = keep.tile([P, 4, D], BF16, name="x_raw%d%d" % (m, half))
+                x_raw[m, half] = t
+        wo_raw = keep.tile([P, PACK, H], BF16, name="wo_raw")
         bo_sb = keep.tile([P, H], BF16, name="bo_sb")
 
         def load_w(c, m):
-            src = w_bytes[m].rearrange("(p j) (r f) -> p (j r) f", j=4, r=R)
+            src = w_bytes[m].rearrange("(p j) (r f) -> p (j r) f", j=PACK, r=R)
             nc.sync.dma_start(
-                out=w_raw[c, m][:].rearrange("p j r f -> p (j r) f"), in_=src[:, :, c * P : (c + 1) * P]
+                out=w_raw[c, m][:].rearrange("p j (r f) -> p (j r) f", r=R), in_=src[:, :, c * P : (c + 1) * P]
             )
 
         def load_x(m, half):
             src = x[m].rearrange("(p a) k -> p a k", a=8)
-            nc.sync.dma_start(out=xr[m, half][:], in_=src[:, 4 * half : 4 * half + 4, :])
+            nc.sync.dma_start(out=x_raw[m, half][:], in_=src[:, 4 * half : 4 * half + 4, :])
 
-        nc.scalar.dma_start(out=ws[:], in_=w_scale.rearrange("a (p j) o -> p (a j o)", j=4))
+        nc.scalar.dma_start(out=ws[:], in_=w_scale.rearrange("a (p j) o -> p (a j o)", j=PACK))
         nc.scalar.dma_start(out=vec[48:64, :], in_=omega.rearrange("r (c f) -> (r c) f", f=P))
         nc.scalar.dma_start(out=vec[0:48, :], in_=b.rearrange("m (q f) -> (m q) f", f=P))
-        order = [(c, m) for c in range(TILES) for m in range(M)]
-        for i in range(6):
-            load_w(*order[i])
+        w_order = [(c, m) for c in range(TILES) for m in range(M)]
+        for i in range(2 * M):
+            load_w(*w_order[i])
             load_x(i % M, i // M)
-        for c, m in order[6:]:
+        for c, m in w_order[2 * M :]:
             load_w(c, m)
-        nc.sync.dma_start(out=wo_raw[:], in_=wo.rearrange("(p j) n -> p j n", j=4))
+        nc.sync.dma_start(out=wo_raw[:], in_=wo.rearrange("(p j) n -> p j n", j=PACK))
         nc.sync.dma_start(out=bo_sb[:], in_=bo.partition_broadcast(P))
 
-        def codes(name, width):
-            c = keep.tile([P, width], U32, name=name + "c", align_bytes=64)
-            s = keep.tile([P, width], U8, name=name + "s", align_bytes=64)
-            return c, s
+        def mx_operand(name, width):
+            codes = keep.tile([P, width], U32, name=name + "_codes", align_bytes=64)
+            scales = keep.tile([P, width], U8, name=name + "_scales", align_bytes=64)
+            return codes, scales
 
-        def quantize(dst, src):
+        def quantize(operand, src):
             nc.vector.quantize_mx(
-                out=dst[0][:].bitcast(FP8X4), scales=dst[1][:], in_=src[:].rearrange("p n j -> p (n j)")
+                out=operand[0][:].bitcast(FP8X4), scales=operand[1][:], in_=src[:].rearrange("p n j -> p (n j)")
             )
 
-        def matmul(bank, lhs, lcols, rhs, rcols):
+        def product(bank, lhs, lhs_from, rhs, rhs_from, width):
+            lcols, rcols = slice(lhs_from, lhs_from + P), slice(rhs_from, rhs_from + width)
             nc.tensor.matmul_mx(
                 out=bank,
                 lhsT=lhs[0][:, lcols].bitcast(FP8X4),
@@ -89,83 +92,70 @@ def tile_lowranktrimodalfusion_kernel(tc, x, w_bytes, w_scale, b, omega, wo, bo,
                 stop=True,
             )
 
-        xq = {(m, half): codes("x%d%d" % (m, half), HALF) for m in range(M) for half in range(2)}
-        wq = {(c, m): codes("w%d%d" % (c, m), R * P) for c in range(TILES) for m in range(M)}
-        woq = codes("wo", H)
+        xq = {(m, half): mx_operand("x%d%d" % (m, half), HALF) for m in range(M) for half in range(2)}
+        x_turned, x_grouped = {}, {}
 
-        turned, grouped = {}, {}
-
-        def turn(key, rows, pair, bank, step):
-            if pair == 0:
-                g = stage.tile([P, HALF, 4], BF16, name="grouped", align_bytes=64, bufs=4)
-                grouped[key] = g
+        def x_turn(m, half, pair, bank):
             t = psum.tile([P, 2, 2, P], F32, name=bank)
-            words = rows[:].rearrange("p a k -> p (a k)").bitcast(F32)
+            words = x_raw[m, half][:].rearrange("p a k -> p (a k)").bitcast(F32)
             for i in range(2):
                 base = (2 * pair + i) * 256
                 for u in range(2):
-                    src = words[:, base + u : base + 256 : 2] if step == 2 else words[:, base + u * P : base + (u + 1) * P]
-                    nc.tensor.transpose(t[:, i, u, :], src, ident[:])
-            turned[key, pair] = t
+                    nc.tensor.transpose(t[:, i, u, :], words[:, base + u : base + 256 : 2], ident[:])
+            x_turned[m, half, pair] = t
 
-        def turn_out(key, pair, on_scalar):
-            dst = grouped[key][:].rearrange("p n j -> p (n j)").bitcast(F32)
-            dst = dst[:, pair * 512 : (pair + 1) * 512].rearrange("p (a r u) -> p a r u", a=2, u=2)
-            src = turned[key, pair][:].rearrange("p a u r -> p a r u")
+        def x_out(m, half, pair, on_scalar=False):
+            if pair == 0:
+                g = stage.tile([P, HALF, PACK], BF16, name="x_grouped", align_bytes=64, bufs=4)
+                x_grouped[m, half] = g
+            dst = x_grouped[m, half][:].rearrange("p n j -> p (n j)").bitcast(F32)
+            dst = dst[:, pair * BANK : (pair + 1) * BANK].rearrange("p (a r u) -> p a r u", a=2, u=2)
+            src = x_turned[m, half, pair][:].rearrange("p a u r -> p a r u")
             if on_scalar:
                 nc.scalar.copy(out=dst, in_=src)
             else:
                 nc.vector.tensor_copy(out=dst, in_=src)
 
-        def x_turn(m, half, pair, bank):
-            turn((m, half), xr[m, half], pair, bank, 2)
-
         def x_quant(m, half):
-            quantize(xq[m, half], grouped[m, half])
+            quantize(xq[m, half], x_grouped[m, half])
 
+        pieces = [(c, m, 1) for c in range(TILES) for m in range(M)]
+        piece_of = {(c, m): (c, m0, count) for c, m0, count in pieces for m in range(m0, m0 + count)}
+        wq = {pc: mx_operand("w%d%d" % pc[:2], pc[2] * R * P) for pc in pieces}
+        woq = mx_operand("wo", H)
         planes, woven = {}, {}
 
-        def w_widen(c, m, j, on_scalar):
-            if (c, m) not in planes:
-                t0 = stage.tile([P, 4, R * P], BF16, name="planes", bufs=6)
-                planes[c, m] = t0
-            src = w_raw[c, m][:, j].rearrange("p r f -> p (r f)").bitcast(FP8)
+        def w_widen(c, m, j, on_scalar=True):
+            pc = piece_of[c, m]
+            if pc not in planes:
+                t = stage.tile([P, PACK, pc[2] * R * P], BF16, name="planes%d" % pc[2], bufs=6)
+                planes[pc] = t
+            dst = planes[pc][:, j, (m - pc[1]) * R * P : (m - pc[1] + 1) * R * P]
+            src = w_raw[c, m][:, j, :].bitcast(FP8)
             if on_scalar:
-                nc.scalar.activation(out=planes[c, m][:, j, :], in_=src, func=ACT.Copy, scale=ws[:, j : j + 1])
+                nc.scalar.activation(out=dst, in_=src, func=ACT.Copy, scale=ws[:, j : j + 1])
             else:
-                nc.vector.tensor_scalar(
-                    out=planes[c, m][:, j, :], in0=src, scalar1=ws[:, j : j + 1], scalar2=None, op0=ALU.mult
-                )
+                nc.vector.tensor_scalar(out=dst, in0=src, scalar1=ws[:, j : j + 1], scalar2=None, op0=ALU.mult)
 
-        def weave(key, src, cols, on_gpsimd):
-            if key not in woven:
-                t0 = stage.tile([P, 512, 4], BF16, name="woven", align_bytes=64, bufs=1)
-                woven[key] = t0
-            dst = woven[key][:, cols, :] if cols.start < 512 else woven[key][:, cols.start - 512 : cols.stop - 512, :]
+        def weave(key, src, width, on_gpsimd=True):
+            dst = stage.tile([P, width, PACK], BF16, name="woven", align_bytes=64, bufs=1)
+            woven[key] = dst
             if on_gpsimd:
                 nc.gpsimd.tensor_scalar(
-                    out=dst, in0=src[:, :, cols].rearrange("p j n -> p n j"), scalar1=1.0, scalar2=0.0,
+                    out=dst[:], in0=src[:].rearrange("p j n -> p n j"), scalar1=1.0, scalar2=0.0,
                     op0=ALU.mult, op1=ALU.add,
                 )
             else:
                 nc.vector.tensor_copy(
-                    out=dst.rearrange("p (c i) j -> p c j i", i=4),
-                    in_=src[:, :, cols].rearrange("p j (c i) -> p c j i", i=4),
+                    out=dst[:].rearrange("p (c i) j -> p c j i", i=4),
+                    in_=src[:].rearrange("p j (c i) -> p c j i", i=4),
                 )
 
-        def w_weave(c, m, r0, r1, on_gpsimd):
-            weave((c, m), planes[c, m], slice(r0 * P, r1 * P), on_gpsimd)
+        def w_weave(pc, on_gpsimd=True):
+            weave(pc, planes[pc], pc[2] * R * P, on_gpsimd)
 
-        def w_quant(c, m):
-            quantize(wq[c, m], woven[c, m])
-
-        def wo_weave():
-            wo_woven = stage.tile([P, H, 4], BF16, name="woven", align_bytes=64, bufs=1)
-            woven["wo"] = wo_woven
-            nc.gpsimd.tensor_scalar(
-                out=wo_woven[:], in0=wo_raw[:].rearrange("p j n -> p n j"), scalar1=1.0, scalar2=0.0,
-                op0=ALU.mult, op1=ALU.add,
-            )
+        def w_quant(pc):
+            quantize(wq[pc], woven[pc])
 
         def wo_quant():
             quantize(woq, woven["wo"])
@@ -173,23 +163,10 @@ def tile_lowranktrimodalfusion_kernel(tc, x, w_bytes, w_scale, b, omega, wo, bo,
         vec32 = keep.tile([P, P], F32, name="vec32")
         cols = keep.tile([P, 64], F32, name="cols")
         ob0 = keep.tile([P, 16], F32, name="ob0")
+        vec_turned = psum.tile([P, P], F32, name="aux")
 
-        def columns_a():
-            nc.vector.tensor_copy(out=vec32[:], in_=vec[:])
-
-        vt = psum.tile([P, P], F32, name="aux")
-
-        def columns_b():
-            nc.tensor.transpose(vt[:], vec32[:], ident[:])
-
-        def columns_c():
-            nc.vector.tensor_copy(out=cols[:], in_=vt[:, 0:64])
-
-        def columns_d():
-            nc.vector.tensor_tensor(out=ob0[:], in0=vt[:, 48:64], in1=cols[:, 0:16], op=ALU.mult)
-
-        def bias(m, r, c):
-            q = 16 * m + 4 * r + c
+        def column(row, r, c):
+            q = 16 * row + 4 * r + c
             return cols[:, q : q + 1]
 
         groups = [(c, half, 0, 4) for c in range(TILES) for half in range(2)][:-1]
@@ -197,28 +174,29 @@ def tile_lowranktrimodalfusion_kernel(tc, x, w_bytes, w_scale, b, omega, wo, bo,
         units = [(g, r) for g in groups for r in range(R)]
         last = len(units) - 1
         wide = 8 * TILES - R
-        hps, a_of, ab_of, pr_of, zps = {}, {}, {}, {}, {}
-        ztok = {}
+        h_of, a_of, ab_of, p_of, z_sum = {}, {}, {}, {}, {}
+        z_rows = {}
         for half in range(2):
-            t0 = keep.tile([P, 4, F], BF16, name="ztok%d" % half)
-            ztok[half] = t0
+            t = keep.tile([P, 4, F], BF16, name="z_rows%d" % half)
+            z_rows[half] = t
 
-        def mm(u, m):
+        def project(u, m):
             (c, half, a0, na), r = units[u]
             if u < wide or m == 0:
                 h = psum.tile([P, na * P], F32, name="h%d%d" % (m, u % 2))
-                hps[u, m] = h[:]
+                h_of[u, m] = h[:]
             elif m == 1:
                 h = psum.tile([P, 2, na * P], F32, name=("h10", "h11", "h20", "h21")[u % 4])
-                hps[u, 1], hps[u, 2] = h[:, 0, :], h[:, 1, :]
-            matmul(hps[u, m], wq[c, m], slice(r * P, (r + 1) * P), xq[m, half], slice(a0 * P, (a0 + na) * P))
+                h_of[u, 1], h_of[u, 2] = h[:, 0, :], h[:, 1, :]
+            pc = piece_of[c, m]
+            product(h_of[u, m], wq[pc], ((m - pc[1]) * R + r) * P, xq[m, half], a0 * P, na * P)
 
         def first_factor(u):
             (c, half, a0, na), r = units[u]
             a = stage.tile([P, na * P], F32, name="a", bufs=4)
             a_of[u] = a
             nc.scalar.activation(
-                out=a[:], in_=hps[u, 0], func=ACT.Identity, scale=bias(3, r, c),
+                out=a[:], in_=h_of[u, 0], func=ACT.Identity, scale=column(3, r, c),
                 bias=ob0[:, 4 * r + c : 4 * r + c + 1],
             )
 
@@ -227,15 +205,15 @@ def tile_lowranktrimodalfusion_kernel(tc, x, w_bytes, w_scale, b, omega, wo, bo,
             ab = stage.tile([P, na * P], F32, name="ab")
             ab_of[u] = ab
             nc.vector.scalar_tensor_tensor(
-                out=ab[:], in0=hps[u, 1], scalar=bias(1, r, c), in1=a_of[u][:], op0=ALU.add, op1=ALU.mult
+                out=ab[:], in0=h_of[u, 1], scalar=column(1, r, c), in1=a_of[u][:], op0=ALU.add, op1=ALU.mult
             )
 
         def third_factor(u):
             (c, half, a0, na), r = units[u]
-            pr = stage.tile([P, na * P], F32, name="pr", bufs=6)
-            pr_of[u] = pr
+            p = stage.tile([P, na * P], F32, name="p", bufs=6)
+            p_of[u] = p
             nc.vector.scalar_tensor_tensor(
-                out=pr[:], in0=hps[u, 2], scalar=bias(2, r, c), in1=ab_of[u][:], op0=ALU.add, op1=ALU.mult
+                out=p[:], in0=h_of[u, 2], scalar=column(2, r, c), in1=ab_of[u][:], op0=ALU.add, op1=ALU.mult
             )
 
         def rank_sum(u):
@@ -243,34 +221,35 @@ def tile_lowranktrimodalfusion_kernel(tc, x, w_bytes, w_scale, b, omega, wo, bo,
             na = g[3]
             if r == 0:
                 z = psum.tile([P, na, P], F32, name="z")
-                zps[g] = z
+                z_sum[g] = z
             for a in range(na):
                 nc.tensor.matmul(
-                    zps[g][:, a, :], lhsT=pr_of[u][:, a * P : (a + 1) * P], rhs=ident[:], is_transpose=True,
+                    z_sum[g][:, a, :], lhsT=p_of[u][:, a * P : (a + 1) * P], rhs=ident[:], is_transpose=True,
                     start=r == 0 and a == 0, stop=r == R - 1 and a == na - 1,
                 )
 
         def z_out(g, a0, na):
             c, half = g[:2]
-            dst = ztok[half][:, a0 : a0 + na, :].rearrange("p a (u q) -> p a u q", u=2)[:, :, :, 64 * c : 64 * c + 64]
+            dst = z_rows[half][:, a0 : a0 + na, :].rearrange("p a (u q) -> p a u q", u=2)[:, :, :, 64 * c : 64 * c + 64]
             nc.scalar.copy(
                 out=dst.rearrange("p a u (q e) -> p a u q e", e=2),
-                in_=zps[g][:, a0 - g[2] : a0 - g[2] + na, :].rearrange("p a (q u e) -> p a u q e", u=2, e=2),
+                in_=z_sum[g][:, a0 - g[2] : a0 - g[2] + na, :].rearrange("p a (q u e) -> p a u q e", u=2, e=2),
             )
 
-        zq = [codes("z%d" % q, 256) for q in range(4)]
-        z_turned, z_grouped = {}, {}
+        zq = [mx_operand("z%d" % q, 256) for q in range(4)]
+        z_turned, z_grouped, y_of, o_of = {}, {}, {}, {}
+        out_rows = out.rearrange("(p a) h -> p a h", a=8)
 
-        def z_turn(q, bank):
-            t = psum.tile([P, 2, 2, P], F32, name=bank)
-            words = ztok[q // 2][:].rearrange("p a k -> p (a k)").bitcast(F32)
+        def z_turn(q):
+            t = psum.tile([P, 2, 2, P], F32, name="aux")
+            words = z_rows[q // 2][:].rearrange("p a k -> p (a k)").bitcast(F32)
             for i in range(4):
                 base = (4 * (q % 2) + i) * P
                 nc.tensor.transpose(t[:, i // 2, i % 2, :], words[:, base : base + P], ident[:])
             z_turned[q] = t
 
         def z_turn_out(q):
-            g = stage.tile([P, 256, 4], BF16, name="z_grouped", align_bytes=64, bufs=2)
+            g = stage.tile([P, 256, PACK], BF16, name="z_grouped", align_bytes=64, bufs=2)
             z_grouped[q] = g
             dst = g[:].rearrange("p n j -> p (n j)").bitcast(F32).rearrange("p (a r u) -> p a r u", a=2, u=2)
             nc.scalar.copy(out=dst, in_=z_turned[q][:].rearrange("p a u r -> p a r u"))
@@ -278,161 +257,156 @@ def tile_lowranktrimodalfusion_kernel(tc, x, w_bytes, w_scale, b, omega, wo, bo,
         def z_quant(q):
             quantize(zq[q], z_grouped[q])
 
-        out_rows = out.rearrange("(p a) h -> p a h", a=8)
-        y_of, o_of = {}, {}
-
-        def out_mm(q, i, bank):
-            y = psum.tile([P, 512], F32, name=bank)
-            matmul(y[:], zq[q], slice(i % 2 * P, (i % 2 + 1) * P), woq, slice(i // 2 * 512, i // 2 * 512 + 512))
+        def out_product(q, i, bank):
+            y = psum.tile([P, BANK], F32, name=bank)
+            product(y[:], zq[q], i % 2 * P, woq, i // 2 * BANK, BANK)
             y_of[q, i] = y
 
-        def out_tile(q, i, on_vector):
-            hs = slice(i // 2 * 512, i // 2 * 512 + 512)
-            o = stage.tile([P, 512], F32, name="o", bufs=12)
-            if on_vector:
-                nc.vector.tensor_tensor(out=o[:], in0=y_of[q, i][:], in1=bo_sb[:, hs], op=ALU.add)
-            else:
-                y = stage.tile([P, 512], F32, name="y", bufs=3)
-                nc.scalar.copy(out=y[:], in_=y_of[q, i][:])
-                nc.gpsimd.tensor_tensor(out=o[:], in0=y[:], in1=bo_sb[:, hs], op=ALU.add)
-            o_of[q, i] = o
-
         def store(q, i):
-            hs = slice(i // 2 * 512, i // 2 * 512 + 512)
+            hs = slice(i // 2 * BANK, (i // 2 + 1) * BANK)
             nc.sync.dma_start(out=out_rows[:, 2 * q + i % 2, hs], in_=o_of[q, i][:])
 
-        tasks = {}
+        def finish(q, i, on_vector=True):
+            hs = slice(i // 2 * BANK, (i // 2 + 1) * BANK)
+            o = stage.tile([P, BANK], F32, name="o", bufs=12)
+            o_of[q, i] = o
+            if on_vector:
+                nc.vector.tensor_tensor(out=o[:], in0=y_of[q, i][:], in1=bo_sb[:, hs], op=ALU.add)
+                store(q, i)
+            else:
+                y = stage.tile([P, BANK], F32, name="y")
+                nc.scalar.copy(out=y[:], in_=y_of[q, i][:])
+                nc.gpsimd.tensor_tensor(out=o[:], in0=y[:], in1=bo_sb[:, hs], op=ALU.add)
 
-        def at(step, fn, *args):
-            tasks.setdefault(step, []).append((fn, args))
+        zeros = keep.tile([P, BANK], BF16, name="zeros")
+        unread = psum.tile([P, BANK], F32, name="z")
+        nc.vector.memset(zeros[:], 0.0)
 
-        halves = {}
+        def warm_up(count):
+            for i in range(count):
+                nc.tensor.matmul(unread[:], lhsT=zeros[:, 0:P], rhs=zeros[:], start=True, stop=True)
 
-        def at_half(time, fn, *args):
-            (tasks if time % 2 else halves).setdefault(time // 2, []).append((fn, args))
-
-        for i, g in enumerate(groups[:-3]):
-            at(4 * i + 6, z_out, g, 0, 4)
-        for j in range(4):
-            w_widen(0, 0, j, j >= 3)
-        w_weave(0, 0, 0, R, False)
+        warm_up(5)
+        for j in range(PACK):
+            w_widen(0, 0, j, j == 3)
+        w_weave(pieces[0], False)
         x_turn(0, 0, 0, "h00")
         x_turn(0, 0, 1, "h01")
-        columns_a()
-        turn_out((0, 0), 0, True)
-        w_quant(0, 0)
-        columns_b()
+        warm_up(2)
+        nc.vector.tensor_copy(out=vec32[:], in_=vec[:])
+        x_out(0, 0, 0, True)
+        w_quant(pieces[0])
+        nc.tensor.transpose(vec_turned[:], vec32[:], ident[:])
         x_turn(1, 0, 0, "h10")
         x_turn(1, 0, 1, "h11")
-        turn_out((0, 0), 1, False)
+        x_out(0, 0, 1)
         for m in range(1, M):
-            for j in range(4):
-                w_widen(0, m, j, m == 2 or j >= 0)
-        columns_c()
+            for j in range(PACK):
+                w_widen(0, m, j)
+        nc.vector.tensor_copy(out=cols[:], in_=vec_turned[:, 0:64])
         x_quant(0, 0)
-        columns_d()
-        turn_out((1, 0), 0, False)
-        w_weave(0, 1, 0, R, False)
-        turn_out((1, 0), 1, False)
-        w_quant(0, 1)
-        w_weave(0, 2, 0, R, True)
+        nc.vector.tensor_tensor(out=ob0[:], in0=vec_turned[:, 48:64], in1=cols[:, 0:16], op=ALU.mult)
+        x_out(1, 0, 0)
+        w_weave(pieces[1], False)
+        x_out(1, 0, 1)
+        w_quant(pieces[1])
+        w_weave(pieces[2])
         x_quant(1, 0)
-        mm(0, 0)
-        mm(1, 0)
+        project(0, 0)
+        project(1, 0)
         x_turn(2, 0, 0, "h20")
         x_turn(2, 0, 1, "h21")
         first_factor(0)
         first_factor(1)
-        for j in range(4):
-            w_widen(1, 0, j, True)
-        mm(0, 1)
-        mm(1, 1)
+        for j in range(PACK):
+            w_widen(1, 0, j)
+        project(0, 1)
+        project(1, 1)
         for pair in range(2):
-            turn_out((2, 0), pair, False)
+            x_out(2, 0, pair)
             second_factor(pair)
-        for u in range(2):
-            w_widen(1, 1, u, True)
+        for j in range(2):
+            w_widen(1, 1, j)
         x_turn(0, 1, 0, "aux")
         x_turn(0, 1, 1, "z")
         x_turn(1, 1, 0, "h21")
         x_quant(2, 0)
-        w_quant(0, 2)
-        w_weave(1, 0, 0, R, True)
+        w_quant(pieces[2])
+        w_weave(pieces[3])
         for pair in range(2):
-            turn_out((0, 1), pair, False)
-        pieces = [(c, m) for c in range(1, TILES) for m in range(M)]
-        due = [3, 7, 13, 18, 24, 30, 36, 41, 47]
-        on_vector = ()
+            x_out(0, 1, pair)
+
+        late, early = {}, {}
+
+        def at(time, fn, *args):
+            (late if time % 2 else early).setdefault(time // 2, []).append((fn, args))
+
+        for i, g in enumerate(groups[:-3]):
+            at(8 * i + 13, z_out, g, 0, 4)
         at(-1, x_turn, 1, 1, 1, "aux")
-        at(-1, turn_out, (1, 1), 0, False)
-        at(0, turn_out, (1, 1), 1, False)
-        at(0, x_turn, 2, 1, 0, "z")
-        at(1, x_turn, 2, 1, 1, "aux")
-        at(2, turn_out, (2, 1), 0, True)
-        at(2, turn_out, (2, 1), 1, False)
-        planes_left = [(c, m, j) for c, m in pieces[1:] for j in range(4) if (c, m, j) not in on_vector][2:]
+        at(-1, x_out, 1, 1, 0)
+        at(1, x_out, 1, 1, 1)
+        at(1, x_turn, 2, 1, 0, "z")
+        at(3, x_turn, 2, 1, 1, "aux")
+        at(5, x_out, 2, 1, 0, True)
+        at(5, x_out, 2, 1, 1)
+        planes_left = [(c, m, j) for c in range(1, TILES) for m in range(M) for j in range(PACK)][6:]
         for i, (c, m, j) in enumerate(planes_left):
-            at(-1 + (i // 2 if i < 14 else 7 + (21 - 7) * (i - 14) // (len(planes_left) - 14)), w_widen, c, m, j, True)
-        at(1, x_quant, 0, 1)
-        at(1, x_quant, 1, 1)
-        at(3, x_quant, 2, 1)
-        for i, (c, m) in enumerate(pieces):
-            if i + 1 < len(pieces) and (*pieces[i + 1], 3) in on_vector:
-                at_half(due[i], w_widen, *pieces[i + 1], 3, False)
-            at_half(due[i], w_quant, c, m)
-            if i + 1 < len(pieces):
-                at_half(due[i], w_weave, *pieces[i + 1], 0, R, True)
-        at(1, mm, 4, 0)
-        at_half(due[-1], wo_weave)
-        at(wide, rank_sum, wide - 2)
-        at(wide, rank_sum, wide - 1)
-        at(wide + 1, wo_quant)
-        at(wide + 1, z_out, groups[-3], 0, 2)
-        at(wide + 2, z_out, groups[-3], 2, 2)
-        at(wide + 2, z_turn, 0, "aux")
-        at(wide + 2, z_turn_out, 0)
-        at_half(2 * wide + 8, z_quant, 0)
-        at(wide + 4, z_turn, 1, "aux")
+            at(2 * (i // 2 if i < 14 else 7 + 14 * (i - 14) // 16) - 1, w_widen, c, m, j)
+        at(3, x_quant, 0, 1)
+        at(3, x_quant, 1, 1)
+        at(7, x_quant, 2, 1)
+        due = [3, 7, 13, 18, 24, 30, 36, 41, 47]
+        for i, pc in enumerate(pieces[3:]):
+            at(due[i], w_quant, pc)
+            if pc != pieces[-1]:
+                at(due[i], w_weave, pieces[i + 4])
+        at(3, project, 4, 0)
+        at(due[-1], weave, "wo", wo_raw, H)
+        at(2 * wide + 1, rank_sum, wide - 2)
+        at(2 * wide + 1, rank_sum, wide - 1)
+        at(2 * wide + 3, wo_quant)
+        at(2 * wide + 3, z_out, groups[-3], 0, 2)
+        at(2 * wide + 5, z_out, groups[-3], 2, 2)
+        at(2 * wide + 5, z_turn, 0)
+        at(2 * wide + 5, z_turn_out, 0)
+        at(2 * wide + 8, z_quant, 0)
+        at(2 * wide + 9, z_turn, 1)
 
         for s in range(-1, wide + 5):
-            if 2 <= s + 2 <= last:
+            if s >= 0:
                 first_factor(s + 2)
-            if 2 <= s <= last:
+            if s >= 2:
                 second_factor(s)
-            for fn, args in halves.get(s, []):
+            for fn, args in early.get(s, []):
                 fn(*args)
-            if 2 <= s + 1 <= last:
-                mm(s + 1, 1)
+            if s >= 1:
+                project(s + 1, 1)
                 if s + 1 >= wide:
-                    mm(s + 1, 2)
+                    project(s + 1, 2)
             if 0 <= s < wide:
-                mm(s, 2)
-            if 0 <= s - 1 <= last:
+                project(s, 2)
+            if s >= 1:
                 third_factor(s - 1)
-            if s + 3 <= last and s != 1:
-                mm(s + 3, 0)
-            if 0 <= s - 2 < wide - 1 and s % 2:
+            if s != 1:
+                project(s + 3, 0)
+            if 2 <= s <= wide and s % 2:
                 rank_sum(s - 3)
                 rank_sum(s - 2)
-            for fn, args in tasks.get(s, []):
+            for fn, args in late.get(s, []):
                 fn(*args)
-
-        def finish(q, i, on_vector=True):
-            out_tile(q, i, on_vector)
-            if on_vector:
-                store(q, i)
 
         first_factor(last)
         z_turn_out(1)
-        out_mm(0, 0, "h00")
-        mm(last - 1, 1)
-        mm(last - 1, 2)
-        out_mm(0, 1, "h01")
-        mm(last, 1)
-        mm(last, 2)
+        out_product(0, 0, "h00")
+        project(last - 1, 1)
+        project(last - 1, 2)
+        out_product(0, 1, "h01")
+        project(last, 1)
+        project(last, 2)
         second_factor(last - 2)
         third_factor(last - 3)
-        out_mm(0, 2, "h10")
+        out_product(0, 2, "h10")
         for u in range(wide, wide + R):
             rank_sum(u)
         finish(0, 1, False)
@@ -443,10 +417,10 @@ def tile_lowranktrimodalfusion_kernel(tc, x, w_bytes, w_scale, b, omega, wo, bo,
         finish(0, 2)
         third_factor(last - 2)
         store(0, 1)
-        out_mm(1, 0, "h00")
-        out_mm(1, 1, "h01")
-        out_mm(0, 3, "h11")
-        z_turn(2, "aux")
+        out_product(1, 0, "h00")
+        out_product(1, 1, "h01")
+        out_product(0, 3, "h11")
+        z_turn(2)
         rank_sum(last - 3)
         rank_sum(last - 2)
         finish(1, 1, False)
@@ -456,19 +430,19 @@ def tile_lowranktrimodalfusion_kernel(tc, x, w_bytes, w_scale, b, omega, wo, bo,
         finish(1, 0)
         third_factor(last)
         rank_sum(last - 1)
-        out_mm(1, 2, "h20")
+        out_product(1, 2, "h20")
         rank_sum(last)
-        out_mm(1, 3, "h10")
+        out_product(1, 3, "h10")
         z_out(groups[-1], 2, 2)
         finish(0, 3)
         store(1, 1)
         z_quant(2)
         finish(1, 2)
-        out_mm(2, 0, "h11")
-        z_turn(3, "aux")
-        out_mm(2, 1, "h21")
-        out_mm(2, 2, "h00")
-        out_mm(2, 3, "h01")
+        out_product(2, 0, "h11")
+        z_turn(3)
+        out_product(2, 1, "h21")
+        out_product(2, 2, "h00")
+        out_product(2, 3, "h01")
         finish(1, 3)
         z_turn_out(3)
         finish(2, 0)
@@ -476,7 +450,7 @@ def tile_lowranktrimodalfusion_kernel(tc, x, w_bytes, w_scale, b, omega, wo, bo,
         finish(2, 1)
         z_quant(3)
         for i, bank in enumerate(("h20", "h10", "aux", "h11")):
-            out_mm(3, i, bank)
+            out_product(3, i, bank)
         finish(2, 2)
         finish(3, 0)
         store(2, 3)

@@ -183,7 +183,8 @@ def tile_lowranktrimodalfusion_kernel(tc, x, w_bytes, w_scale, b, omega, wo, bo,
         def project(u, m):
             (c, half, a0, na), r = units[u]
             if u < wide or m == 0:
-                h = psum.tile([P, na * P], F32, name="h%d%d" % (m, u % 2))
+                bank = ("h10", "h11", "aux")[(u - 4) % 3] if m == 1 and u >= 4 else "h%d%d" % (m, u % 2)
+                h = psum.tile([P, na * P], F32, name=bank)
                 h_of[u, m] = h[:]
             elif m == 1:
                 h = psum.tile([P, 2, na * P], F32, name=("h10", "h11", "h20", "h21")[u % 4])
@@ -328,7 +329,9 @@ def tile_lowranktrimodalfusion_kernel(tc, x, w_bytes, w_scale, b, omega, wo, bo,
         for j in range(2):
             w_widen(1, 1, j)
         x_turn(0, 1, 0, "aux")
+        project(2, 0)
         x_turn(0, 1, 1, "z")
+        project(3, 0)
         x_turn(1, 1, 0, "h21")
         x_quant(2, 0)
         w_quant(pieces[2])
@@ -380,15 +383,17 @@ def tile_lowranktrimodalfusion_kernel(tc, x, w_bytes, w_scale, b, omega, wo, bo,
                 second_factor(s)
             for fn, args in early.get(s, []):
                 fn(*args)
-            if s >= 1:
+            if 1 <= s <= 4 or s + 1 >= wide:
                 project(s + 1, 1)
                 if s + 1 >= wide:
                     project(s + 1, 2)
             if 0 <= s < wide:
                 project(s, 2)
+            if 6 <= s + 2 < wide:
+                project(s + 2, 1)
             if s >= 1:
                 third_factor(s - 1)
-            if s != 1:
+            if s >= 2:
                 project(s + 3, 0)
             if 2 <= s <= wide and s % 2:
                 rank_sum(s - 3)
@@ -412,8 +417,8 @@ def tile_lowranktrimodalfusion_kernel(tc, x, w_bytes, w_scale, b, omega, wo, bo,
         finish(0, 1, False)
         z_out(groups[-2], 0, 2)
         finish(0, 0)
-        second_factor(last - 1)
         z_quant(1)
+        second_factor(last - 1)
         finish(0, 2)
         third_factor(last - 2)
         store(0, 1)

@@ -182,7 +182,11 @@ def tile_lowranktrimodalfusion_kernel(tc, x, w_bytes, w_scale, b, omega, wo, bo,
 
         def project(u, m):
             (c, half, a0, na), r = units[u]
-            if u < wide or m == 0:
+            if u >= wide and m == 0:
+                if u % 2 == 0:
+                    h = psum.tile([P, 2, na * P], F32, name="h0%d" % (u // 2 % 2))
+                    h_of[u, 0], h_of[u + 1, 0] = h[:, 0, :], h[:, 1, :]
+            elif u < wide:
                 bank = ("h10", "h11", "aux")[(u - 4) % 3] if m == 1 and u >= 4 else "h%d%d" % (m, u % 2)
                 h = psum.tile([P, na * P], F32, name=bank)
                 h_of[u, m] = h[:]
@@ -194,10 +198,11 @@ def tile_lowranktrimodalfusion_kernel(tc, x, w_bytes, w_scale, b, omega, wo, bo,
 
         def first_factor(u):
             (c, half, a0, na), r = units[u]
-            a = stage.tile([P, na * P], F32, name="a", bufs=4)
-            a_of[u] = a
+            if u < wide or u % 2 == 0:
+                a = stage.tile([P, BANK], F32, name="a", bufs=4)
+                a_of[u], a_of[u + 1] = a[:, 0 : na * P], a[:, BANK - na * P : BANK]
             nc.scalar.activation(
-                out=a[:], in_=h_of[u, 0], func=ACT.Identity, scale=column(3, r, c),
+                out=a_of[u], in_=h_of[u, 0], func=ACT.Identity, scale=column(3, r, c),
                 bias=ob0[:, 4 * r + c : 4 * r + c + 1],
             )
 
@@ -206,7 +211,7 @@ def tile_lowranktrimodalfusion_kernel(tc, x, w_bytes, w_scale, b, omega, wo, bo,
             ab = stage.tile([P, na * P], F32, name="ab")
             ab_of[u] = ab
             nc.vector.scalar_tensor_tensor(
-                out=ab[:], in0=h_of[u, 1], scalar=column(1, r, c), in1=a_of[u][:], op0=ALU.add, op1=ALU.mult
+                out=ab[:], in0=h_of[u, 1], scalar=column(1, r, c), in1=a_of[u], op0=ALU.add, op1=ALU.mult
             )
 
         def third_factor(u):
@@ -359,41 +364,47 @@ def tile_lowranktrimodalfusion_kernel(tc, x, w_bytes, w_scale, b, omega, wo, bo,
         at(3, x_quant, 0, 1)
         at(3, x_quant, 1, 1)
         at(7, x_quant, 2, 1)
-        due = [3, 7, 13, 18, 24, 30, 36, 41, 47]
+        due = [3] + [7 + (40 * k + 3) // 7 for k in range(8)]
         for i, pc in enumerate(pieces[3:]):
             at(due[i], w_quant, pc)
             if pc != pieces[-1]:
                 at(due[i], w_weave, pieces[i + 4])
         at(3, project, 4, 0)
         at(due[-1], weave, "wo", wo_raw, H)
-        at(2 * wide + 1, rank_sum, wide - 2)
+        at(2 * wide - 1, rank_sum, wide - 2)
         at(2 * wide + 1, rank_sum, wide - 1)
+        for m in (1, 2):
+            at(2 * wide + 1, project, wide + 2, m)
+        for i in range(4):
+            for u in (wide + 2 * i, wide + 2 * i + 1):
+                at(2 * wide + (-6, -4, 1, 4)[i], project, u, 0)
+                at(2 * wide + (-4, -2, 2, 5)[i], first_factor, u)
+        at(2 * wide + 1, z_out, groups[-3], 0, 2)
         at(2 * wide + 3, wo_quant)
-        at(2 * wide + 3, z_out, groups[-3], 0, 2)
-        at(2 * wide + 5, z_out, groups[-3], 2, 2)
-        at(2 * wide + 5, z_turn, 0)
-        at(2 * wide + 5, z_turn_out, 0)
+        at(2 * wide + 3, z_turn, 0)
+        at(2 * wide + 3, z_out, groups[-3], 2, 2)
+        at(2 * wide + 3, z_turn_out, 0)
         at(2 * wide + 8, z_quant, 0)
         at(2 * wide + 9, z_turn, 1)
 
         for s in range(-1, wide + 5):
-            if s >= 0:
+            if 0 <= s < wide - 2:
                 first_factor(s + 2)
             if s >= 2:
                 second_factor(s)
             for fn, args in early.get(s, []):
                 fn(*args)
-            if 1 <= s <= 4 or s + 1 >= wide:
+            if 1 <= s <= 4:
                 project(s + 1, 1)
-                if s + 1 >= wide:
-                    project(s + 1, 2)
             if 0 <= s < wide:
                 project(s, 2)
-            if 6 <= s + 2 < wide:
+            if s >= 4 and s != wide:
                 project(s + 2, 1)
+            if s + 2 >= wide and s != wide:
+                project(s + 2, 2)
             if s >= 1:
                 third_factor(s - 1)
-            if s >= 2:
+            if 2 <= s < wide - 3:
                 project(s + 3, 0)
             if 2 <= s <= wide and s % 2:
                 rank_sum(s - 3)
@@ -401,11 +412,8 @@ def tile_lowranktrimodalfusion_kernel(tc, x, w_bytes, w_scale, b, omega, wo, bo,
             for fn, args in late.get(s, []):
                 fn(*args)
 
-        first_factor(last)
         z_turn_out(1)
         out_product(0, 0, "h00")
-        project(last - 1, 1)
-        project(last - 1, 2)
         out_product(0, 1, "h01")
         project(last, 1)
         project(last, 2)

@@ -301,11 +301,11 @@ def tile_lowranktrimodalfusion_kernel(tc, x, w_bytes, w_scale, b, omega, wo, bo,
         warm_up(2)
         nc.vector.tensor_copy(out=vec32[:], in_=vec[:])
         x_out(0, 0, 0, True)
+        x_out(0, 0, 1)
         w_quant(pieces[0])
         nc.tensor.transpose(vec_turned[:], vec32[:], ident[:])
         x_turn(1, 0, 0, "h10")
         x_turn(1, 0, 1, "h11")
-        x_out(0, 0, 1)
         for m in range(1, M):
             for j in range(PACK):
                 w_widen(0, m, j)
@@ -330,7 +330,8 @@ def tile_lowranktrimodalfusion_kernel(tc, x, w_bytes, w_scale, b, omega, wo, bo,
         project(1, 1)
         for pair in range(2):
             x_out(2, 0, pair)
-            second_factor(pair)
+        for u in range(2):
+            second_factor(u)
         for j in range(2):
             w_widen(1, 1, j)
         x_turn(0, 1, 0, "aux")
@@ -338,11 +339,13 @@ def tile_lowranktrimodalfusion_kernel(tc, x, w_bytes, w_scale, b, omega, wo, bo,
         x_turn(0, 1, 1, "z")
         project(3, 0)
         x_turn(1, 1, 0, "h21")
+        project(2, 1)
+        project(3, 1)
+        x_out(0, 1, 0)
         x_quant(2, 0)
         w_quant(pieces[2])
         w_weave(pieces[3])
-        for pair in range(2):
-            x_out(0, 1, pair)
+        x_out(0, 1, 1)
 
         late, early = {}, {}
 
@@ -360,16 +363,17 @@ def tile_lowranktrimodalfusion_kernel(tc, x, w_bytes, w_scale, b, omega, wo, bo,
         at(5, x_out, 2, 1, 1)
         planes_left = [(c, m, j) for c in range(1, TILES) for m in range(M) for j in range(PACK)][6:]
         for i, (c, m, j) in enumerate(planes_left):
-            at(2 * (i // 2 if i < 14 else 7 + 14 * (i - 14) // 16) - 1, w_widen, c, m, j)
-        at(3, x_quant, 0, 1)
-        at(3, x_quant, 1, 1)
-        at(7, x_quant, 2, 1)
-        due = [3] + [7 + (40 * k + 3) // 7 for k in range(8)]
+            at(2 * (i // 2 if i < 10 else 5 + 16 * (i - 10) // 20) - 1, w_widen, c, m, j)
+        at(4, x_quant, 0, 1)
+        at(4, x_quant, 1, 1)
+        at(8, x_quant, 2, 1)
+        due = [4] + [8 + (39 * k + 3) // 7 for k in range(8)]
         for i, pc in enumerate(pieces[3:]):
             at(due[i], w_quant, pc)
             if pc != pieces[-1]:
                 at(due[i], w_weave, pieces[i + 4])
-        at(3, project, 4, 0)
+        at(4, project, 4, 0)
+        at(5, first_factor, 4)
         at(due[-1], weave, "wo", wo_raw, H)
         at(2 * wide - 1, rank_sum, wide - 2)
         at(2 * wide + 1, rank_sum, wide - 1)
@@ -388,13 +392,13 @@ def tile_lowranktrimodalfusion_kernel(tc, x, w_bytes, w_scale, b, omega, wo, bo,
         at(2 * wide + 9, z_turn, 1)
 
         for s in range(-1, wide + 5):
-            if 0 <= s < wide - 2:
+            if 0 <= s < wide - 2 and s != 2:
                 first_factor(s + 2)
             if s >= 2:
                 second_factor(s)
             for fn, args in early.get(s, []):
                 fn(*args)
-            if 1 <= s <= 4:
+            if 3 <= s <= 4:
                 project(s + 1, 1)
             if 0 <= s < wide:
                 project(s, 2)

@@ -119,18 +119,16 @@ def tile_lowranktrimodalfusion_kernel(tc, x, w_bytes, w_scale, b, omega, wo, bo,
         def x_quant(m, half):
             quantize(xq[m, half], x_grouped[m, half])
 
-        pieces = [(c, m, 1) for c in range(TILES) for m in range(M)]
-        piece_of = {(c, m): (c, m0, count) for c, m0, count in pieces for m in range(m0, m0 + count)}
-        wq = {pc: mx_operand("w%d%d" % pc[:2], pc[2] * R * P) for pc in pieces}
+        pieces = [(c, m) for c in range(TILES) for m in range(M)]
+        wq = {pc: mx_operand("w%d%d" % pc, R * P) for pc in pieces}
         woq = mx_operand("wo", H)
         planes, woven = {}, {}
 
         def w_widen(c, m, j, on_scalar=True):
-            pc = piece_of[c, m]
-            if pc not in planes:
-                t = stage.tile([P, PACK, pc[2] * R * P], BF16, name="planes%d" % pc[2], bufs=6)
-                planes[pc] = t
-            dst = planes[pc][:, j, (m - pc[1]) * R * P : (m - pc[1] + 1) * R * P]
+            if j == 0:
+                t = stage.tile([P, PACK, R * P], BF16, name="planes", bufs=6)
+                planes[c, m] = t
+            dst = planes[c, m][:, j, :]
             src = w_raw[c, m][:, j, :].bitcast(FP8)
             if on_scalar:
                 nc.scalar.activation(out=dst, in_=src, func=ACT.Copy, scale=ws[:, j : j + 1])
@@ -152,7 +150,7 @@ def tile_lowranktrimodalfusion_kernel(tc, x, w_bytes, w_scale, b, omega, wo, bo,
                 )
 
         def w_weave(pc, on_gpsimd=True):
-            weave(pc, planes[pc], pc[2] * R * P, on_gpsimd)
+            weave(pc, planes[pc], R * P, on_gpsimd)
 
         def w_quant(pc):
             quantize(wq[pc], woven[pc])
@@ -193,8 +191,7 @@ def tile_lowranktrimodalfusion_kernel(tc, x, w_bytes, w_scale, b, omega, wo, bo,
             elif m == 1:
                 h = psum.tile([P, 2, na * P], F32, name=("h10", "h11", "h20", "h21")[u % 4])
                 h_of[u, 1], h_of[u, 2] = h[:, 0, :], h[:, 1, :]
-            pc = piece_of[c, m]
-            product(h_of[u, m], wq[pc], ((m - pc[1]) * R + r) * P, xq[m, half], a0 * P, na * P)
+            product(h_of[u, m], wq[c, m], r * P, xq[m, half], a0 * P, na * P)
 
         def first_factor(u):
             (c, half, a0, na), r = units[u]
@@ -313,11 +310,11 @@ def tile_lowranktrimodalfusion_kernel(tc, x, w_bytes, w_scale, b, omega, wo, bo,
         x_quant(0, 0)
         nc.vector.tensor_tensor(out=ob0[:], in0=vec_turned[:, 48:64], in1=cols[:, 0:16], op=ALU.mult)
         x_out(1, 0, 0)
-        w_weave(pieces[1], False)
         x_out(1, 0, 1)
+        w_weave(pieces[1], False)
+        x_quant(1, 0)
         w_quant(pieces[1])
         w_weave(pieces[2])
-        x_quant(1, 0)
         project(0, 0)
         project(1, 0)
         x_turn(2, 0, 0, "h20")
@@ -341,11 +338,11 @@ def tile_lowranktrimodalfusion_kernel(tc, x, w_bytes, w_scale, b, omega, wo, bo,
         x_turn(1, 1, 0, "h21")
         project(2, 1)
         project(3, 1)
-        x_out(0, 1, 0)
         x_quant(2, 0)
         w_quant(pieces[2])
         w_weave(pieces[3])
-        x_out(0, 1, 1)
+        for pair in range(2):
+            x_out(0, 1, pair)
 
         late, early = {}, {}
 
@@ -364,25 +361,30 @@ def tile_lowranktrimodalfusion_kernel(tc, x, w_bytes, w_scale, b, omega, wo, bo,
         planes_left = [(c, m, j) for c in range(1, TILES) for m in range(M) for j in range(PACK)][6:]
         for i, (c, m, j) in enumerate(planes_left):
             at(2 * (i // 2 if i < 10 else 5 + 16 * (i - 10) // 20) - 1, w_widen, c, m, j)
-        at(4, x_quant, 0, 1)
-        at(4, x_quant, 1, 1)
-        at(8, x_quant, 2, 1)
-        due = [4] + [8 + (39 * k + 3) // 7 for k in range(8)]
+        at(3, x_quant, 0, 1)
+        at(3, x_quant, 1, 1)
+        at(7, x_quant, 2, 1)
+        due = [3] + [7 + (40 * k + 3) // 7 for k in range(8)]
         for i, pc in enumerate(pieces[3:]):
             at(due[i], w_quant, pc)
             if pc != pieces[-1]:
                 at(due[i], w_weave, pieces[i + 4])
-        at(4, project, 4, 0)
-        at(5, first_factor, 4)
+        at(3, project, 4, 0)
         at(due[-1], weave, "wo", wo_raw, H)
         at(2 * wide - 1, rank_sum, wide - 2)
         at(2 * wide + 1, rank_sum, wide - 1)
         for m in (1, 2):
             at(2 * wide + 1, project, wide + 2, m)
-        for i in range(4):
-            for u in (wide + 2 * i, wide + 2 * i + 1):
-                at(2 * wide + (-6, -4, 1, 4)[i], project, u, 0)
-                at(2 * wide + (-4, -2, 2, 5)[i], first_factor, u)
+
+        def first_pair(u, projected, read):
+            for v in (u, u + 1):
+                at(projected, project, v, 0)
+                at(read, first_factor, v)
+
+        first_pair(wide, 2 * (wide - 3), 2 * (wide - 2))
+        first_pair(wide + 2, 2 * (wide - 2), 2 * (wide - 1))
+        first_pair(wide + 4, 2 * wide + 1, 2 * (wide + 1))
+        first_pair(wide + 6, 2 * (wide + 2), 2 * (wide + 2) + 1)
         at(2 * wide + 1, z_out, groups[-3], 0, 2)
         at(2 * wide + 3, wo_quant)
         at(2 * wide + 3, z_turn, 0)
@@ -392,7 +394,7 @@ def tile_lowranktrimodalfusion_kernel(tc, x, w_bytes, w_scale, b, omega, wo, bo,
         at(2 * wide + 9, z_turn, 1)
 
         for s in range(-1, wide + 5):
-            if 0 <= s < wide - 2 and s != 2:
+            if 0 <= s < wide - 2:
                 first_factor(s + 2)
             if s >= 2:
                 second_factor(s)

@@ -20,6 +20,7 @@ PACK = 4
 HALF = 512
 TILES = F // P
 BANK = 512
+RING = 7
 
 
 def tile_lowranktrimodalfusion_kernel(tc, x, w_bytes, w_scale, b, omega, wo, bo, out):
@@ -30,42 +31,58 @@ def tile_lowranktrimodalfusion_kernel(tc, x, w_bytes, w_scale, b, omega, wo, bo,
         psum = ctx.enter_context(tc.psum_pool(name="psum", bufs=1))
         ctx.enter_context(tc.manual_schedule())
 
+        taken = []
+
+        def bank(shape, dtype=F32):
+            t = psum.tile(shape, dtype, name="ring%d" % (len(taken) % RING))
+            taken.append(t)
+            return t
+
         ws = keep.tile([P, PACK], F32, name="ws")
         vec = keep.tile([P, P], BF16, name="vec")
+        vec32 = keep.tile([P, P], F32, name="vec32")
         ident = keep.tile([P, P], F32, name="ident")
-        nc.gpsimd.memset(vec[64:128, :], 0.0)
+        zeros = keep.tile([P, BANK], BF16, name="zeros")
+        nc.vector.memset(zeros[:], 0.0)
+        nc.scalar.dma_start(out=ws[:], in_=w_scale.rearrange("a (p j) o -> p (a j o)", j=PACK))
+        nc.scalar.dma_start(out=vec[48:64, :], in_=omega.rearrange("r (c f) -> (r c) f", f=P))
+        nc.scalar.dma_start(out=vec[0:48, :], in_=b.rearrange("m (q f) -> (m q) f", f=P))
         make_identity(nc, ident[:])
+        nc.gpsimd.memset(vec32[64:128, :], 0.0)
 
+        pieces = [(c, m) for c in range(TILES) for m in range(M)]
         w_raw, x_raw = {}, {}
-        for c in range(TILES):
-            for m in range(M):
-                t = keep.tile([P, PACK, R * P], U8, name="w_raw%d%d" % (c, m))
-                w_raw[c, m] = t
+        for jj in range(2):
+            t = keep.tile([P, 2, R * P], U8, name="w_raw%d" % jj)
+            w_raw[0, 0, jj] = t
         for m in range(M):
             for half in range(2):
                 t = keep.tile([P, 4, D], BF16, name="x_raw%d%d" % (m, half))
                 x_raw[m, half] = t
         wo_raw = keep.tile([P, PACK, H], BF16, name="wo_raw")
         bo_sb = keep.tile([P, H], BF16, name="bo_sb")
+        w_whole = {}
 
         def load_w(c, m):
-            src = w_bytes[m].rearrange("(p j) (r f) -> p (j r) f", j=PACK, r=R)
-            nc.sync.dma_start(
-                out=w_raw[c, m][:].rearrange("p j (r f) -> p (j r) f", r=R), in_=src[:, :, c * P : (c + 1) * P]
-            )
+            src = w_bytes[m].rearrange("(p j) (r f) -> p (j r) f", j=PACK, r=R)[:, :, c * P : (c + 1) * P]
+            if (c, m) == (0, 0):
+                for jj in range(2):
+                    nc.sync.dma_start(
+                        out=w_raw[c, m, jj][:].rearrange("p j (r f) -> p (j r) f", r=R), in_=src[:, 8 * jj : 8 * jj + 8, :]
+                    )
+            else:
+                t = keep.tile([P, PACK, R * P], U8, name="w_whole%d%d" % (c, m))
+                w_whole[c, m] = t
+                nc.sync.dma_start(out=t[:].rearrange("p j (r f) -> p (j r) f", r=R), in_=src)
 
         def load_x(m, half):
             src = x[m].rearrange("(p a) k -> p a k", a=8)
             nc.sync.dma_start(out=x_raw[m, half][:], in_=src[:, 4 * half : 4 * half + 4, :])
 
-        nc.scalar.dma_start(out=ws[:], in_=w_scale.rearrange("a (p j) o -> p (a j o)", j=PACK))
-        nc.scalar.dma_start(out=vec[48:64, :], in_=omega.rearrange("r (c f) -> (r c) f", f=P))
-        nc.scalar.dma_start(out=vec[0:48, :], in_=b.rearrange("m (q f) -> (m q) f", f=P))
-        w_order = [(c, m) for c in range(TILES) for m in range(M)]
         for i in range(2 * M):
-            load_w(*w_order[i])
+            load_w(*pieces[i])
             load_x(i % M, i // M)
-        for c, m in w_order[2 * M :]:
+        for c, m in pieces[2 * M :]:
             load_w(c, m)
         nc.sync.dma_start(out=wo_raw[:], in_=wo.rearrange("(p j) n -> p j n", j=PACK))
         nc.sync.dma_start(out=bo_sb[:], in_=bo.partition_broadcast(P))
@@ -80,10 +97,10 @@ def tile_lowranktrimodalfusion_kernel(tc, x, w_bytes, w_scale, b, omega, wo, bo,
                 out=operand[0][:].bitcast(FP8X4), scales=operand[1][:], in_=src[:].rearrange("p n j -> p (n j)")
             )
 
-        def product(bank, lhs, lhs_from, rhs, rhs_from, width):
+        def product(dst, lhs, lhs_from, rhs, rhs_from, width):
             lcols, rcols = slice(lhs_from, lhs_from + P), slice(rhs_from, rhs_from + width)
             nc.tensor.matmul_mx(
-                out=bank,
+                out=dst,
                 lhsT=lhs[0][:, lcols].bitcast(FP8X4),
                 lhsT_scale=lhs[1][:, lcols],
                 rhs=rhs[0][:, rcols].bitcast(FP8X4),
@@ -95,8 +112,8 @@ def tile_lowranktrimodalfusion_kernel(tc, x, w_bytes, w_scale, b, omega, wo, bo,
         xq = {(m, half): mx_operand("x%d%d" % (m, half), HALF) for m in range(M) for half in range(2)}
         x_turned, x_grouped = {}, {}
 
-        def x_turn(m, half, pair, bank):
-            t = psum.tile([P, 2, 2, P], F32, name=bank)
+        def x_turn(m, half, pair):
+            t = bank([P, 2, 2, P])
             words = x_raw[m, half][:].rearrange("p a k -> p (a k)").bitcast(F32)
             for i in range(2):
                 base = (2 * pair + i) * 256
@@ -106,7 +123,7 @@ def tile_lowranktrimodalfusion_kernel(tc, x, w_bytes, w_scale, b, omega, wo, bo,
 
         def x_out(m, half, pair, on_scalar=False):
             if pair == 0:
-                g = stage.tile([P, HALF, PACK], BF16, name="x_grouped", align_bytes=64, bufs=4)
+                g = stage.tile([P, HALF, PACK], BF16, name="x_grouped", align_bytes=64, bufs=3)
                 x_grouped[m, half] = g
             dst = x_grouped[m, half][:].rearrange("p n j -> p (n j)").bitcast(F32)
             dst = dst[:, pair * BANK : (pair + 1) * BANK].rearrange("p (a r u) -> p a r u", a=2, u=2)
@@ -119,24 +136,24 @@ def tile_lowranktrimodalfusion_kernel(tc, x, w_bytes, w_scale, b, omega, wo, bo,
         def x_quant(m, half):
             quantize(xq[m, half], x_grouped[m, half])
 
-        pieces = [(c, m) for c in range(TILES) for m in range(M)]
         wq = {pc: mx_operand("w%d%d" % pc, R * P) for pc in pieces}
-        woq = mx_operand("wo", H)
+        woq = [mx_operand("wo%d" % i, BANK) for i in range(2)]
         planes, woven = {}, {}
 
         def w_widen(c, m, j, on_scalar=True):
             if j == 0:
-                t = stage.tile([P, PACK, R * P], BF16, name="planes", bufs=6)
+                t = stage.tile([P, PACK, R * P], BF16, name="planes", align_bytes=64, bufs=5)
                 planes[c, m] = t
             dst = planes[c, m][:, j, :]
-            src = w_raw[c, m][:, j, :].bitcast(FP8)
+            raw = w_raw[c, m, j // 2][:, j % 2, :] if (c, m) == (0, 0) else w_whole[c, m][:, j, :]
+            src = raw.bitcast(FP8)
             if on_scalar:
                 nc.scalar.activation(out=dst, in_=src, func=ACT.Copy, scale=ws[:, j : j + 1])
             else:
                 nc.vector.tensor_scalar(out=dst, in0=src, scalar1=ws[:, j : j + 1], scalar2=None, op0=ALU.mult)
 
-        def weave(key, src, width, on_gpsimd=True):
-            dst = stage.tile([P, width, PACK], BF16, name="woven", align_bytes=64, bufs=1)
+        def weave(key, src, width, on_gpsimd=True, tag="woven"):
+            dst = stage.tile([P, width, PACK], BF16, name=tag, align_bytes=64, bufs=1)
             woven[key] = dst
             if on_gpsimd:
                 nc.gpsimd.tensor_scalar(
@@ -149,94 +166,126 @@ def tile_lowranktrimodalfusion_kernel(tc, x, w_bytes, w_scale, b, omega, wo, bo,
                     in_=src[:].rearrange("p j (c i) -> p c j i", i=4),
                 )
 
-        def w_weave(pc, on_gpsimd=True):
-            weave(pc, planes[pc], R * P, on_gpsimd)
+        def w_weave(pc, on_gpsimd=True, tag="woven"):
+            weave(pc, planes[pc], R * P, on_gpsimd, tag)
 
         def w_quant(pc):
             quantize(wq[pc], woven[pc])
 
-        def wo_quant():
-            quantize(woq, woven["wo"])
+        def wo_weave(i):
+            if i % 2 == 0:
+                t = stage.tile([P, BANK, PACK], BF16, name="planes", align_bytes=64, bufs=5)
+                woven["wo", i // 2] = t
+            nc.scalar.copy(
+                out=woven["wo", i // 2][:, 256 * (i % 2) : 256 * (i % 2 + 1), :].rearrange("p (c i) j -> p c j i", i=4),
+                in_=wo_raw[:, :, 256 * i : 256 * (i + 1)].rearrange("p j (c i) -> p c j i", i=4),
+            )
 
-        vec32 = keep.tile([P, P], F32, name="vec32")
+        def wo_quant(i):
+            quantize(woq[i], woven["wo", i])
+
         cols = keep.tile([P, 64], F32, name="cols")
         ob0 = keep.tile([P, 16], F32, name="ob0")
-        vec_turned = psum.tile([P, P], F32, name="aux")
 
         def column(row, r, c):
             q = 16 * row + 4 * r + c
             return cols[:, q : q + 1]
 
-        groups = [(c, half, 0, 4) for c in range(TILES) for half in range(2)][:-1]
-        groups += [(TILES - 1, 1, a0, 2) for a0 in (0, 2)]
-        units = [(g, r) for g in groups for r in range(R)]
+        groups = [(c, half, 0, 4) for c in range(TILES - 1) for half in range(2)] + [(TILES - 1, q // 2, 2 * (q % 2), 2) for q in range(4)]
+        units = []
+        for g in groups:
+            na = g[3]
+            per = 4 // na
+            for i in range(R // per):
+                units.append((g, list(range(i * per, (i + 1) * per))))
         last = len(units) - 1
-        wide = 8 * TILES - R
         h_of, a_of, ab_of, p_of, z_sum = {}, {}, {}, {}, {}
         z_rows = {}
         for half in range(2):
             t = keep.tile([P, 4, F], BF16, name="z_rows%d" % half)
             z_rows[half] = t
 
+        def parts(u):
+            (c, half, a0, na), ranks = units[u]
+            return [(r, slice(i * na * P, (i + 1) * na * P)) for i, r in enumerate(ranks)]
+
         def project(u, m):
-            (c, half, a0, na), r = units[u]
-            if u >= wide and m == 0:
-                if u % 2 == 0:
-                    h = psum.tile([P, 2, na * P], F32, name="h0%d" % (u // 2 % 2))
-                    h_of[u, 0], h_of[u + 1, 0] = h[:, 0, :], h[:, 1, :]
-            elif u < wide:
-                bank = ("h10", "h11", "aux")[(u - 4) % 3] if m == 1 and u >= 4 else "h%d%d" % (m, u % 2)
-                h = psum.tile([P, na * P], F32, name=bank)
-                h_of[u, m] = h[:]
-            elif m == 1:
-                h = psum.tile([P, 2, na * P], F32, name=("h10", "h11", "h20", "h21")[u % 4])
-                h_of[u, 1], h_of[u, 2] = h[:, 0, :], h[:, 1, :]
-            product(h_of[u, m], wq[c, m], r * P, xq[m, half], a0 * P, na * P)
+            c, half, a0, na = units[u][0]
+            h = bank([P, BANK])
+            h_of[u, m] = h
+            for r, cs in parts(u):
+                product(h[:, cs], wq[c, m], r * P, xq[m, half], a0 * P, na * P)
 
         def first_factor(u):
-            (c, half, a0, na), r = units[u]
-            if u < wide or u % 2 == 0:
-                a = stage.tile([P, BANK], F32, name="a", bufs=4)
-                a_of[u], a_of[u + 1] = a[:, 0 : na * P], a[:, BANK - na * P : BANK]
-            nc.scalar.activation(
-                out=a_of[u], in_=h_of[u, 0], func=ACT.Identity, scale=column(3, r, c),
-                bias=ob0[:, 4 * r + c : 4 * r + c + 1],
-            )
-
-        def second_factor(u):
-            (c, half, a0, na), r = units[u]
-            ab = stage.tile([P, na * P], F32, name="ab")
-            ab_of[u] = ab
-            nc.vector.scalar_tensor_tensor(
-                out=ab[:], in0=h_of[u, 1], scalar=column(1, r, c), in1=a_of[u], op0=ALU.add, op1=ALU.mult
-            )
-
-        def third_factor(u):
-            (c, half, a0, na), r = units[u]
-            p = stage.tile([P, na * P], F32, name="p", bufs=6)
-            p_of[u] = p
-            nc.vector.scalar_tensor_tensor(
-                out=p[:], in0=h_of[u, 2], scalar=column(2, r, c), in1=ab_of[u][:], op0=ALU.add, op1=ALU.mult
-            )
-
-        def rank_sum(u):
-            g, r = units[u]
-            na = g[3]
-            if r == 0:
-                z = psum.tile([P, na, P], F32, name="z")
-                z_sum[g] = z
-            for a in range(na):
-                nc.tensor.matmul(
-                    z_sum[g][:, a, :], lhsT=p_of[u][:, a * P : (a + 1) * P], rhs=ident[:], is_transpose=True,
-                    start=r == 0 and a == 0, stop=r == R - 1 and a == na - 1,
+            c = units[u][0][0]
+            a = stage.tile([P, BANK], F32, name="a", bufs=5)
+            a_of[u] = a
+            for r, cs in parts(u):
+                nc.scalar.activation(
+                    out=a[:, cs], in_=h_of[u, 0][:, cs], func=ACT.Identity, scale=column(3, r, c),
+                    bias=ob0[:, 4 * r + c : 4 * r + c + 1],
                 )
 
-        def z_out(g, a0, na):
-            c, half = g[:2]
+        def second_factor(u):
+            c = units[u][0][0]
+            ab = stage.tile([P, BANK], F32, name="ab", bufs=5)
+            ab_of[u] = ab
+            for r, cs in parts(u):
+                nc.vector.scalar_tensor_tensor(
+                    out=ab[:, cs], in0=h_of[u, 1][:, cs], scalar=column(1, r, c), in1=a_of[u][:, cs], op0=ALU.add, op1=ALU.mult
+                )
+
+        def third_factor(u):
+            c = units[u][0][0]
+            p = stage.tile([P, BANK], F32, name="p", bufs=7)
+            p_of[u] = p
+            for r, cs in parts(u):
+                nc.vector.scalar_tensor_tensor(
+                    out=p[:, cs], in0=h_of[u, 2][:, cs], scalar=column(2, r, c), in1=ab_of[u][:, cs], op0=ALU.add, op1=ALU.mult
+                )
+
+        factor_sb = {}
+
+        def factor_out(u, m):
+            c = units[u][0][0]
+            t = stage.tile([P, BANK], F32, name="y", bufs=4)
+            factor_sb[u, m] = t
+            for r, cs in parts(u):
+                nc.scalar.activation(out=t[:, cs], in_=h_of[u, m][:, cs], func=ACT.Identity, bias=column(m, r, c))
+
+        def third_on_gpsimd(u, tag="pg"):
+            p = stage.tile([P, BANK], F32, name=tag, align_bytes=64, bufs=1)
+            p_of[u] = p
+            nc.gpsimd.tensor_tensor(out=p[:], in0=factor_sb[u, 2][:], in1=ab_of[u][:], op=ALU.mult)
+
+        def second_on_gpsimd(u, tag="abg"):
+            ab = stage.tile([P, BANK], F32, name=tag, align_bytes=64, bufs=1)
+            ab_of[u] = ab
+            nc.gpsimd.tensor_tensor(out=ab[:], in0=factor_sb[u, 1][:], in1=a_of[u][:], op=ALU.mult)
+
+        def rank_sum(u):
+            g, ranks = units[u]
+            na = g[3]
+            if ranks[0] == 0:
+                if na < 4 and u > 24:
+                    z = bank([P, na, P])
+                else:
+                    z = psum.tile([P, na, P], F32, name="z")
+                z_sum[g] = z
+            for i, r in enumerate(ranks):
+                for a in range(na):
+                    at_col = (i * na + a) * P
+                    nc.tensor.matmul(
+                        z_sum[g][:, a, :], lhsT=p_of[u][:, at_col : at_col + P], rhs=ident[:], is_transpose=True,
+                        start=r == 0 and a == 0, stop=r == R - 1 and a == na - 1,
+                    )
+
+        def z_out(g):
+            c, half, a0, na = g
             dst = z_rows[half][:, a0 : a0 + na, :].rearrange("p a (u q) -> p a u q", u=2)[:, :, :, 64 * c : 64 * c + 64]
             nc.scalar.copy(
                 out=dst.rearrange("p a u (q e) -> p a u q e", e=2),
-                in_=z_sum[g][:, a0 - g[2] : a0 - g[2] + na, :].rearrange("p a (q u e) -> p a u q e", u=2, e=2),
+                in_=z_sum[g][:].rearrange("p a (q u e) -> p a u q e", u=2, e=2),
             )
 
         zq = [mx_operand("z%d" % q, 256) for q in range(4)]
@@ -244,7 +293,7 @@ def tile_lowranktrimodalfusion_kernel(tc, x, w_bytes, w_scale, b, omega, wo, bo,
         out_rows = out.rearrange("(p a) h -> p a h", a=8)
 
         def z_turn(q):
-            t = psum.tile([P, 2, 2, P], F32, name="aux")
+            t = bank([P, 2, 2, P])
             words = z_rows[q // 2][:].rearrange("p a k -> p (a k)").bitcast(F32)
             for i in range(4):
                 base = (4 * (q % 2) + i) * P
@@ -252,7 +301,7 @@ def tile_lowranktrimodalfusion_kernel(tc, x, w_bytes, w_scale, b, omega, wo, bo,
             z_turned[q] = t
 
         def z_turn_out(q):
-            g = stage.tile([P, 256, PACK], BF16, name="z_grouped", align_bytes=64, bufs=2)
+            g = stage.tile([P, 256, PACK], BF16, name="z_grouped%d" % q, align_bytes=64, bufs=1)
             z_grouped[q] = g
             dst = g[:].rearrange("p n j -> p (n j)").bitcast(F32).rearrange("p (a r u) -> p a r u", a=2, u=2)
             nc.scalar.copy(out=dst, in_=z_turned[q][:].rearrange("p a u r -> p a r u"))
@@ -260,30 +309,36 @@ def tile_lowranktrimodalfusion_kernel(tc, x, w_bytes, w_scale, b, omega, wo, bo,
         def z_quant(q):
             quantize(zq[q], z_grouped[q])
 
-        def out_product(q, i, bank):
-            y = psum.tile([P, BANK], F32, name=bank)
-            product(y[:], zq[q], i % 2 * P, woq, i // 2 * BANK, BANK)
+        def out_product(q, i, spare=False):
+            y = psum.tile([P, BANK], F32, name="z") if spare else bank([P, BANK])
+            product(y[:], zq[q], i % 2 * P, woq[i // 2], 0, BANK)
             y_of[q, i] = y
 
         def store(q, i):
             hs = slice(i // 2 * BANK, (i // 2 + 1) * BANK)
             nc.sync.dma_start(out=out_rows[:, 2 * q + i % 2, hs], in_=o_of[q, i][:])
 
-        def finish(q, i, on_vector=True):
+        def finish(q, i):
             hs = slice(i // 2 * BANK, (i // 2 + 1) * BANK)
-            o = stage.tile([P, BANK], F32, name="o", bufs=12)
+            o = stage.tile([P, BANK], F32, name="o", bufs=8)
             o_of[q, i] = o
-            if on_vector:
-                nc.vector.tensor_tensor(out=o[:], in0=y_of[q, i][:], in1=bo_sb[:, hs], op=ALU.add)
-                store(q, i)
-            else:
-                y = stage.tile([P, BANK], F32, name="y")
-                nc.scalar.copy(out=y[:], in_=y_of[q, i][:])
-                nc.gpsimd.tensor_tensor(out=o[:], in0=y[:], in1=bo_sb[:, hs], op=ALU.add)
+            nc.vector.tensor_tensor(out=o[:], in0=y_of[q, i][:], in1=bo_sb[:, hs], op=ALU.add)
+            store(q, i)
 
-        zeros = keep.tile([P, BANK], BF16, name="zeros")
+        y_sb = {}
+
+        def y_out(q, i):
+            y = stage.tile([P, BANK], F32, name="y", bufs=4)
+            y_sb[q, i] = y
+            nc.scalar.copy(out=y[:], in_=y_of[q, i][:])
+
+        def add_bo(q, i, tag="og"):
+            hs = slice(i // 2 * BANK, (i // 2 + 1) * BANK)
+            o = stage.tile([P, BANK], F32, name=tag, align_bytes=64, bufs=2 if tag == "og" else 1)
+            o_of[q, i] = o
+            nc.gpsimd.tensor_tensor(out=o[:], in0=y_sb[q, i][:], in1=bo_sb[:, hs], op=ALU.add)
+
         unread = psum.tile([P, BANK], F32, name="z")
-        nc.vector.memset(zeros[:], 0.0)
 
         def warm_up(count):
             for i in range(count):
@@ -293,22 +348,23 @@ def tile_lowranktrimodalfusion_kernel(tc, x, w_bytes, w_scale, b, omega, wo, bo,
         for j in range(PACK):
             w_widen(0, 0, j, j == 3)
         w_weave(pieces[0], False)
-        x_turn(0, 0, 0, "h00")
-        x_turn(0, 0, 1, "h01")
+        x_turn(0, 0, 0)
+        x_turn(0, 0, 1)
         warm_up(2)
-        nc.vector.tensor_copy(out=vec32[:], in_=vec[:])
+        nc.gpsimd.tensor_scalar(out=vec32[0:64, :], in0=vec[0:64, :], scalar1=1.0, scalar2=0.0, op0=ALU.mult, op1=ALU.add)
         x_out(0, 0, 0, True)
         x_out(0, 0, 1)
         w_quant(pieces[0])
+        vec_turned = bank([P, P])
         nc.tensor.transpose(vec_turned[:], vec32[:], ident[:])
-        x_turn(1, 0, 0, "h10")
-        x_turn(1, 0, 1, "h11")
+        x_turn(1, 0, 0)
+        x_turn(1, 0, 1)
+        nc.scalar.copy(out=cols[:], in_=vec_turned[:, 0:64])
         for m in range(1, M):
             for j in range(PACK):
                 w_widen(0, m, j)
-        nc.vector.tensor_copy(out=cols[:], in_=vec_turned[:, 0:64])
         x_quant(0, 0)
-        nc.vector.tensor_tensor(out=ob0[:], in0=vec_turned[:, 48:64], in1=cols[:, 0:16], op=ALU.mult)
+        nc.gpsimd.tensor_tensor(out=ob0[:], in0=cols[:, 48:64], in1=cols[:, 0:16], op=ALU.mult)
         x_out(1, 0, 0)
         x_out(1, 0, 1)
         w_weave(pieces[1], False)
@@ -317,162 +373,186 @@ def tile_lowranktrimodalfusion_kernel(tc, x, w_bytes, w_scale, b, omega, wo, bo,
         w_weave(pieces[2])
         project(0, 0)
         project(1, 0)
-        x_turn(2, 0, 0, "h20")
-        x_turn(2, 0, 1, "h21")
+        x_turn(2, 0, 0)
+        x_turn(2, 0, 1)
         first_factor(0)
         first_factor(1)
         for j in range(PACK):
             w_widen(1, 0, j)
-        project(0, 1)
-        project(1, 1)
         for pair in range(2):
             x_out(2, 0, pair)
-        for u in range(2):
-            second_factor(u)
+        project(0, 1)
+        project(1, 1)
+        x_turn(0, 1, 0)
+        x_turn(0, 1, 1)
+        project(2, 0)
+        second_factor(0)
+        second_factor(1)
+        project(3, 0)
+        first_factor(2)
         for j in range(2):
             w_widen(1, 1, j)
-        x_turn(0, 1, 0, "aux")
-        project(2, 0)
-        x_turn(0, 1, 1, "z")
-        project(3, 0)
-        x_turn(1, 1, 0, "h21")
-        project(2, 1)
-        project(3, 1)
-        x_quant(2, 0)
-        w_quant(pieces[2])
-        w_weave(pieces[3])
         for pair in range(2):
             x_out(0, 1, pair)
+        x_turn(1, 1, 0)
+        x_turn(1, 1, 1)
+        project(2, 1)
+        x_quant(2, 0)
+        x_quant(0, 1)
+        w_quant(pieces[2])
+        w_weave(pieces[3])
+        first_factor(3)
+        for pair in range(2):
+            x_out(1, 1, pair)
+        project(4, 0)
 
         late, early = {}, {}
 
         def at(time, fn, *args):
             (late if time % 2 else early).setdefault(time // 2, []).append((fn, args))
 
-        for i, g in enumerate(groups[:-3]):
-            at(8 * i + 13, z_out, g, 0, 4)
-        at(-1, x_turn, 1, 1, 1, "aux")
-        at(-1, x_out, 1, 1, 0)
-        at(1, x_out, 1, 1, 1)
-        at(1, x_turn, 2, 1, 0, "z")
-        at(3, x_turn, 2, 1, 1, "aux")
-        at(5, x_out, 2, 1, 0, True)
-        at(5, x_out, 2, 1, 1)
+        ends = {}
+        for u, (g, ranks) in enumerate(units):
+            ends[g] = u
+        for u in range(1, 24, 2):
+            at(2 * (u + 3) + 1, rank_sum, u - 1)
+            at(2 * (u + 3) + 1, rank_sum, u)
+        for g in groups[:6]:
+            at(2 * (ends[g] + 3 + 1) + 1, z_out, g)
         planes_left = [(c, m, j) for c in range(1, TILES) for m in range(M) for j in range(PACK)][6:]
         for i, (c, m, j) in enumerate(planes_left):
-            at(2 * (i // 2 if i < 10 else 5 + 16 * (i - 10) // 20) - 1, w_widen, c, m, j)
-        at(3, x_quant, 0, 1)
-        at(3, x_quant, 1, 1)
-        at(7, x_quant, 2, 1)
-        due = [3] + [7 + (40 * k + 3) // 7 for k in range(8)]
+            at(2 * (2 + (i // 3 if i < 12 else 4 + 17 * (i - 12) // 18)) + 1, w_widen, c, m, j)
+        deferred = [(4, 1), (24, 1), (24, 2)]
+        at(5, x_turn, 2, 1, 0)
+        at(5, x_turn, 2, 1, 1)
+        at(7, x_quant, 1, 1)
+        at(11, x_quant, 2, 1)
+        due = [7,11,17,23,29,35,41,47,53]
+
         for i, pc in enumerate(pieces[3:]):
             at(due[i], w_quant, pc)
-            if pc != pieces[-1]:
+            if i + 4 < len(pieces) - 0:
                 at(due[i], w_weave, pieces[i + 4])
-        at(3, project, 4, 0)
-        at(due[-1], weave, "wo", wo_raw, H)
-        at(2 * wide - 1, rank_sum, wide - 2)
-        at(2 * wide + 1, rank_sum, wide - 1)
-        for m in (1, 2):
-            at(2 * wide + 1, project, wide + 2, m)
-
-        def first_pair(u, projected, read):
-            for v in (u, u + 1):
-                at(projected, project, v, 0)
-                at(read, first_factor, v)
-
-        first_pair(wide, 2 * (wide - 3), 2 * (wide - 2))
-        first_pair(wide + 2, 2 * (wide - 2), 2 * (wide - 1))
-        first_pair(wide + 4, 2 * wide + 1, 2 * (wide + 1))
-        first_pair(wide + 6, 2 * (wide + 2), 2 * (wide + 2) + 1)
-        at(2 * wide + 1, z_out, groups[-3], 0, 2)
-        at(2 * wide + 3, wo_quant)
-        at(2 * wide + 3, z_turn, 0)
-        at(2 * wide + 3, z_out, groups[-3], 2, 2)
-        at(2 * wide + 3, z_turn_out, 0)
-        at(2 * wide + 8, z_quant, 0)
-        at(2 * wide + 9, z_turn, 1)
-
-        for s in range(-1, wide + 5):
-            if 0 <= s < wide - 2:
+        at(7, project, 4, 1)
+        at(47, project, 24, 1)
+        at(7, x_out, 2, 1, 0)
+        at(7, x_out, 2, 1, 1)
+        at(47, wo_weave, 0)
+        at(51, wo_weave, 1)
+        at(53, weave, ("wo", 1), wo_raw[:, :, BANK:H], BANK)
+        for s in range(2, 27):
+            if s + 2 <= last and s + 2 not in a_of:
                 first_factor(s + 2)
-            if s >= 2:
-                second_factor(s)
+            if 0 <= s - 3 <= last and s - 3 not in p_of:
+                third_factor(s - 3)
             for fn, args in early.get(s, []):
                 fn(*args)
-            if 3 <= s <= 4:
-                project(s + 1, 1)
-            if 0 <= s < wide:
-                project(s, 2)
-            if s >= 4 and s != wide:
-                project(s + 2, 1)
-            if s + 2 >= wide and s != wide:
-                project(s + 2, 2)
-            if s >= 1:
-                third_factor(s - 1)
-            if 2 <= s < wide - 3:
+            if s <= last and s not in ab_of:
+                second_factor(s)
+            if 0 <= s + 1 - 3 <= last and (s + 1 - 3, 2) not in h_of and (s + 1 - 3, 2) not in deferred:
+                project(s + 1 - 3, 2)
+            if s + 3 <= last and (s + 3, 0) not in h_of and (s + 3, 0) not in deferred:
                 project(s + 3, 0)
-            if 2 <= s <= wide and s % 2:
-                rank_sum(s - 3)
-                rank_sum(s - 2)
+            if s + 1 <= last and (s + 1, 1) not in h_of and (s + 1, 1) not in deferred:
+                project(s + 1, 1)
             for fn, args in late.get(s, []):
                 fn(*args)
-
+        project(24, 2)
+        project(25, 2)
+        z_out(groups[5])
+        first_factor(29)
+        second_factor(27)
+        project(26, 2)
+        project(27, 2)
+        third_factor(24)
+        project(28, 1)
+        third_factor(25)
+        project(30, 0)
+        rank_sum(24)
+        rank_sum(25)
+        third_factor(26)
+        project(29, 1)
+        z_out(groups[6])
+        first_factor(30)
+        third_factor(27)
+        project(31, 0)
+        project(28, 2)
+        z_turn(0)
+        rank_sum(26)
+        rank_sum(27)
+        second_factor(28)
+        wo_quant(0)
+        wo_quant(1)
+        z_turn_out(0)
+        z_out(groups[7])
+        first_factor(31)
+        project(29, 2)
+        second_factor(29)
+        project(30, 1)
+        z_turn(1)
+        z_quant(0)
+        third_factor(28)
+        out_product(0, 0, True)
+        project(31, 1)
+        out_product(0, 1)
         z_turn_out(1)
-        out_product(0, 0, "h00")
-        out_product(0, 1, "h01")
-        project(last, 1)
-        project(last, 2)
-        second_factor(last - 2)
-        third_factor(last - 3)
-        out_product(0, 2, "h10")
-        for u in range(wide, wide + R):
-            rank_sum(u)
-        finish(0, 1, False)
-        z_out(groups[-2], 0, 2)
-        finish(0, 0)
+        third_factor(29)
+        y_out(0, 0)
+        project(30, 2)
+        second_factor(30)
+        rank_sum(28)
+        rank_sum(29)
         z_quant(1)
-        second_factor(last - 1)
-        finish(0, 2)
-        third_factor(last - 2)
-        store(0, 1)
-        out_product(1, 0, "h00")
-        out_product(1, 1, "h01")
-        out_product(0, 3, "h11")
+        add_bo(0, 0, "z_grouped1")
+        y_out(0, 1)
+        add_bo(0, 1)
+        project(31, 2)
+        z_out(groups[8])
+        second_factor(31)
+        out_product(0, 2, True)
+        out_product(0, 3)
+        third_factor(30)
         z_turn(2)
-        rank_sum(last - 3)
-        rank_sum(last - 2)
-        finish(1, 1, False)
+        store(0, 0)
+        out_product(1, 0)
+        out_product(1, 1)
+        third_factor(31)
         z_turn_out(2)
-        second_factor(last)
-        third_factor(last - 1)
+        y_out(0, 3)
+        rank_sum(30)
+        rank_sum(31)
+        finish(0, 2)
+        store(0, 1)
         finish(1, 0)
-        third_factor(last)
-        rank_sum(last - 1)
-        out_product(1, 2, "h20")
-        rank_sum(last)
-        out_product(1, 3, "h10")
-        z_out(groups[-1], 2, 2)
-        finish(0, 3)
-        store(1, 1)
         z_quant(2)
-        finish(1, 2)
-        out_product(2, 0, "h11")
+        add_bo(0, 3, "z_grouped2")
+        z_out(groups[9])
+        out_product(1, 2)
+        out_product(1, 3, True)
+        y_out(1, 1)
+        add_bo(1, 1)
         z_turn(3)
-        out_product(2, 1, "h21")
-        out_product(2, 2, "h00")
-        out_product(2, 3, "h01")
-        finish(1, 3)
+        out_product(2, 0)
+        out_product(2, 1)
+        finish(1, 2)
+        store(0, 3)
         z_turn_out(3)
+        finish(1, 3)
+        out_product(2, 2)
+        out_product(2, 3, True)
+        y_out(2, 1)
         finish(2, 0)
-        finish(2, 3, False)
-        finish(2, 1)
-        z_quant(3)
-        for i, bank in enumerate(("h20", "h10", "aux", "h11")):
-            out_product(3, i, bank)
+        store(1, 1)
         finish(2, 2)
+        z_quant(3)
+        add_bo(2, 1, "z_grouped3")
+        for i in range(4):
+            out_product(3, i)
+        finish(2, 3)
+        y_out(3, 1)
+        add_bo(3, 1)
         finish(3, 0)
-        store(2, 3)
-        finish(3, 1)
+        store(2, 1)
         finish(3, 2)
         finish(3, 3)
+        store(3, 1)

@@ -348,23 +348,23 @@ def tile_lowranktrimodalfusion_kernel(tc, x, w_bytes, w_scale, b, omega, wo, bo,
         for j in range(PACK):
             w_widen(0, 0, j, j == 3)
         w_weave(pieces[0], False)
+        nc.vector.tensor_copy(out=vec32[0:64, :], in_=vec[0:64, :])
         x_turn(0, 0, 0)
         x_turn(0, 0, 1)
         warm_up(2)
-        nc.gpsimd.tensor_scalar(out=vec32[0:64, :], in0=vec[0:64, :], scalar1=1.0, scalar2=0.0, op0=ALU.mult, op1=ALU.add)
-        x_out(0, 0, 0, True)
-        x_out(0, 0, 1)
-        w_quant(pieces[0])
         vec_turned = bank([P, P])
         nc.tensor.transpose(vec_turned[:], vec32[:], ident[:])
+        x_out(0, 0, 0, True)
+        w_quant(pieces[0])
+        x_out(0, 0, 1)
+        nc.vector.tensor_copy(out=cols[:], in_=vec_turned[:, 0:64])
         x_turn(1, 0, 0)
         x_turn(1, 0, 1)
-        nc.scalar.copy(out=cols[:], in_=vec_turned[:, 0:64])
         for m in range(1, M):
             for j in range(PACK):
                 w_widen(0, m, j)
         x_quant(0, 0)
-        nc.gpsimd.tensor_tensor(out=ob0[:], in0=cols[:, 48:64], in1=cols[:, 0:16], op=ALU.mult)
+        nc.vector.tensor_tensor(out=ob0[:], in0=vec_turned[:, 48:64], in1=cols[:, 0:16], op=ALU.mult)
         x_out(1, 0, 0)
         x_out(1, 0, 1)
         w_weave(pieces[1], False)
@@ -489,58 +489,56 @@ def tile_lowranktrimodalfusion_kernel(tc, x, w_bytes, w_scale, b, omega, wo, bo,
         project(29, 2)
         second_factor(29)
         project(30, 1)
-        z_turn(1)
         z_quant(0)
         third_factor(28)
         out_product(0, 0, True)
+        z_turn(1)
         project(31, 1)
         out_product(0, 1)
+        y_out(0, 0)
+        add_bo(0, 0)
         z_turn_out(1)
         third_factor(29)
-        y_out(0, 0)
         project(30, 2)
+        out_product(0, 2, True)
         second_factor(30)
         rank_sum(28)
         rank_sum(29)
-        z_quant(1)
-        add_bo(0, 0, "z_grouped1")
-        y_out(0, 1)
-        add_bo(0, 1)
         project(31, 2)
+        y_out(0, 2)
         z_out(groups[8])
         second_factor(31)
-        out_product(0, 2, True)
-        out_product(0, 3)
+        finish(0, 1)
+        z_quant(1)
+        add_bo(0, 2, "z_grouped1")
+        store(0, 0)
+        out_product(0, 3, True)
         third_factor(30)
         z_turn(2)
-        store(0, 0)
         out_product(1, 0)
         out_product(1, 1)
         third_factor(31)
         z_turn_out(2)
-        y_out(0, 3)
+        y_out(1, 1)
         rank_sum(30)
         rank_sum(31)
-        finish(0, 2)
-        store(0, 1)
+        finish(0, 3)
+        out_product(1, 2, True)
+        out_product(1, 3)
         finish(1, 0)
-        z_quant(2)
-        add_bo(0, 3, "z_grouped2")
         z_out(groups[9])
-        out_product(1, 2)
-        out_product(1, 3, True)
-        y_out(1, 1)
-        add_bo(1, 1)
-        z_turn(3)
+        store(0, 2)
+        z_quant(2)
+        add_bo(1, 1, "z_grouped2")
         out_product(2, 0)
         out_product(2, 1)
+        z_turn(3)
         finish(1, 2)
-        store(0, 3)
+        y_out(2, 1)
         z_turn_out(3)
         finish(1, 3)
         out_product(2, 2)
         out_product(2, 3, True)
-        y_out(2, 1)
         finish(2, 0)
         store(1, 1)
         finish(2, 2)
@@ -549,10 +547,8 @@ def tile_lowranktrimodalfusion_kernel(tc, x, w_bytes, w_scale, b, omega, wo, bo,
         for i in range(4):
             out_product(3, i)
         finish(2, 3)
-        y_out(3, 1)
-        add_bo(3, 1)
         finish(3, 0)
+        finish(3, 1)
         store(2, 1)
         finish(3, 2)
         finish(3, 3)
-        store(3, 1)

@@ -288,38 +288,46 @@ def tile_lowranktrimodalfusion_kernel(tc, x, w_bytes, w_scale, b, omega, wo, bo,
                 in_=z_sum[g][:].rearrange("p a (q u e) -> p a u q e", u=2, e=2),
             )
 
-        zq = [mx_operand("z%d" % q, 256) for q in range(4)]
+        last_groups = groups[2 * (TILES - 1) :]
+        zq = [mx_operand("z%d" % q, g[3] * P) for q, g in enumerate(last_groups)]
         z_turned, z_grouped, y_of, o_of = {}, {}, {}, {}
         out_rows = out.rearrange("(p a) h -> p a h", a=8)
 
+        def place(q, i):
+            c, half, a0, na = last_groups[q]
+            return i % na, slice(i // na * BANK, (i // na + 1) * BANK)
+
         def z_turn(q):
-            t = bank([P, 2, 2, P])
-            words = z_rows[q // 2][:].rearrange("p a k -> p (a k)").bitcast(F32)
-            for i in range(4):
-                base = (4 * (q % 2) + i) * P
+            c, half, a0, na = last_groups[q]
+            t = bank([P, na, 2, P])
+            words = z_rows[half][:].rearrange("p a k -> p (a k)").bitcast(F32)
+            for i in range(2 * na):
+                base = (2 * a0 + i) * P
                 nc.tensor.transpose(t[:, i // 2, i % 2, :], words[:, base : base + P], ident[:])
             z_turned[q] = t
 
         def z_turn_out(q):
-            g = stage.tile([P, 256, PACK], BF16, name="z_grouped%d" % q, align_bytes=64, bufs=1)
+            g = stage.tile([P, last_groups[q][3] * P, PACK], BF16, name="z_grouped%d" % q, align_bytes=64, bufs=1)
             z_grouped[q] = g
-            dst = g[:].rearrange("p n j -> p (n j)").bitcast(F32).rearrange("p (a r u) -> p a r u", a=2, u=2)
+            dst = g[:].rearrange("p n j -> p (n j)").bitcast(F32).rearrange("p (a r u) -> p a r u", r=P, u=2)
             nc.scalar.copy(out=dst, in_=z_turned[q][:].rearrange("p a u r -> p a r u"))
 
         def z_quant(q):
             quantize(zq[q], z_grouped[q])
 
         def out_product(q, i, spare=False):
+            a, hs = place(q, i)
             y = psum.tile([P, BANK], F32, name="z") if spare else bank([P, BANK])
-            product(y[:], zq[q], i % 2 * P, woq[i // 2], 0, BANK)
+            product(y[:], zq[q], a * P, woq[hs.start // BANK], 0, BANK)
             y_of[q, i] = y
 
         def store(q, i):
-            hs = slice(i // 2 * BANK, (i // 2 + 1) * BANK)
-            nc.sync.dma_start(out=out_rows[:, 2 * q + i % 2, hs], in_=o_of[q, i][:])
+            a, hs = place(q, i)
+            c, half, a0, na = last_groups[q]
+            nc.sync.dma_start(out=out_rows[:, 4 * half + a0 + a, hs], in_=o_of[q, i][:])
 
         def finish(q, i):
-            hs = slice(i // 2 * BANK, (i // 2 + 1) * BANK)
+            a, hs = place(q, i)
             o = stage.tile([P, BANK], F32, name="o", bufs=8)
             o_of[q, i] = o
             nc.vector.tensor_tensor(out=o[:], in0=y_of[q, i][:], in1=bo_sb[:, hs], op=ALU.add)
@@ -333,7 +341,7 @@ def tile_lowranktrimodalfusion_kernel(tc, x, w_bytes, w_scale, b, omega, wo, bo,
             nc.scalar.copy(out=y[:], in_=y_of[q, i][:])
 
         def add_bo(q, i, tag="og"):
-            hs = slice(i // 2 * BANK, (i // 2 + 1) * BANK)
+            a, hs = place(q, i)
             o = stage.tile([P, BANK], F32, name=tag, align_bytes=64, bufs=2 if tag == "og" else 1)
             o_of[q, i] = o
             nc.gpsimd.tensor_tensor(out=o[:], in0=y_sb[q, i][:], in1=bo_sb[:, hs], op=ALU.add)
@@ -355,19 +363,20 @@ def tile_lowranktrimodalfusion_kernel(tc, x, w_bytes, w_scale, b, omega, wo, bo,
         vec_turned = bank([P, P])
         nc.tensor.transpose(vec_turned[:], vec32[:], ident[:])
         x_out(0, 0, 0, True)
+        x_out(0, 0, 1, True)
         w_quant(pieces[0])
-        x_out(0, 0, 1)
+        for j in range(PACK):
+            w_widen(0, 1, j, j >= 2)
         nc.vector.tensor_copy(out=cols[:], in_=vec_turned[:, 0:64])
         x_turn(1, 0, 0)
         x_turn(1, 0, 1)
-        for m in range(1, M):
-            for j in range(PACK):
-                w_widen(0, m, j)
         x_quant(0, 0)
         nc.vector.tensor_tensor(out=ob0[:], in0=vec_turned[:, 48:64], in1=cols[:, 0:16], op=ALU.mult)
-        x_out(1, 0, 0)
-        x_out(1, 0, 1)
+        x_out(1, 0, 0, True)
+        x_out(1, 0, 1, True)
         w_weave(pieces[1], False)
+        for j in range(PACK):
+            w_widen(0, 2, j, j >= 2)
         x_quant(1, 0)
         w_quant(pieces[1])
         w_weave(pieces[2])
@@ -397,13 +406,14 @@ def tile_lowranktrimodalfusion_kernel(tc, x, w_bytes, w_scale, b, omega, wo, bo,
         x_turn(1, 1, 0)
         x_turn(1, 1, 1)
         project(2, 1)
+        project(3, 1)
         x_quant(2, 0)
         x_quant(0, 1)
         w_quant(pieces[2])
         w_weave(pieces[3])
         first_factor(3)
         for pair in range(2):
-            x_out(1, 1, pair)
+            x_out(1, 1, pair, False)
         project(4, 0)
 
         late, early = {}, {}
@@ -419,7 +429,10 @@ def tile_lowranktrimodalfusion_kernel(tc, x, w_bytes, w_scale, b, omega, wo, bo,
             at(2 * (u + 3) + 1, rank_sum, u)
         for g in groups[:6]:
             at(2 * (ends[g] + 3 + 1) + 1, z_out, g)
+        due = [7,11,17,23,29,35,41,47,53]
+        on_vector = [pieces[i] + (3,) for i in []]
         planes_left = [(c, m, j) for c in range(1, TILES) for m in range(M) for j in range(PACK)][6:]
+        planes_left = [pl for pl in planes_left if pl not in on_vector]
         for i, (c, m, j) in enumerate(planes_left):
             at(2 * (2 + (i // 3 if i < 12 else 4 + 17 * (i - 12) // 18)) + 1, w_widen, c, m, j)
         deferred = [(4, 1), (24, 1), (24, 2)]
@@ -427,11 +440,11 @@ def tile_lowranktrimodalfusion_kernel(tc, x, w_bytes, w_scale, b, omega, wo, bo,
         at(5, x_turn, 2, 1, 1)
         at(7, x_quant, 1, 1)
         at(11, x_quant, 2, 1)
-        due = [7,11,17,23,29,35,41,47,53]
-
         for i, pc in enumerate(pieces[3:]):
+            if i + 4 < len(pieces) and pieces[i + 4] + (3,) in on_vector:
+                at(due[i], w_widen, *pieces[i + 4], 3, False)
             at(due[i], w_quant, pc)
-            if i + 4 < len(pieces) - 0:
+            if i + 4 < len(pieces):
                 at(due[i], w_weave, pieces[i + 4])
         at(7, project, 4, 1)
         at(47, project, 24, 1)

@@ -191,7 +191,7 @@ def tile_lowranktrimodalfusion_kernel(tc, x, w_bytes, w_scale, b, omega, wo, bo,
             q = 16 * row + 4 * r + c
             return cols[:, q : q + 1]
 
-        groups = [(c, half, 0, 4) for c in range(TILES - 1) for half in range(2)] + [(TILES - 1, q // 2, 2 * (q % 2), 2) for q in range(4)]
+        groups = [(0, 0, 0, 4), (0, 1, 0, 4), (1, 0, 0, 4), (1, 1, 0, 4), (2, 0, 0, 4), (2, 1, 0, 4), (3, 0, 0, 4), (3, 1, 0, 2), (3, 1, 2, 2)]
         units = []
         for g in groups:
             na = g[3]
@@ -280,15 +280,17 @@ def tile_lowranktrimodalfusion_kernel(tc, x, w_bytes, w_scale, b, omega, wo, bo,
                         start=r == 0 and a == 0, stop=r == R - 1 and a == na - 1,
                     )
 
-        def z_out(g):
-            c, half, a0, na = g
+        def z_out(g, first=0, na=None):
+            c, half, a0 = g[:3]
+            na = na or g[3]
+            a0 = a0 + first
             dst = z_rows[half][:, a0 : a0 + na, :].rearrange("p a (u q) -> p a u q", u=2)[:, :, :, 64 * c : 64 * c + 64]
             nc.scalar.copy(
                 out=dst.rearrange("p a u (q e) -> p a u q e", e=2),
-                in_=z_sum[g][:].rearrange("p a (q u e) -> p a u q e", u=2, e=2),
+                in_=z_sum[g][:, first : first + na, :].rearrange("p a (q u e) -> p a u q e", u=2, e=2),
             )
 
-        last_groups = groups[2 * (TILES - 1) :]
+        last_groups = [(TILES - 1, q // 2, 2 * (q % 2), 2) for q in range(4)]
         zq = [mx_operand("z%d" % q, g[3] * P) for q, g in enumerate(last_groups)]
         z_turned, z_grouped, y_of, o_of = {}, {}, {}, {}
         out_rows = out.rearrange("(p a) h -> p a h", a=8)
@@ -485,76 +487,77 @@ def tile_lowranktrimodalfusion_kernel(tc, x, w_bytes, w_scale, b, omega, wo, bo,
         rank_sum(25)
         third_factor(26)
         project(29, 1)
-        z_out(groups[6])
         first_factor(30)
         third_factor(27)
-        project(31, 0)
+        project(30, 1)
         project(28, 2)
-        z_turn(0)
         rank_sum(26)
         rank_sum(27)
         second_factor(28)
+        factor_out(30, 1)
         wo_quant(0)
         wo_quant(1)
-        z_turn_out(0)
-        z_out(groups[7])
-        first_factor(31)
+        second_on_gpsimd(30, "woven")
+        z_out(groups[6], 0, 2)
+        z_out(groups[6], 2, 2)
+        project(31, 0)
         project(29, 2)
         second_factor(29)
-        project(30, 1)
-        z_quant(0)
-        third_factor(28)
-        out_product(0, 0, True)
+        z_turn(0)
         z_turn(1)
         project(31, 1)
-        out_product(0, 1)
-        y_out(0, 0)
-        add_bo(0, 0)
+        third_factor(28)
+        z_turn_out(0)
         z_turn_out(1)
+        first_factor(31)
         third_factor(29)
         project(30, 2)
-        out_product(0, 2, True)
-        second_factor(30)
+        z_quant(0)
+        z_quant(1)
         rank_sum(28)
         rank_sum(29)
-        project(31, 2)
-        y_out(0, 2)
-        z_out(groups[8])
+        out_product(0, 0, True)
+        out_product(0, 1)
         second_factor(31)
-        finish(0, 1)
-        z_quant(1)
-        add_bo(0, 2, "z_grouped1")
-        store(0, 0)
+        project(31, 2)
+        y_out(0, 0)
+        add_bo(0, 0)
+        z_out(groups[7])
+        out_product(0, 2)
         out_product(0, 3, True)
         third_factor(30)
+        y_out(0, 2)
+        add_bo(0, 2)
+        finish(0, 1)
         z_turn(2)
         out_product(1, 0)
         out_product(1, 1)
         third_factor(31)
         z_turn_out(2)
-        y_out(1, 1)
+        finish(0, 3)
+        store(0, 0)
         rank_sum(30)
         rank_sum(31)
-        finish(0, 3)
         out_product(1, 2, True)
         out_product(1, 3)
         finish(1, 0)
-        z_out(groups[9])
+        z_out(groups[8])
+        y_out(1, 3)
+        finish(1, 1)
         store(0, 2)
+        z_turn(3)
         z_quant(2)
-        add_bo(1, 1, "z_grouped2")
+        add_bo(1, 3, "z_grouped2")
+        z_turn_out(3)
         out_product(2, 0)
         out_product(2, 1)
-        z_turn(3)
         finish(1, 2)
-        y_out(2, 1)
-        z_turn_out(3)
-        finish(1, 3)
         out_product(2, 2)
         out_product(2, 3, True)
+        y_out(2, 1)
         finish(2, 0)
-        store(1, 1)
         finish(2, 2)
+        store(1, 3)
         z_quant(3)
         add_bo(2, 1, "z_grouped3")
         for i in range(4):

@@ -191,7 +191,7 @@ def tile_lowranktrimodalfusion_kernel(tc, x, w_bytes, w_scale, b, omega, wo, bo,
             q = 16 * row + 4 * r + c
             return cols[:, q : q + 1]
 
-        groups = [(0, 0, 0, 4), (0, 1, 0, 4), (1, 0, 0, 4), (1, 1, 0, 4), (2, 0, 0, 4), (2, 1, 0, 4), (3, 0, 0, 4), (3, 1, 0, 2), (3, 1, 2, 2)]
+        groups = [(c, half, 0, 4) for c in range(TILES - 1) for half in range(2)] + [(TILES - 1, q // 2, 2 * (q % 2), 2) for q in range(4)]
         units = []
         for g in groups:
             na = g[3]
@@ -280,17 +280,15 @@ def tile_lowranktrimodalfusion_kernel(tc, x, w_bytes, w_scale, b, omega, wo, bo,
                         start=r == 0 and a == 0, stop=r == R - 1 and a == na - 1,
                     )
 
-        def z_out(g, first=0, na=None):
-            c, half, a0 = g[:3]
-            na = na or g[3]
-            a0 = a0 + first
+        def z_out(g):
+            c, half, a0, na = g
             dst = z_rows[half][:, a0 : a0 + na, :].rearrange("p a (u q) -> p a u q", u=2)[:, :, :, 64 * c : 64 * c + 64]
             nc.scalar.copy(
                 out=dst.rearrange("p a u (q e) -> p a u q e", e=2),
-                in_=z_sum[g][:, first : first + na, :].rearrange("p a (q u e) -> p a u q e", u=2, e=2),
+                in_=z_sum[g][:].rearrange("p a (q u e) -> p a u q e", u=2, e=2),
             )
 
-        last_groups = [(TILES - 1, q // 2, 2 * (q % 2), 2) for q in range(4)]
+        last_groups = groups[2 * (TILES - 1) :]
         zq = [mx_operand("z%d" % q, g[3] * P) for q, g in enumerate(last_groups)]
         z_turned, z_grouped, y_of, o_of = {}, {}, {}, {}
         out_rows = out.rearrange("(p a) h -> p a h", a=8)
@@ -400,11 +398,11 @@ def tile_lowranktrimodalfusion_kernel(tc, x, w_bytes, w_scale, b, omega, wo, bo,
         second_factor(0)
         second_factor(1)
         project(3, 0)
+        x_out(0, 1, 0, True)
         first_factor(2)
         for j in range(2):
             w_widen(1, 1, j)
-        for pair in range(2):
-            x_out(0, 1, pair)
+        x_out(0, 1, 1)
         x_turn(1, 1, 0)
         x_turn(1, 1, 1)
         project(2, 1)
@@ -436,7 +434,7 @@ def tile_lowranktrimodalfusion_kernel(tc, x, w_bytes, w_scale, b, omega, wo, bo,
         planes_left = [(c, m, j) for c in range(1, TILES) for m in range(M) for j in range(PACK)][6:]
         planes_left = [pl for pl in planes_left if pl not in on_vector]
         for i, (c, m, j) in enumerate(planes_left):
-            at(2 * (2 + (i // 3 if i < 12 else 4 + 17 * (i - 12) // 18)) + 1, w_widen, c, m, j)
+            at(2 * (2 + (4 * i // 9 if i < 9 else 4 + 17 * (i - 9) // 21)) + 1, w_widen, c, m, j)
         deferred = [(4, 1), (24, 1), (24, 2)]
         at(5, x_turn, 2, 1, 0)
         at(5, x_turn, 2, 1, 1)
@@ -450,7 +448,7 @@ def tile_lowranktrimodalfusion_kernel(tc, x, w_bytes, w_scale, b, omega, wo, bo,
                 at(due[i], w_weave, pieces[i + 4])
         at(7, project, 4, 1)
         at(47, project, 24, 1)
-        at(7, x_out, 2, 1, 0)
+        at(6, x_out, 2, 1, 0, True)
         at(7, x_out, 2, 1, 1)
         at(47, wo_weave, 0)
         at(51, wo_weave, 1)
@@ -487,77 +485,76 @@ def tile_lowranktrimodalfusion_kernel(tc, x, w_bytes, w_scale, b, omega, wo, bo,
         rank_sum(25)
         third_factor(26)
         project(29, 1)
+        z_out(groups[6])
         first_factor(30)
         third_factor(27)
-        project(30, 1)
+        project(31, 0)
         project(28, 2)
+        z_turn(0)
         rank_sum(26)
         rank_sum(27)
         second_factor(28)
-        factor_out(30, 1)
         wo_quant(0)
         wo_quant(1)
-        second_on_gpsimd(30, "woven")
-        z_out(groups[6], 0, 2)
-        z_out(groups[6], 2, 2)
-        project(31, 0)
+        z_turn_out(0)
+        z_out(groups[7])
+        first_factor(31)
         project(29, 2)
         second_factor(29)
-        z_turn(0)
+        project(30, 1)
+        z_quant(0)
+        third_factor(28)
+        out_product(0, 0, True)
         z_turn(1)
         project(31, 1)
-        third_factor(28)
-        z_turn_out(0)
-        z_turn_out(1)
-        first_factor(31)
-        third_factor(29)
-        project(30, 2)
-        z_quant(0)
-        z_quant(1)
-        rank_sum(28)
-        rank_sum(29)
-        out_product(0, 0, True)
         out_product(0, 1)
-        second_factor(31)
-        project(31, 2)
         y_out(0, 0)
         add_bo(0, 0)
-        z_out(groups[7])
-        out_product(0, 2)
+        z_turn_out(1)
+        third_factor(29)
+        project(30, 2)
+        out_product(0, 2, True)
+        second_factor(30)
+        rank_sum(28)
+        rank_sum(29)
+        project(31, 2)
+        y_out(0, 2)
+        z_out(groups[8])
+        second_factor(31)
+        finish(0, 1)
+        z_quant(1)
+        add_bo(0, 2, "z_grouped1")
+        store(0, 0)
         out_product(0, 3, True)
         third_factor(30)
-        y_out(0, 2)
-        add_bo(0, 2)
-        finish(0, 1)
         z_turn(2)
         out_product(1, 0)
         out_product(1, 1)
         third_factor(31)
         z_turn_out(2)
-        finish(0, 3)
-        store(0, 0)
+        y_out(1, 1)
         rank_sum(30)
         rank_sum(31)
+        finish(0, 3)
         out_product(1, 2, True)
         out_product(1, 3)
         finish(1, 0)
-        z_out(groups[8])
-        y_out(1, 3)
-        finish(1, 1)
+        z_out(groups[9])
         store(0, 2)
-        z_turn(3)
         z_quant(2)
-        add_bo(1, 3, "z_grouped2")
-        z_turn_out(3)
+        add_bo(1, 1, "z_grouped2")
         out_product(2, 0)
         out_product(2, 1)
+        z_turn(3)
         finish(1, 2)
+        y_out(2, 1)
+        z_turn_out(3)
+        finish(1, 3)
         out_product(2, 2)
         out_product(2, 3, True)
-        y_out(2, 1)
         finish(2, 0)
+        store(1, 1)
         finish(2, 2)
-        store(1, 3)
         z_quant(3)
         add_bo(2, 1, "z_grouped3")
         for i in range(4):

@@ -21,6 +21,11 @@ HALF = 512
 TILES = F // P
 BANK = 512
 RING = 7
+LEAD = 2
+LAG = 3
+TURN = 3
+EARLY_PLANES = 9
+RUN = 4
 
 
 def tile_lowranktrimodalfusion_kernel(tc, x, w_bytes, w_scale, b, omega, wo, bo, out):
@@ -33,9 +38,13 @@ def tile_lowranktrimodalfusion_kernel(tc, x, w_bytes, w_scale, b, omega, wo, bo,
 
         taken = []
 
-        def bank(shape, dtype=F32):
-            t = psum.tile(shape, dtype, name="ring%d" % (len(taken) % RING))
+        def bank(shape):
+            t = psum.tile(shape, F32, name="ring%d" % (len(taken) % RING))
             taken.append(t)
+            return t
+
+        def z_bank(shape):
+            t = psum.tile(shape, F32, name="z")
             return t
 
         ws = keep.tile([P, PACK], F32, name="ws")
@@ -51,28 +60,26 @@ def tile_lowranktrimodalfusion_kernel(tc, x, w_bytes, w_scale, b, omega, wo, bo,
         nc.gpsimd.memset(vec32[64:128, :], 0.0)
 
         pieces = [(c, m) for c in range(TILES) for m in range(M)]
-        w_raw, x_raw = {}, {}
-        for jj in range(2):
-            t = keep.tile([P, 2, R * P], U8, name="w_raw%d" % jj)
-            w_raw[0, 0, jj] = t
+        first_raw, w_raw, x_raw = {}, {}, {}
+        for part in range(2):
+            t = keep.tile([P, 2, R * P], U8, name="first_raw%d" % part)
+            first_raw[part] = t
         for m in range(M):
             for half in range(2):
                 t = keep.tile([P, 4, D], BF16, name="x_raw%d%d" % (m, half))
                 x_raw[m, half] = t
         wo_raw = keep.tile([P, PACK, H], BF16, name="wo_raw")
         bo_sb = keep.tile([P, H], BF16, name="bo_sb")
-        w_whole = {}
 
         def load_w(c, m):
             src = w_bytes[m].rearrange("(p j) (r f) -> p (j r) f", j=PACK, r=R)[:, :, c * P : (c + 1) * P]
-            if (c, m) == (0, 0):
-                for jj in range(2):
-                    nc.sync.dma_start(
-                        out=w_raw[c, m, jj][:].rearrange("p j (r f) -> p (j r) f", r=R), in_=src[:, 8 * jj : 8 * jj + 8, :]
-                    )
+            if (c, m) == pieces[0]:
+                for part in range(2):
+                    rows = slice(2 * R * part, 2 * R * (part + 1))
+                    nc.sync.dma_start(out=first_raw[part][:].rearrange("p j (r f) -> p (j r) f", r=R), in_=src[:, rows, :])
             else:
-                t = keep.tile([P, PACK, R * P], U8, name="w_whole%d%d" % (c, m))
-                w_whole[c, m] = t
+                t = keep.tile([P, PACK, R * P], U8, name="w_raw%d%d" % (c, m))
+                w_raw[c, m] = t
                 nc.sync.dma_start(out=t[:].rearrange("p j (r f) -> p (j r) f", r=R), in_=src)
 
         def load_x(m, half):
@@ -112,16 +119,17 @@ def tile_lowranktrimodalfusion_kernel(tc, x, w_bytes, w_scale, b, omega, wo, bo,
         xq = {(m, half): mx_operand("x%d%d" % (m, half), HALF) for m in range(M) for half in range(2)}
         x_turned, x_grouped = {}, {}
 
-        def x_turn(m, half, pair):
-            t = bank([P, 2, 2, P])
+        def x_turn(m, half):
             words = x_raw[m, half][:].rearrange("p a k -> p (a k)").bitcast(F32)
-            for i in range(2):
-                base = (2 * pair + i) * 256
-                for u in range(2):
-                    nc.tensor.transpose(t[:, i, u, :], words[:, base + u : base + 256 : 2], ident[:])
-            x_turned[m, half, pair] = t
+            for pair in range(2):
+                t = bank([P, 2, 2, P])
+                for i in range(2):
+                    base = (2 * pair + i) * (D // 2)
+                    for u in range(2):
+                        nc.tensor.transpose(t[:, i, u, :], words[:, base + u : base + D // 2 : 2], ident[:])
+                x_turned[m, half, pair] = t
 
-        def x_out(m, half, pair, on_scalar=False):
+        def x_out(m, half, pair, on_scalar):
             if pair == 0:
                 g = stage.tile([P, HALF, PACK], BF16, name="x_grouped", align_bytes=64, bufs=3)
                 x_grouped[m, half] = g
@@ -136,78 +144,77 @@ def tile_lowranktrimodalfusion_kernel(tc, x, w_bytes, w_scale, b, omega, wo, bo,
         def x_quant(m, half):
             quantize(xq[m, half], x_grouped[m, half])
 
-        wq = {pc: mx_operand("w%d%d" % pc, R * P) for pc in pieces}
-        woq = [mx_operand("wo%d" % i, BANK) for i in range(2)]
+        wq = {piece: mx_operand("w%d%d" % piece, R * P) for piece in pieces}
+        woq = [mx_operand("wo%d" % side, BANK) for side in range(2)]
         planes, woven = {}, {}
 
-        def w_widen(c, m, j, on_scalar=True):
+        def planes_tile(shape):
+            t = stage.tile(shape, BF16, name="planes", align_bytes=64, bufs=5)
+            return t
+
+        def widen(piece, j, on_scalar):
             if j == 0:
-                t = stage.tile([P, PACK, R * P], BF16, name="planes", align_bytes=64, bufs=5)
-                planes[c, m] = t
-            dst = planes[c, m][:, j, :]
-            raw = w_raw[c, m, j // 2][:, j % 2, :] if (c, m) == (0, 0) else w_whole[c, m][:, j, :]
-            src = raw.bitcast(FP8)
+                planes[piece] = planes_tile([P, PACK, R * P])
+            raw = first_raw[j // 2][:, j % 2, :] if piece == pieces[0] else w_raw[piece][:, j, :]
+            dst, src = planes[piece][:, j, :], raw.bitcast(FP8)
             if on_scalar:
                 nc.scalar.activation(out=dst, in_=src, func=ACT.Copy, scale=ws[:, j : j + 1])
             else:
                 nc.vector.tensor_scalar(out=dst, in0=src, scalar1=ws[:, j : j + 1], scalar2=None, op0=ALU.mult)
 
-        def weave(key, src, width, on_gpsimd=True, tag="woven"):
-            dst = stage.tile([P, width, PACK], BF16, name=tag, align_bytes=64, bufs=1)
+        def in_runs(dst, src):
+            return dst.rearrange("p (c i) j -> p c j i", i=RUN), src.rearrange("p j (c i) -> p c j i", i=RUN)
+
+        def weave(key, src, on_gpsimd):
+            dst = stage.tile([P, BANK, PACK], BF16, name="woven", align_bytes=64, bufs=1)
             woven[key] = dst
             if on_gpsimd:
                 nc.gpsimd.tensor_scalar(
-                    out=dst[:], in0=src[:].rearrange("p j n -> p n j"), scalar1=1.0, scalar2=0.0,
-                    op0=ALU.mult, op1=ALU.add,
+                    out=dst[:], in0=src.rearrange("p j n -> p n j"), scalar1=1.0, scalar2=0.0, op0=ALU.mult, op1=ALU.add
                 )
             else:
-                nc.vector.tensor_copy(
-                    out=dst[:].rearrange("p (c i) j -> p c j i", i=4),
-                    in_=src[:].rearrange("p j (c i) -> p c j i", i=4),
-                )
+                to, of = in_runs(dst[:], src)
+                nc.vector.tensor_copy(out=to, in_=of)
 
-        def w_weave(pc, on_gpsimd=True, tag="woven"):
-            weave(pc, planes[pc], R * P, on_gpsimd, tag)
+        def w_weave(piece, on_gpsimd):
+            weave(piece, planes[piece][:], on_gpsimd)
 
-        def w_quant(pc):
-            quantize(wq[pc], woven[pc])
+        def w_quant(piece):
+            quantize(wq[piece], woven[piece])
 
-        def wo_weave(i):
-            if i % 2 == 0:
-                t = stage.tile([P, BANK, PACK], BF16, name="planes", align_bytes=64, bufs=5)
-                woven["wo", i // 2] = t
-            nc.scalar.copy(
-                out=woven["wo", i // 2][:, 256 * (i % 2) : 256 * (i % 2 + 1), :].rearrange("p (c i) j -> p c j i", i=4),
-                in_=wo_raw[:, :, 256 * i : 256 * (i + 1)].rearrange("p j (c i) -> p c j i", i=4),
-            )
+        def wo_left_weave(part):
+            if part == 0:
+                woven["wo", 0] = planes_tile([P, BANK, PACK])
+            cs = slice(part * BANK // 2, (part + 1) * BANK // 2)
+            to, of = in_runs(woven["wo", 0][:, cs, :], wo_raw[:, :, cs])
+            nc.scalar.copy(out=to, in_=of)
 
-        def wo_quant(i):
-            quantize(woq[i], woven["wo", i])
+        def wo_right_weave():
+            weave(("wo", 1), wo_raw[:, :, BANK:H], True)
+
+        def wo_quant(side):
+            quantize(woq[side], woven["wo", side])
 
         cols = keep.tile([P, 64], F32, name="cols")
-        ob0 = keep.tile([P, 16], F32, name="ob0")
+        omega_b0 = keep.tile([P, 16], F32, name="omega_b0")
 
-        def column(row, r, c):
+        def column(tile, row, r, c):
             q = 16 * row + 4 * r + c
-            return cols[:, q : q + 1]
+            return tile[:, q : q + 1]
 
-        groups = [(c, half, 0, 4) for c in range(TILES - 1) for half in range(2)] + [(TILES - 1, q // 2, 2 * (q % 2), 2) for q in range(4)]
-        units = []
-        for g in groups:
-            na = g[3]
-            per = 4 // na
-            for i in range(R // per):
-                units.append((g, list(range(i * per, (i + 1) * per))))
-        last = len(units) - 1
-        h_of, a_of, ab_of, p_of, z_sum = {}, {}, {}, {}, {}
-        z_rows = {}
+        halves = [(c, half, 0, 4) for c in range(TILES - 1) for half in range(2)]
+        quarters = [(TILES - 1, q // 2, 2 * (q % 2), 2) for q in range(4)]
+        units = [(g, [r]) for g in halves for r in range(R)] + [(g, [r, r + 1]) for g in quarters for r in (0, 2)]
+        wide = R * len(halves)
+        h_of, a_of, ab_of, p_of, z_sum, z_rows = {}, {}, {}, {}, {}, {}
         for half in range(2):
             t = keep.tile([P, 4, F], BF16, name="z_rows%d" % half)
             z_rows[half] = t
 
         def parts(u):
-            (c, half, a0, na), ranks = units[u]
-            return [(r, slice(i * na * P, (i + 1) * na * P)) for i, r in enumerate(ranks)]
+            g, ranks = units[u]
+            width = g[3] * P
+            return [(r, slice(i * width, (i + 1) * width)) for i, r in enumerate(ranks)]
 
         def project(u, m):
             c, half, a0, na = units[u][0]
@@ -218,67 +225,43 @@ def tile_lowranktrimodalfusion_kernel(tc, x, w_bytes, w_scale, b, omega, wo, bo,
 
         def first_factor(u):
             c = units[u][0][0]
-            a = stage.tile([P, BANK], F32, name="a", bufs=5)
+            a = stage.tile([P, BANK], F32, name="a", bufs=LEAD + 3)
             a_of[u] = a
             for r, cs in parts(u):
                 nc.scalar.activation(
-                    out=a[:, cs], in_=h_of[u, 0][:, cs], func=ACT.Identity, scale=column(3, r, c),
-                    bias=ob0[:, 4 * r + c : 4 * r + c + 1],
+                    out=a[:, cs], in_=h_of[u, 0][:, cs], func=ACT.Identity, scale=column(cols, M, r, c), bias=column(omega_b0, 0, r, c)
+                )
+
+        def times_factor(dst, u, m, so_far):
+            c = units[u][0][0]
+            for r, cs in parts(u):
+                nc.vector.scalar_tensor_tensor(
+                    out=dst[:, cs], in0=h_of[u, m][:, cs], scalar=column(cols, m, r, c), in1=so_far[:, cs], op0=ALU.add, op1=ALU.mult
                 )
 
         def second_factor(u):
-            c = units[u][0][0]
-            ab = stage.tile([P, BANK], F32, name="ab", bufs=5)
+            ab = stage.tile([P, BANK], F32, name="ab", bufs=LAG + 2)
             ab_of[u] = ab
-            for r, cs in parts(u):
-                nc.vector.scalar_tensor_tensor(
-                    out=ab[:, cs], in0=h_of[u, 1][:, cs], scalar=column(1, r, c), in1=a_of[u][:, cs], op0=ALU.add, op1=ALU.mult
-                )
+            times_factor(ab, u, 1, a_of[u])
 
         def third_factor(u):
-            c = units[u][0][0]
             p = stage.tile([P, BANK], F32, name="p", bufs=7)
             p_of[u] = p
-            for r, cs in parts(u):
-                nc.vector.scalar_tensor_tensor(
-                    out=p[:, cs], in0=h_of[u, 2][:, cs], scalar=column(2, r, c), in1=ab_of[u][:, cs], op0=ALU.add, op1=ALU.mult
-                )
+            times_factor(p, u, 2, ab_of[u])
 
-        factor_sb = {}
-
-        def factor_out(u, m):
-            c = units[u][0][0]
-            t = stage.tile([P, BANK], F32, name="y", bufs=4)
-            factor_sb[u, m] = t
-            for r, cs in parts(u):
-                nc.scalar.activation(out=t[:, cs], in_=h_of[u, m][:, cs], func=ACT.Identity, bias=column(m, r, c))
-
-        def third_on_gpsimd(u, tag="pg"):
-            p = stage.tile([P, BANK], F32, name=tag, align_bytes=64, bufs=1)
-            p_of[u] = p
-            nc.gpsimd.tensor_tensor(out=p[:], in0=factor_sb[u, 2][:], in1=ab_of[u][:], op=ALU.mult)
-
-        def second_on_gpsimd(u, tag="abg"):
-            ab = stage.tile([P, BANK], F32, name=tag, align_bytes=64, bufs=1)
-            ab_of[u] = ab
-            nc.gpsimd.tensor_tensor(out=ab[:], in0=factor_sb[u, 1][:], in1=a_of[u][:], op=ALU.mult)
-
-        def rank_sum(u):
-            g, ranks = units[u]
-            na = g[3]
-            if ranks[0] == 0:
-                if na < 4 and u > 24:
-                    z = bank([P, na, P])
-                else:
-                    z = psum.tile([P, na, P], F32, name="z")
-                z_sum[g] = z
-            for i, r in enumerate(ranks):
-                for a in range(na):
-                    at_col = (i * na + a) * P
-                    nc.tensor.matmul(
-                        z_sum[g][:, a, :], lhsT=p_of[u][:, at_col : at_col + P], rhs=ident[:], is_transpose=True,
-                        start=r == 0 and a == 0, stop=r == R - 1 and a == na - 1,
-                    )
+        def rank_sums(first):
+            for u in (first, first + 1):
+                g, ranks = units[u]
+                na = g[3]
+                if ranks[0] == 0:
+                    z_sum[g] = bank([P, na, P]) if u > wide else z_bank([P, na, P])
+                for i, r in enumerate(ranks):
+                    for a in range(na):
+                        cs = slice((i * na + a) * P, (i * na + a + 1) * P)
+                        nc.tensor.matmul(
+                            z_sum[g][:, a, :], lhsT=p_of[u][:, cs], rhs=ident[:], is_transpose=True,
+                            start=r == 0 and a == 0, stop=r == R - 1 and a == na - 1,
+                        )
 
         def z_out(g):
             c, half, a0, na = g
@@ -288,26 +271,23 @@ def tile_lowranktrimodalfusion_kernel(tc, x, w_bytes, w_scale, b, omega, wo, bo,
                 in_=z_sum[g][:].rearrange("p a (q u e) -> p a u q e", u=2, e=2),
             )
 
-        last_groups = groups[2 * (TILES - 1) :]
-        zq = [mx_operand("z%d" % q, g[3] * P) for q, g in enumerate(last_groups)]
-        z_turned, z_grouped, y_of, o_of = {}, {}, {}, {}
+        zq = [mx_operand("z%d" % q, 2 * P) for q in range(4)]
+        z_turned, z_grouped, y_of, y_sb, o_of = {}, {}, {}, {}, {}
         out_rows = out.rearrange("(p a) h -> p a h", a=8)
 
-        def place(q, i):
-            c, half, a0, na = last_groups[q]
-            return i % na, slice(i // na * BANK, (i // na + 1) * BANK)
+        def side_cols(i):
+            return slice(i // 2 * BANK, (i // 2 + 1) * BANK)
 
         def z_turn(q):
-            c, half, a0, na = last_groups[q]
-            t = bank([P, na, 2, P])
-            words = z_rows[half][:].rearrange("p a k -> p (a k)").bitcast(F32)
-            for i in range(2 * na):
-                base = (2 * a0 + i) * P
+            t = bank([P, 2, 2, P])
+            words = z_rows[q // 2][:].rearrange("p a k -> p (a k)").bitcast(F32)
+            for i in range(4):
+                base = (4 * (q % 2) + i) * P
                 nc.tensor.transpose(t[:, i // 2, i % 2, :], words[:, base : base + P], ident[:])
             z_turned[q] = t
 
         def z_turn_out(q):
-            g = stage.tile([P, last_groups[q][3] * P, PACK], BF16, name="z_grouped%d" % q, align_bytes=64, bufs=1)
+            g = stage.tile([P, 2 * P, PACK], BF16, name="z_grouped%d" % q, align_bytes=64, bufs=1)
             z_grouped[q] = g
             dst = g[:].rearrange("p n j -> p (n j)").bitcast(F32).rearrange("p (a r u) -> p a r u", r=P, u=2)
             nc.scalar.copy(out=dst, in_=z_turned[q][:].rearrange("p a u r -> p a r u"))
@@ -315,38 +295,31 @@ def tile_lowranktrimodalfusion_kernel(tc, x, w_bytes, w_scale, b, omega, wo, bo,
         def z_quant(q):
             quantize(zq[q], z_grouped[q])
 
-        def out_product(q, i, spare=False):
-            a, hs = place(q, i)
-            y = psum.tile([P, BANK], F32, name="z") if spare else bank([P, BANK])
-            product(y[:], zq[q], a * P, woq[hs.start // BANK], 0, BANK)
+        def out_product(q, i, take=bank):
+            y = take([P, BANK])
+            product(y[:], zq[q], i % 2 * P, woq[i // 2], 0, BANK)
             y_of[q, i] = y
 
         def store(q, i):
-            a, hs = place(q, i)
-            c, half, a0, na = last_groups[q]
-            nc.sync.dma_start(out=out_rows[:, 4 * half + a0 + a, hs], in_=o_of[q, i][:])
+            nc.sync.dma_start(out=out_rows[:, 2 * q + i % 2, side_cols(i)], in_=o_of[q, i][:])
 
         def finish(q, i):
-            a, hs = place(q, i)
             o = stage.tile([P, BANK], F32, name="o", bufs=8)
             o_of[q, i] = o
-            nc.vector.tensor_tensor(out=o[:], in0=y_of[q, i][:], in1=bo_sb[:, hs], op=ALU.add)
+            nc.vector.tensor_tensor(out=o[:], in0=y_of[q, i][:], in1=bo_sb[:, side_cols(i)], op=ALU.add)
             store(q, i)
-
-        y_sb = {}
 
         def y_out(q, i):
             y = stage.tile([P, BANK], F32, name="y", bufs=4)
             y_sb[q, i] = y
             nc.scalar.copy(out=y[:], in_=y_of[q, i][:])
 
-        def add_bo(q, i, tag="og"):
-            a, hs = place(q, i)
-            o = stage.tile([P, BANK], F32, name=tag, align_bytes=64, bufs=2 if tag == "og" else 1)
+        def add_bo(q, i, buffer):
+            o = stage.tile([P, BANK], F32, name=buffer, align_bytes=64, bufs=1)
             o_of[q, i] = o
-            nc.gpsimd.tensor_tensor(out=o[:], in0=y_sb[q, i][:], in1=bo_sb[:, hs], op=ALU.add)
+            nc.gpsimd.tensor_tensor(out=o[:], in0=y_sb[q, i][:], in1=bo_sb[:, side_cols(i)], op=ALU.add)
 
-        unread = psum.tile([P, BANK], F32, name="z")
+        unread = z_bank([P, BANK])
 
         def warm_up(count):
             for i in range(count):
@@ -354,192 +327,178 @@ def tile_lowranktrimodalfusion_kernel(tc, x, w_bytes, w_scale, b, omega, wo, bo,
 
         warm_up(5)
         for j in range(PACK):
-            w_widen(0, 0, j, j == 3)
-        w_weave(pieces[0], False)
+            widen(pieces[0], j, on_scalar=j == 3)
+        w_weave(pieces[0], on_gpsimd=False)
         nc.vector.tensor_copy(out=vec32[0:64, :], in_=vec[0:64, :])
-        x_turn(0, 0, 0)
-        x_turn(0, 0, 1)
+        x_turn(0, 0)
         warm_up(2)
         vec_turned = bank([P, P])
         nc.tensor.transpose(vec_turned[:], vec32[:], ident[:])
-        x_out(0, 0, 0, True)
-        x_out(0, 0, 1, True)
+        for pair in range(2):
+            x_out(0, 0, pair, on_scalar=True)
         w_quant(pieces[0])
         for j in range(PACK):
-            w_widen(0, 1, j, j >= 2)
+            widen(pieces[1], j, on_scalar=j >= 2)
         nc.vector.tensor_copy(out=cols[:], in_=vec_turned[:, 0:64])
-        x_turn(1, 0, 0)
-        x_turn(1, 0, 1)
+        x_turn(1, 0)
         x_quant(0, 0)
-        nc.vector.tensor_tensor(out=ob0[:], in0=vec_turned[:, 48:64], in1=cols[:, 0:16], op=ALU.mult)
-        x_out(1, 0, 0, True)
-        x_out(1, 0, 1, True)
-        w_weave(pieces[1], False)
+        nc.vector.tensor_tensor(out=omega_b0[:], in0=vec_turned[:, 48:64], in1=cols[:, 0:16], op=ALU.mult)
+        for pair in range(2):
+            x_out(1, 0, pair, on_scalar=True)
+        w_weave(pieces[1], on_gpsimd=False)
         for j in range(PACK):
-            w_widen(0, 2, j, j >= 2)
+            widen(pieces[2], j, on_scalar=j >= 2)
         x_quant(1, 0)
         w_quant(pieces[1])
-        w_weave(pieces[2])
-        project(0, 0)
-        project(1, 0)
-        x_turn(2, 0, 0)
-        x_turn(2, 0, 1)
-        first_factor(0)
-        first_factor(1)
+        w_weave(pieces[2], on_gpsimd=True)
+        for u in range(2):
+            project(u, 0)
+        x_turn(2, 0)
+        for u in range(2):
+            first_factor(u)
         for j in range(PACK):
-            w_widen(1, 0, j)
+            widen(pieces[3], j, on_scalar=True)
         for pair in range(2):
-            x_out(2, 0, pair)
-        project(0, 1)
-        project(1, 1)
-        x_turn(0, 1, 0)
-        x_turn(0, 1, 1)
+            x_out(2, 0, pair, on_scalar=False)
+        for u in range(2):
+            project(u, 1)
+        x_turn(0, 1)
         project(2, 0)
-        second_factor(0)
-        second_factor(1)
+        for u in range(2):
+            second_factor(u)
         project(3, 0)
-        x_out(0, 1, 0, True)
+        x_out(0, 1, 0, on_scalar=True)
         first_factor(2)
         for j in range(2):
-            w_widen(1, 1, j)
-        x_out(0, 1, 1)
-        x_turn(1, 1, 0)
-        x_turn(1, 1, 1)
+            widen(pieces[4], j, on_scalar=True)
+        x_out(0, 1, 1, on_scalar=False)
         project(2, 1)
+        x_turn(1, 1)
         project(3, 1)
         x_quant(2, 0)
         x_quant(0, 1)
         w_quant(pieces[2])
-        w_weave(pieces[3])
+        w_weave(pieces[3], on_gpsimd=True)
         first_factor(3)
         for pair in range(2):
-            x_out(1, 1, pair, False)
+            x_out(1, 1, pair, on_scalar=False)
         project(4, 0)
 
-        late, early = {}, {}
+        first_step = 2
+        last_step = wide + LAG - 1
+        behind = {s: [] for s in range(first_step, last_step + 1)}
 
-        def at(time, fn, *args):
-            (late if time % 2 else early).setdefault(time // 2, []).append((fn, args))
+        def after(s, fn, *args):
+            behind[s].append((fn, args))
 
-        ends = {}
-        for u, (g, ranks) in enumerate(units):
-            ends[g] = u
-        for u in range(1, 24, 2):
-            at(2 * (u + 3) + 1, rank_sum, u - 1)
-            at(2 * (u + 3) + 1, rank_sum, u)
-        for g in groups[:6]:
-            at(2 * (ends[g] + 3 + 1) + 1, z_out, g)
-        due = [7,11,17,23,29,35,41,47,53]
-        on_vector = [pieces[i] + (3,) for i in []]
-        planes_left = [(c, m, j) for c in range(1, TILES) for m in range(M) for j in range(PACK)][6:]
-        planes_left = [pl for pl in planes_left if pl not in on_vector]
-        for i, (c, m, j) in enumerate(planes_left):
-            at(2 * (2 + (4 * i // 9 if i < 9 else 4 + 17 * (i - 9) // 21)) + 1, w_widen, c, m, j)
-        deferred = [(4, 1), (24, 1), (24, 2)]
-        at(5, x_turn, 2, 1, 0)
-        at(5, x_turn, 2, 1, 1)
-        at(7, x_quant, 1, 1)
-        at(11, x_quant, 2, 1)
-        for i, pc in enumerate(pieces[3:]):
-            if i + 4 < len(pieces) and pieces[i + 4] + (3,) in on_vector:
-                at(due[i], w_widen, *pieces[i + 4], 3, False)
-            at(due[i], w_quant, pc)
-            if i + 4 < len(pieces):
-                at(due[i], w_weave, pieces[i + 4])
-        at(7, project, 4, 1)
-        at(47, project, 24, 1)
-        at(6, x_out, 2, 1, 0, True)
-        at(7, x_out, 2, 1, 1)
-        at(47, wo_weave, 0)
-        at(51, wo_weave, 1)
-        at(53, weave, ("wo", 1), wo_raw[:, :, BANK:H], BANK)
-        for s in range(2, 27):
-            if s + 2 <= last and s + 2 not in a_of:
-                first_factor(s + 2)
-            if 0 <= s - 3 <= last and s - 3 not in p_of:
-                third_factor(s - 3)
-            for fn, args in early.get(s, []):
+        for u in range(0, wide, 2):
+            after(u + 1 + LAG, rank_sums, u)
+        for i, g in enumerate(halves[:-1]):
+            after(R * (i + 1) + LAG, z_out, g)
+        planes_left = [(piece, j) for piece in pieces[4:] for j in range(PACK)][2:]
+        late_planes = len(planes_left) - EARLY_PLANES
+        late_steps = last_step - TURN - (first_step + 4)
+        for i, (piece, j) in enumerate(planes_left):
+            if i < EARLY_PLANES:
+                after(first_step + 4 * i // EARLY_PLANES, widen, piece, j, True)
+            else:
+                after(first_step + 4 + late_steps * (i - EARLY_PLANES) // late_planes, widen, piece, j, True)
+        turns = [first_step + 1] + list(range(last_step, first_step + 2, -TURN))[::-1]
+        after(first_step, x_turn, 2, 1)
+        after(turns[0], x_quant, 1, 1)
+        after(turns[1], x_quant, 2, 1)
+        for s, piece in zip(turns, pieces[3:]):
+            after(s, w_quant, piece)
+            if piece != pieces[-1]:
+                after(s, w_weave, pieces[pieces.index(piece) + 1], True)
+        held_back = [(R, 1), (wide, 1), (wide, 2)]
+        for u, m in held_back[:2]:
+            after(u - 1, project, u, m)
+        after(turns[0], x_out, 2, 1, 1, False)
+        after(turns[-2], wo_left_weave, 0)
+        after(last_step - 1, wo_left_weave, 1)
+        after(last_step, wo_right_weave)
+
+        for s in range(first_step, last_step + 1):
+            first_factor(s + LEAD)
+            if s >= LAG:
+                third_factor(s - LAG)
+            if s == turns[0]:
+                x_out(2, 1, 0, on_scalar=True)
+            second_factor(s)
+            for u, m in ((s + 1 - LAG, 2), (s + 1 + LEAD, 0), (s + 1, 1)):
+                if (u, m) not in h_of and (u, m) not in held_back:
+                    project(u, m)
+            for fn, args in behind[s]:
                 fn(*args)
-            if s <= last and s not in ab_of:
-                second_factor(s)
-            if 0 <= s + 1 - 3 <= last and (s + 1 - 3, 2) not in h_of and (s + 1 - 3, 2) not in deferred:
-                project(s + 1 - 3, 2)
-            if s + 3 <= last and (s + 3, 0) not in h_of and (s + 3, 0) not in deferred:
-                project(s + 3, 0)
-            if s + 1 <= last and (s + 1, 1) not in h_of and (s + 1, 1) not in deferred:
-                project(s + 1, 1)
-            for fn, args in late.get(s, []):
-                fn(*args)
-        project(24, 2)
-        project(25, 2)
-        z_out(groups[5])
-        first_factor(29)
-        second_factor(27)
-        project(26, 2)
-        project(27, 2)
-        third_factor(24)
-        project(28, 1)
-        third_factor(25)
-        project(30, 0)
-        rank_sum(24)
-        rank_sum(25)
-        third_factor(26)
-        project(29, 1)
-        z_out(groups[6])
-        first_factor(30)
-        third_factor(27)
-        project(31, 0)
-        project(28, 2)
+
+        u = list(range(wide, len(units)))
+        project(u[0], 2)
+        project(u[1], 2)
+        z_out(halves[-1])
+        first_factor(u[5])
+        second_factor(u[3])
+        project(u[2], 2)
+        project(u[3], 2)
+        third_factor(u[0])
+        project(u[4], 1)
+        third_factor(u[1])
+        project(u[6], 0)
+        rank_sums(u[0])
+        third_factor(u[2])
+        project(u[5], 1)
+        z_out(quarters[0])
+        first_factor(u[6])
+        third_factor(u[3])
+        project(u[7], 0)
+        project(u[4], 2)
         z_turn(0)
-        rank_sum(26)
-        rank_sum(27)
-        second_factor(28)
-        wo_quant(0)
-        wo_quant(1)
+        rank_sums(u[2])
+        second_factor(u[4])
+        for side in range(2):
+            wo_quant(side)
         z_turn_out(0)
-        z_out(groups[7])
-        first_factor(31)
-        project(29, 2)
-        second_factor(29)
-        project(30, 1)
+        z_out(quarters[1])
+        first_factor(u[7])
+        project(u[5], 2)
+        second_factor(u[5])
+        project(u[6], 1)
         z_quant(0)
-        third_factor(28)
-        out_product(0, 0, True)
+        third_factor(u[4])
+        out_product(0, 0, z_bank)
         z_turn(1)
-        project(31, 1)
+        project(u[7], 1)
         out_product(0, 1)
         y_out(0, 0)
-        add_bo(0, 0)
+        add_bo(0, 0, "first_add")
         z_turn_out(1)
-        third_factor(29)
-        project(30, 2)
-        out_product(0, 2, True)
-        second_factor(30)
-        rank_sum(28)
-        rank_sum(29)
-        project(31, 2)
+        third_factor(u[5])
+        project(u[6], 2)
+        out_product(0, 2, z_bank)
+        second_factor(u[6])
+        rank_sums(u[4])
+        project(u[7], 2)
         y_out(0, 2)
-        z_out(groups[8])
-        second_factor(31)
+        z_out(quarters[2])
+        second_factor(u[7])
         finish(0, 1)
         z_quant(1)
         add_bo(0, 2, "z_grouped1")
         store(0, 0)
-        out_product(0, 3, True)
-        third_factor(30)
+        out_product(0, 3, z_bank)
+        third_factor(u[6])
         z_turn(2)
         out_product(1, 0)
         out_product(1, 1)
-        third_factor(31)
+        third_factor(u[7])
         z_turn_out(2)
         y_out(1, 1)
-        rank_sum(30)
-        rank_sum(31)
+        rank_sums(u[6])
         finish(0, 3)
-        out_product(1, 2, True)
+        out_product(1, 2, z_bank)
         out_product(1, 3)
         finish(1, 0)
-        z_out(groups[9])
+        z_out(quarters[3])
         store(0, 2)
         z_quant(2)
         add_bo(1, 1, "z_grouped2")
@@ -551,7 +510,7 @@ def tile_lowranktrimodalfusion_kernel(tc, x, w_bytes, w_scale, b, omega, wo, bo,
         z_turn_out(3)
         finish(1, 3)
         out_product(2, 2)
-        out_product(2, 3, True)
+        out_product(2, 3, z_bank)
         finish(2, 0)
         store(1, 1)
         finish(2, 2)

@@ -51,8 +51,6 @@ def tile_lowranktrimodalfusion_kernel(tc, x, w_bytes, w_scale, b, omega, wo, bo,
         vec = keep.tile([P, P], BF16, name="vec")
         vec32 = keep.tile([P, P], F32, name="vec32")
         ident = keep.tile([P, P], F32, name="ident")
-        zeros = keep.tile([P, BANK], BF16, name="zeros")
-        nc.vector.memset(zeros[:], 0.0)
         nc.scalar.dma_start(out=ws[:], in_=w_scale.rearrange("a (p j) o -> p (a j o)", j=PACK))
         nc.scalar.dma_start(out=vec[48:64, :], in_=omega.rearrange("r (c f) -> (r c) f", f=P))
         nc.scalar.dma_start(out=vec[0:48, :], in_=b.rearrange("m (q f) -> (m q) f", f=P))
@@ -319,19 +317,11 @@ def tile_lowranktrimodalfusion_kernel(tc, x, w_bytes, w_scale, b, omega, wo, bo,
             o_of[q, i] = o
             nc.gpsimd.tensor_tensor(out=o[:], in0=y_sb[q, i][:], in1=bo_sb[:, side_cols(i)], op=ALU.add)
 
-        unread = z_bank([P, BANK])
-
-        def warm_up(count):
-            for i in range(count):
-                nc.tensor.matmul(unread[:], lhsT=zeros[:, 0:P], rhs=zeros[:], start=True, stop=True)
-
-        warm_up(5)
         for j in range(PACK):
             widen(pieces[0], j, on_scalar=j == 3)
         w_weave(pieces[0], on_gpsimd=False)
         nc.vector.tensor_copy(out=vec32[0:64, :], in_=vec[0:64, :])
         x_turn(0, 0)
-        warm_up(2)
         vec_turned = bank([P, P])
         nc.tensor.transpose(vec_turned[:], vec32[:], ident[:])
         for pair in range(2):

@@ -22,9 +22,10 @@ TILES = F // P
 BANK = 512
 RING = 7
 LEAD = 2
-LAG = 3
 TURN = 3
-EARLY_PLANES = 9
+LAG = TURN
+EARLY_TURNS = 4
+EARLY_PLANES = 7
 RUN = 4
 
 
@@ -166,12 +167,10 @@ def tile_lowranktrimodalfusion_kernel(tc, x, w_bytes, w_scale, b, omega, wo, bo,
         def weave(key, src, on_gpsimd):
             dst = stage.tile([P, BANK, PACK], BF16, name="woven", align_bytes=64, bufs=1)
             woven[key] = dst
+            to, of = in_runs(dst[:], src)
             if on_gpsimd:
-                nc.gpsimd.tensor_scalar(
-                    out=dst[:], in0=src.rearrange("p j n -> p n j"), scalar1=1.0, scalar2=0.0, op0=ALU.mult, op1=ALU.add
-                )
+                nc.gpsimd.tensor_scalar(out=to, in0=of, scalar1=1.0, scalar2=0.0, op0=ALU.mult, op1=ALU.add)
             else:
-                to, of = in_runs(dst[:], src)
                 nc.vector.tensor_copy(out=to, in_=of)
 
         def w_weave(piece, on_gpsimd):
@@ -346,7 +345,7 @@ def tile_lowranktrimodalfusion_kernel(tc, x, w_bytes, w_scale, b, omega, wo, bo,
         x_turn(2, 0)
         for u in range(2):
             first_factor(u)
-        for j in range(PACK):
+        for j in range(PACK - 1):
             widen(pieces[3], j, on_scalar=True)
         for pair in range(2):
             x_out(2, 0, pair, on_scalar=False)
@@ -357,11 +356,12 @@ def tile_lowranktrimodalfusion_kernel(tc, x, w_bytes, w_scale, b, omega, wo, bo,
         for u in range(2):
             second_factor(u)
         project(3, 0)
-        x_out(0, 1, 0, on_scalar=True)
+        for pair in range(2):
+            x_out(0, 1, pair, on_scalar=True)
+        widen(pieces[3], PACK - 1, on_scalar=True)
         first_factor(2)
         for j in range(2):
             widen(pieces[4], j, on_scalar=True)
-        x_out(0, 1, 1, on_scalar=False)
         project(2, 1)
         x_turn(1, 1)
         project(3, 1)
@@ -397,17 +397,15 @@ def tile_lowranktrimodalfusion_kernel(tc, x, w_bytes, w_scale, b, omega, wo, bo,
         after(first_step, x_turn, 2, 1)
         after(turns[0], x_quant, 1, 1)
         after(turns[1], x_quant, 2, 1)
-        for s, piece in zip(turns, pieces[3:]):
-            after(s, w_quant, piece)
-            if piece != pieces[-1]:
-                after(s, w_weave, pieces[pieces.index(piece) + 1], True)
-        held_back = [(R, 1), (wide, 1), (wide, 2)]
-        for u, m in held_back[:2]:
-            after(u - 1, project, u, m)
+        for i, s in enumerate(turns[:-EARLY_TURNS]):
+            after(s, w_quant, pieces[3 + i])
+            after(s, w_weave, pieces[4 + i], True)
+        in_middle = {s: len(pieces) - EARLY_TURNS + i for i, s in enumerate(turns[-EARLY_TURNS:])}
+        held_back = [(R, 1), (wide, 2)]
+        after(R - 1, project, R, 1)
         after(turns[0], x_out, 2, 1, 1, False)
         after(turns[-2], wo_left_weave, 0)
         after(last_step - 1, wo_left_weave, 1)
-        after(last_step, wo_right_weave)
 
         for s in range(first_step, last_step + 1):
             first_factor(s + LEAD)
@@ -415,6 +413,12 @@ def tile_lowranktrimodalfusion_kernel(tc, x, w_bytes, w_scale, b, omega, wo, bo,
                 third_factor(s - LAG)
             if s == turns[0]:
                 x_out(2, 1, 0, on_scalar=True)
+            if s in in_middle:
+                w_quant(pieces[in_middle[s]])
+                if s < last_step:
+                    w_weave(pieces[in_middle[s] + 1], on_gpsimd=True)
+                else:
+                    wo_right_weave()
             second_factor(s)
             for u, m in ((s + 1 - LAG, 2), (s + 1 + LEAD, 0), (s + 1, 1)):
                 if (u, m) not in h_of and (u, m) not in held_back:

@@ -385,7 +385,8 @@ def tile_lowranktrimodalfusion_kernel(tc, x, w_bytes, w_scale, b, omega, wo, bo,
             after(u + 1 + LAG, rank_sums, u)
         for i, g in enumerate(halves[:-1]):
             after(R * (i + 1) + LAG, z_out, g)
-        planes_left = [(piece, j) for piece in pieces[4:] for j in range(PACK)][2:]
+        shared = (pieces[7], PACK - 1)
+        planes_left = [(piece, j) for piece in pieces[4:] for j in range(PACK) if (piece, j) != shared][2:]
         late_planes = len(planes_left) - EARLY_PLANES
         late_steps = last_step - TURN - (first_step + 4)
         for i, (piece, j) in enumerate(planes_left):
@@ -398,6 +399,8 @@ def tile_lowranktrimodalfusion_kernel(tc, x, w_bytes, w_scale, b, omega, wo, bo,
         after(turns[0], x_quant, 1, 1)
         after(turns[1], x_quant, 2, 1)
         for i, s in enumerate(turns[:-EARLY_TURNS]):
+            if pieces[4 + i] == shared[0]:
+                after(s, widen, *shared, False)
             after(s, w_quant, pieces[3 + i])
             after(s, w_weave, pieces[4 + i], True)
         in_middle = {s: len(pieces) - EARLY_TURNS + i for i, s in enumerate(turns[-EARLY_TURNS:])}

@@ -20,12 +20,9 @@ PACK = 4
 HALF = 512
 TILES = F // P
 BANK = 512
-RING = 7
+BANKS = 8
 LEAD = 2
-TURN = 3
-LAG = TURN
-EARLY_TURNS = 4
-EARLY_PLANES = 7
+LAG = 3
 RUN = 4
 
 
@@ -33,20 +30,20 @@ def tile_lowranktrimodalfusion_kernel(tc, x, w_bytes, w_scale, b, omega, wo, bo,
     nc = tc.nc
     with ExitStack() as ctx:
         keep = ctx.enter_context(tc.tile_pool(name="keep", bufs=1))
-        stage = ctx.enter_context(tc.tile_pool(name="stage", bufs=3))
+        stage = ctx.enter_context(tc.tile_pool(name="stage", bufs=1))
         psum = ctx.enter_context(tc.psum_pool(name="psum", bufs=1))
         ctx.enter_context(tc.manual_schedule())
 
-        taken = []
+        free_banks = list(range(BANKS))
+        bank_of = {}
 
-        def bank(shape):
-            t = psum.tile(shape, F32, name="ring%d" % (len(taken) % RING))
-            taken.append(t)
+        def bank(key, shape):
+            bank_of[key] = free_banks.pop(0)
+            t = psum.tile(shape, F32, name="bank%d" % bank_of[key])
             return t
 
-        def z_bank(shape):
-            t = psum.tile(shape, F32, name="z")
-            return t
+        def release(key):
+            free_banks.append(bank_of[key])
 
         ws = keep.tile([P, PACK], F32, name="ws")
         vec = keep.tile([P, P], BF16, name="vec")
@@ -56,10 +53,10 @@ def tile_lowranktrimodalfusion_kernel(tc, x, w_bytes, w_scale, b, omega, wo, bo,
         nc.scalar.dma_start(out=vec[48:64, :], in_=omega.rearrange("r (c f) -> (r c) f", f=P))
         nc.scalar.dma_start(out=vec[0:48, :], in_=b.rearrange("m (q f) -> (m q) f", f=P))
         make_identity(nc, ident[:])
-        nc.gpsimd.memset(vec32[64:128, :], 0.0)
+        nc.scalar.activation(out=vec32[64:128, :], in_=ident[64:128, :], func=ACT.Copy, scale=0.0)
 
         pieces = [(c, m) for c in range(TILES) for m in range(M)]
-        first_raw, w_raw, x_raw = {}, {}, {}
+        first_raw, w_raw, x_raw, planes = {}, {}, {}, {}
         for part in range(2):
             t = keep.tile([P, 2, R * P], U8, name="first_raw%d" % part)
             first_raw[part] = t
@@ -70,9 +67,10 @@ def tile_lowranktrimodalfusion_kernel(tc, x, w_bytes, w_scale, b, omega, wo, bo,
         wo_raw = keep.tile([P, PACK, H], BF16, name="wo_raw")
         bo_sb = keep.tile([P, H], BF16, name="bo_sb")
 
-        def load_w(c, m):
+        def load_w(i):
+            c, m = pieces[i]
             src = w_bytes[m].rearrange("(p j) (r f) -> p (j r) f", j=PACK, r=R)[:, :, c * P : (c + 1) * P]
-            if (c, m) == pieces[0]:
+            if i == 0:
                 for part in range(2):
                     rows = slice(2 * R * part, 2 * R * (part + 1))
                     nc.sync.dma_start(out=first_raw[part][:].rearrange("p j (r f) -> p (j r) f", r=R), in_=src[:, rows, :])
@@ -85,12 +83,19 @@ def tile_lowranktrimodalfusion_kernel(tc, x, w_bytes, w_scale, b, omega, wo, bo,
             src = x[m].rearrange("(p a) k -> p a k", a=8)
             nc.sync.dma_start(out=x_raw[m, half][:], in_=src[:, 4 * half : 4 * half + 4, :])
 
+        def planes_of(piece):
+            if piece not in planes:
+                t = stage.tile([P, PACK, R * P], BF16, name="planes", align_bytes=64, bufs=5)
+                planes[piece] = t
+            return planes[piece]
+
         for i in range(2 * M):
-            load_w(*pieces[i])
+            load_w(i)
             load_x(i % M, i // M)
-        for c, m in pieces[2 * M :]:
-            load_w(c, m)
-        nc.sync.dma_start(out=wo_raw[:], in_=wo.rearrange("(p j) n -> p j n", j=PACK))
+        for i in range(2 * M, len(pieces)):
+            load_w(i)
+            if i == 7:
+                nc.sync.dma_start(out=wo_raw[:], in_=wo.rearrange("(p j) n -> p j n", j=PACK))
         nc.sync.dma_start(out=bo_sb[:], in_=bo.partition_broadcast(P))
 
         def mx_operand(name, width):
@@ -98,10 +103,15 @@ def tile_lowranktrimodalfusion_kernel(tc, x, w_bytes, w_scale, b, omega, wo, bo,
             scales = keep.tile([P, width], U8, name=name + "_scales", align_bytes=64)
             return codes, scales
 
-        def quantize(operand, src):
+        def quantize(operand, src, first=0):
+            cols = slice(first, first + src.shape[1])
             nc.vector.quantize_mx(
-                out=operand[0][:].bitcast(FP8X4), scales=operand[1][:], in_=src[:].rearrange("p n j -> p (n j)")
+                out=operand[0][:, cols].bitcast(FP8X4), scales=operand[1][:, cols], in_=src.rearrange("p n j -> p (n j)")
             )
+
+        def grouped(slot):
+            t = stage.tile([P, BANK, PACK], BF16, name="grouped%d" % slot, align_bytes=64, bufs=1)
+            return t
 
         def product(dst, lhs, lhs_from, rhs, rhs_from, width):
             lcols, rcols = slice(lhs_from, lhs_from + P), slice(rhs_from, rhs_from + width)
@@ -117,11 +127,12 @@ def tile_lowranktrimodalfusion_kernel(tc, x, w_bytes, w_scale, b, omega, wo, bo,
 
         xq = {(m, half): mx_operand("x%d%d" % (m, half), HALF) for m in range(M) for half in range(2)}
         x_turned, x_grouped = {}, {}
+        x_slot = ((0, 1, 2), (0, 2, 3))
 
         def x_turn(m, half):
             words = x_raw[m, half][:].rearrange("p a k -> p (a k)").bitcast(F32)
             for pair in range(2):
-                t = bank([P, 2, 2, P])
+                t = bank(("x", m, half, pair), [P, 2, 2, P])
                 for i in range(2):
                     base = (2 * pair + i) * (D // 2)
                     for u in range(2):
@@ -129,9 +140,8 @@ def tile_lowranktrimodalfusion_kernel(tc, x, w_bytes, w_scale, b, omega, wo, bo,
                 x_turned[m, half, pair] = t
 
         def x_out(m, half, pair, on_scalar):
-            if pair == 0:
-                g = stage.tile([P, HALF, PACK], BF16, name="x_grouped", align_bytes=64, bufs=3)
-                x_grouped[m, half] = g
+            if (m, half) not in x_grouped:
+                x_grouped[m, half] = grouped(x_slot[half][m])
             dst = x_grouped[m, half][:].rearrange("p n j -> p (n j)").bitcast(F32)
             dst = dst[:, pair * BANK : (pair + 1) * BANK].rearrange("p (a r u) -> p a r u", a=2, u=2)
             src = x_turned[m, half, pair][:].rearrange("p a u r -> p a r u")
@@ -139,23 +149,19 @@ def tile_lowranktrimodalfusion_kernel(tc, x, w_bytes, w_scale, b, omega, wo, bo,
                 nc.scalar.copy(out=dst, in_=src)
             else:
                 nc.vector.tensor_copy(out=dst, in_=src)
+            release(("x", m, half, pair))
 
         def x_quant(m, half):
-            quantize(xq[m, half], x_grouped[m, half])
+            quantize(xq[m, half], x_grouped[m, half][:])
 
         wq = {piece: mx_operand("w%d%d" % piece, R * P) for piece in pieces}
-        woq = [mx_operand("wo%d" % side, BANK) for side in range(2)]
-        planes, woven = {}, {}
-
-        def planes_tile(shape):
-            t = stage.tile(shape, BF16, name="planes", align_bytes=64, bufs=5)
-            return t
+        woq = mx_operand("wo", H)
+        woven = {}
+        w_slot = (3, 3, 1, 0) + tuple((1, 3, 0)[i % 3] for i in range(8))
 
         def widen(piece, j, on_scalar):
-            if j == 0:
-                planes[piece] = planes_tile([P, PACK, R * P])
             raw = first_raw[j // 2][:, j % 2, :] if piece == pieces[0] else w_raw[piece][:, j, :]
-            dst, src = planes[piece][:, j, :], raw.bitcast(FP8)
+            dst, src = planes_of(piece)[:, j, :], raw.bitcast(FP8)
             if on_scalar:
                 nc.scalar.activation(out=dst, in_=src, func=ACT.Copy, scale=ws[:, j : j + 1])
             else:
@@ -164,36 +170,60 @@ def tile_lowranktrimodalfusion_kernel(tc, x, w_bytes, w_scale, b, omega, wo, bo,
         def in_runs(dst, src):
             return dst.rearrange("p (c i) j -> p c j i", i=RUN), src.rearrange("p j (c i) -> p c j i", i=RUN)
 
-        def weave(key, src, on_gpsimd):
-            dst = stage.tile([P, BANK, PACK], BF16, name="woven", align_bytes=64, bufs=1)
-            woven[key] = dst
-            to, of = in_runs(dst[:], src)
+        def weave(dst, src, on_gpsimd):
+            to, of = in_runs(dst, src)
             if on_gpsimd:
                 nc.gpsimd.tensor_scalar(out=to, in0=of, scalar1=1.0, scalar2=0.0, op0=ALU.mult, op1=ALU.add)
             else:
                 nc.vector.tensor_copy(out=to, in_=of)
 
-        def w_weave(piece, on_gpsimd):
-            weave(piece, planes[piece][:], on_gpsimd)
+        def w_weave(i, on_gpsimd):
+            t = grouped(w_slot[i])
+            woven[i] = t
+            weave(t[:], planes[pieces[i]][:], on_gpsimd)
 
-        def w_quant(piece):
-            quantize(wq[piece], woven[piece])
+        def w_quant(i, first=0, width=R * P):
+            quantize(wq[pieces[i]], woven[i][:, first : first + width, :], first)
+
+        def wo_right_weave(s):
+            if s == 0:
+                woven["wo", 1] = grouped(2)
+            weave(woven["wo", 1][:, s * P : (s + 1) * P, :], wo_raw[:, :, BANK + s * P : BANK + (s + 1) * P], True)
 
         def wo_left_weave(part):
             if part == 0:
-                woven["wo", 0] = planes_tile([P, BANK, PACK])
+                woven["wo", 0] = grouped(0)
             cs = slice(part * BANK // 2, (part + 1) * BANK // 2)
             to, of = in_runs(woven["wo", 0][:, cs, :], wo_raw[:, :, cs])
             nc.scalar.copy(out=to, in_=of)
 
-        def wo_right_weave():
-            weave(("wo", 1), wo_raw[:, :, BANK:H], True)
-
         def wo_quant(side):
-            quantize(woq[side], woven["wo", side])
+            quantize(woq, woven["wo", side][:], side * BANK)
 
         cols = keep.tile([P, 64], F32, name="cols")
         omega_b0 = keep.tile([P, 16], F32, name="omega_b0")
+
+        vec_turned = {}
+
+        def vec_widen():
+            nc.scalar.copy(out=vec32[0:64, :], in_=vec[0:64, :])
+
+        def vec_turn():
+            vec_turned[0] = bank("vec", [P, P])
+            nc.tensor.transpose(vec_turned[0][:], vec32[:], ident[:])
+
+        def vec_cols():
+            nc.scalar.copy(out=cols[:], in_=vec_turned[0][:, 0:64])
+
+        def vec_bias():
+            nc.vector.tensor_tensor(out=omega_b0[:], in0=vec_turned[0][:, 48:64], in1=cols[:, 0:16], op=ALU.mult)
+            release("vec")
+
+        def warm_up(n):
+            t = bank("warm", [P, BANK])
+            for i in range(n):
+                nc.tensor.matmul(t[:], lhsT=x_raw[0, 0][:, 0, 0:P], rhs=x_raw[0, 0][:, 1, :], start=True, stop=True)
+            release("warm")
 
         def column(tile, row, r, c):
             q = 16 * row + 4 * r + c
@@ -202,11 +232,19 @@ def tile_lowranktrimodalfusion_kernel(tc, x, w_bytes, w_scale, b, omega, wo, bo,
         halves = [(c, half, 0, 4) for c in range(TILES - 1) for half in range(2)]
         quarters = [(TILES - 1, q // 2, 2 * (q % 2), 2) for q in range(4)]
         units = [(g, [r]) for g in halves for r in range(R)] + [(g, [r, r + 1]) for g in quarters for r in (0, 2)]
-        wide = R * len(halves)
-        h_of, a_of, ab_of, p_of, z_sum, z_rows = {}, {}, {}, {}, {}, {}
+        last_tiles = [(TILES - 1, 1, 2 + a, 1) for a in range(2)]
+        h_of, a_of, b_of, ab_of, p_of, z_sum, z_rows = {}, {}, {}, {}, {}, {}, {}
         for half in range(2):
             t = keep.tile([P, 4, F], BF16, name="z_rows%d" % half)
             z_rows[half] = t
+
+        first_step, last_step = 7, 23
+        turn_at, reads = {}, 2 * first_step - 1
+        with_slice = [5, 6, 9, 10]
+        for i in range(5, 11):
+            reads = reads + (6 if i in with_slice else 5)
+            turn_at[reads] = i
+        holds_back = {reads // 2: i + 1 for reads, i in turn_at.items() if reads % 2 == 1}
 
         def parts(u):
             g, ranks = units[u]
@@ -215,19 +253,23 @@ def tile_lowranktrimodalfusion_kernel(tc, x, w_bytes, w_scale, b, omega, wo, bo,
 
         def project(u, m):
             c, half, a0, na = units[u][0]
-            h = bank([P, BANK])
+            h = bank((u, m), [P, BANK])
             h_of[u, m] = h
             for r, cs in parts(u):
                 product(h[:, cs], wq[c, m], r * P, xq[m, half], a0 * P, na * P)
 
         def first_factor(u):
             c = units[u][0][0]
-            a = stage.tile([P, BANK], F32, name="a", bufs=LEAD + 3)
+            if u in holds_back:
+                a = stage.tile([P, BANK], F32, name="grouped%d" % w_slot[holds_back[u]], align_bytes=64, bufs=1)
+            else:
+                a = stage.tile([P, BANK], F32, name="a", bufs=LEAD + 4)
             a_of[u] = a
             for r, cs in parts(u):
                 nc.scalar.activation(
                     out=a[:, cs], in_=h_of[u, 0][:, cs], func=ACT.Identity, scale=column(cols, M, r, c), bias=column(omega_b0, 0, r, c)
                 )
+            release((u, 0))
 
         def times_factor(dst, u, m, so_far):
             c = units[u][0][0]
@@ -235,30 +277,46 @@ def tile_lowranktrimodalfusion_kernel(tc, x, w_bytes, w_scale, b, omega, wo, bo,
                 nc.vector.scalar_tensor_tensor(
                     out=dst[:, cs], in0=h_of[u, m][:, cs], scalar=column(cols, m, r, c), in1=so_far[:, cs], op0=ALU.add, op1=ALU.mult
                 )
+            release((u, m))
 
         def second_factor(u):
             ab = stage.tile([P, BANK], F32, name="ab", bufs=LAG + 2)
             ab_of[u] = ab
             times_factor(ab, u, 1, a_of[u])
 
+        def second_out(u):
+            c = units[u][0][0]
+            t = stage.tile([P, BANK], F32, name="for_gpsimd", bufs=4)
+            b_of[u] = t
+            for r, cs in parts(u):
+                nc.scalar.activation(out=t[:, cs], in_=h_of[u, 1][:, cs], func=ACT.Identity, bias=column(cols, 1, r, c))
+            release((u, 1))
+
+        def second_times(u, buffer):
+            ab = stage.tile([P, BANK], F32, name=buffer, align_bytes=64, bufs=1)
+            ab_of[u] = ab
+            nc.gpsimd.tensor_tensor(out=ab[:], in0=a_of[u][:], in1=b_of[u][:], op=ALU.mult)
+
         def third_factor(u):
-            p = stage.tile([P, BANK], F32, name="p", bufs=7)
+            p = stage.tile([P, BANK], F32, name="p", bufs=10)
             p_of[u] = p
             times_factor(p, u, 2, ab_of[u])
 
-        def rank_sums(first):
-            for u in (first, first + 1):
+        def rank_sums(first, split=False, count=2):
+            for u in range(first, first + count):
                 g, ranks = units[u]
-                na = g[3]
-                if ranks[0] == 0:
-                    z_sum[g] = bank([P, na, P]) if u > wide else z_bank([P, na, P])
-                for i, r in enumerate(ranks):
-                    for a in range(na):
-                        cs = slice((i * na + a) * P, (i * na + a + 1) * P)
-                        nc.tensor.matmul(
-                            z_sum[g][:, a, :], lhsT=p_of[u][:, cs], rhs=ident[:], is_transpose=True,
-                            start=r == 0 and a == 0, stop=r == R - 1 and a == na - 1,
-                        )
+                c, half, a0, na = g
+                sums = [(c, half, a0 + a, 1) for a in range(na)] if split else [g]
+                for s in sums:
+                    if ranks[0] == 0:
+                        z_sum[s] = bank(s, [P, s[3], P])
+                    for i, r in enumerate(ranks):
+                        for a in range(s[3]):
+                            col = (i * na + s[2] - a0 + a) * P
+                            nc.tensor.matmul(
+                                z_sum[s][:, a, :], lhsT=p_of[u][:, col : col + P], rhs=ident[:], is_transpose=True,
+                                start=r == 0 and a == 0, stop=r == R - 1 and a == s[3] - 1,
+                            )
 
         def z_out(g):
             c, half, a0, na = g
@@ -267,6 +325,7 @@ def tile_lowranktrimodalfusion_kernel(tc, x, w_bytes, w_scale, b, omega, wo, bo,
                 out=dst.rearrange("p a u (q e) -> p a u q e", e=2),
                 in_=z_sum[g][:].rearrange("p a (q u e) -> p a u q e", u=2, e=2),
             )
+            release(g)
 
         zq = [mx_operand("z%d" % q, 2 * P) for q in range(4)]
         z_turned, z_grouped, y_of, y_sb, o_of = {}, {}, {}, {}, {}
@@ -275,26 +334,27 @@ def tile_lowranktrimodalfusion_kernel(tc, x, w_bytes, w_scale, b, omega, wo, bo,
         def side_cols(i):
             return slice(i // 2 * BANK, (i // 2 + 1) * BANK)
 
-        def z_turn(q):
-            t = bank([P, 2, 2, P])
+        def z_turn(q, a=0, n=2):
+            t = bank(("z", q, a), [P, n, 2, P])
             words = z_rows[q // 2][:].rearrange("p a k -> p (a k)").bitcast(F32)
-            for i in range(4):
-                base = (4 * (q % 2) + i) * P
+            for i in range(2 * n):
+                base = (4 * (q % 2) + 2 * a + i) * P
                 nc.tensor.transpose(t[:, i // 2, i % 2, :], words[:, base : base + P], ident[:])
-            z_turned[q] = t
+            z_turned[q, a] = t
 
-        def z_turn_out(q):
-            g = stage.tile([P, 2 * P, PACK], BF16, name="z_grouped%d" % q, align_bytes=64, bufs=1)
-            z_grouped[q] = g
+        def z_turn_out(q, a=0, n=2):
+            g = stage.tile([P, n * P, PACK], BF16, name="z_grouped%d" % (q + a), align_bytes=64, bufs=1)
+            z_grouped[q, a] = g
             dst = g[:].rearrange("p n j -> p (n j)").bitcast(F32).rearrange("p (a r u) -> p a r u", r=P, u=2)
-            nc.scalar.copy(out=dst, in_=z_turned[q][:].rearrange("p a u r -> p a r u"))
+            nc.scalar.copy(out=dst, in_=z_turned[q, a][:].rearrange("p a u r -> p a r u"))
+            release(("z", q, a))
 
-        def z_quant(q):
-            quantize(zq[q], z_grouped[q])
+        def z_quant(q, a=0):
+            quantize(zq[q], z_grouped[q, a][:], a * P)
 
-        def out_product(q, i, take=bank):
-            y = take([P, BANK])
-            product(y[:], zq[q], i % 2 * P, woq[i // 2], 0, BANK)
+        def out_product(q, i):
+            y = bank(("y", q, i), [P, BANK])
+            product(y[:], zq[q], i % 2 * P, woq, i // 2 * BANK, BANK)
             y_of[q, i] = y
 
         def store(q, i):
@@ -304,220 +364,294 @@ def tile_lowranktrimodalfusion_kernel(tc, x, w_bytes, w_scale, b, omega, wo, bo,
             o = stage.tile([P, BANK], F32, name="o", bufs=8)
             o_of[q, i] = o
             nc.vector.tensor_tensor(out=o[:], in0=y_of[q, i][:], in1=bo_sb[:, side_cols(i)], op=ALU.add)
+            release(("y", q, i))
             store(q, i)
 
         def y_out(q, i):
-            y = stage.tile([P, BANK], F32, name="y", bufs=4)
+            y = stage.tile([P, BANK], F32, name="for_gpsimd", bufs=4)
             y_sb[q, i] = y
             nc.scalar.copy(out=y[:], in_=y_of[q, i][:])
+            release(("y", q, i))
 
         def add_bo(q, i, buffer):
             o = stage.tile([P, BANK], F32, name=buffer, align_bytes=64, bufs=1)
             o_of[q, i] = o
             nc.gpsimd.tensor_tensor(out=o[:], in0=y_sb[q, i][:], in1=bo_sb[:, side_cols(i)], op=ALU.add)
 
-        for j in range(PACK):
-            widen(pieces[0], j, on_scalar=j == 3)
-        w_weave(pieces[0], on_gpsimd=False)
-        nc.vector.tensor_copy(out=vec32[0:64, :], in_=vec[0:64, :])
         x_turn(0, 0)
-        vec_turned = bank([P, P])
-        nc.tensor.transpose(vec_turned[:], vec32[:], ident[:])
-        for pair in range(2):
-            x_out(0, 0, pair, on_scalar=True)
-        w_quant(pieces[0])
-        for j in range(PACK):
-            widen(pieces[1], j, on_scalar=j >= 2)
-        nc.vector.tensor_copy(out=cols[:], in_=vec_turned[:, 0:64])
+        widen(pieces[0], 0, on_scalar=False)
+        widen(pieces[0], 1, on_scalar=False)
+        widen(pieces[0], 3, on_scalar=True)
+        widen(pieces[0], 2, on_scalar=False)
+        vec_widen()
+        vec_turn()
+        warm_up(3)
         x_turn(1, 0)
+        w_weave(0, on_gpsimd=False)
+        x_out(0, 0, 0, on_scalar=True)
+        x_out(0, 0, 1, on_scalar=True)
+        w_quant(0)
+        widen(pieces[1], 3, on_scalar=True)
+        widen(pieces[1], 0, on_scalar=False)
+        widen(pieces[1], 1, on_scalar=False)
+        vec_cols()
+        widen(pieces[1], 2, on_scalar=False)
         x_quant(0, 0)
-        nc.vector.tensor_tensor(out=omega_b0[:], in0=vec_turned[:, 48:64], in1=cols[:, 0:16], op=ALU.mult)
-        for pair in range(2):
-            x_out(1, 0, pair, on_scalar=True)
-        w_weave(pieces[1], on_gpsimd=False)
-        for j in range(PACK):
-            widen(pieces[2], j, on_scalar=j >= 2)
-        x_quant(1, 0)
-        w_quant(pieces[1])
-        w_weave(pieces[2], on_gpsimd=True)
-        for u in range(2):
-            project(u, 0)
+        project(0, 0)
+        project(1, 0)
+        warm_up(2)
         x_turn(2, 0)
-        for u in range(2):
-            first_factor(u)
-        for j in range(PACK - 1):
-            widen(pieces[3], j, on_scalar=True)
-        for pair in range(2):
-            x_out(2, 0, pair, on_scalar=False)
-        for u in range(2):
-            project(u, 1)
-        x_turn(0, 1)
         project(2, 0)
-        for u in range(2):
-            second_factor(u)
-        project(3, 0)
-        for pair in range(2):
-            x_out(0, 1, pair, on_scalar=True)
-        widen(pieces[3], PACK - 1, on_scalar=True)
-        first_factor(2)
-        for j in range(2):
-            widen(pieces[4], j, on_scalar=True)
+        vec_bias()
+        w_weave(1, on_gpsimd=False)
+        x_out(1, 0, 0, on_scalar=True)
+        x_out(1, 0, 1, on_scalar=True)
+        widen(pieces[2], 0, on_scalar=False)
+        widen(pieces[2], 1, on_scalar=False)
+        widen(pieces[2], 2, on_scalar=True)
+        x_quant(1, 0)
+        widen(pieces[2], 3, on_scalar=True)
+        w_weave(2, on_gpsimd=True)
+        w_quant(1)
+        project(0, 1)
+        project(1, 1)
         project(2, 1)
-        x_turn(1, 1)
+        first_factor(0)
+        x_out(2, 0, 0, on_scalar=False)
+        x_turn(0, 1)
+        first_factor(1)
+        project(3, 0)
+        x_out(2, 0, 1, on_scalar=False)
         project(3, 1)
+        first_factor(2)
+        second_factor(0)
+        x_turn(1, 1)
+        widen(pieces[3], 0, on_scalar=True)
+        second_factor(1)
+        widen(pieces[3], 1, on_scalar=True)
+        second_factor(2)
+        x_out(0, 1, 0, on_scalar=True)
         x_quant(2, 0)
+        x_out(0, 1, 1, on_scalar=True)
+        widen(pieces[3], 3, on_scalar=False)
+        widen(pieces[3], 2, on_scalar=True)
         x_quant(0, 1)
-        w_quant(pieces[2])
-        w_weave(pieces[3], on_gpsimd=True)
-        first_factor(3)
-        for pair in range(2):
-            x_out(1, 1, pair, on_scalar=False)
         project(4, 0)
+        w_weave(3, on_gpsimd=True)
+        first_factor(3)
+        w_quant(2)
+        project(0, 2)
+        project(1, 2)
+        project(2, 2)
+        project(5, 0)
+        widen(pieces[4], 0, on_scalar=True)
+        second_factor(3)
+        x_out(1, 1, 0, on_scalar=True)
+        x_turn(2, 1)
+        x_out(1, 1, 1, on_scalar=False)
+        project(3, 2)
+        first_factor(4)
+        project(6, 0)
+        third_factor(0)
+        widen(pieces[4], 1, on_scalar=True)
+        third_factor(1)
+        widen(pieces[4], 2, on_scalar=True)
+        third_factor(2)
+        first_factor(5)
+        x_quant(1, 1)
+        project(4, 1)
+        project(5, 1)
+        rank_sums(0)
+        project(7, 0)
+        x_out(2, 1, 0, on_scalar=True)
+        project(6, 1)
+        widen(pieces[4], 3, on_scalar=False)
+        w_weave(4, on_gpsimd=True)
+        widen(pieces[5], 0, on_scalar=True)
+        w_quant(3)
+        first_factor(6)
+        project(8, 0)
+        third_factor(3)
+        rank_sums(2)
+        project(7, 1)
+        widen(pieces[5], 1, on_scalar=True)
+        x_out(2, 1, 1, on_scalar=False)
+        project(9, 0)
+        widen(pieces[5], 2, on_scalar=True)
+        second_factor(4)
+        first_factor(7)
+        second_factor(5)
+        widen(pieces[6], 0, on_scalar=True)
+        second_factor(6)
+        first_factor(8)
+        x_quant(2, 1)
+        project(4, 2)
+        widen(pieces[6], 1, on_scalar=True)
+        widen(pieces[5], 3, on_scalar=False)
+        w_quant(4)
+        w_weave(5, on_gpsimd=True)
+        wo_right_weave(0)
 
-        first_step = 2
-        last_step = wide + LAG - 1
-        behind = {s: [] for s in range(first_step, last_step + 1)}
+        planes_left = [(piece, j) for piece in pieces[6:] for j in range(PACK)][2:]
+        shared = (7, 8)
+        planes_left = [(piece, j) for piece, j in planes_left if j < PACK - 1 or pieces.index(piece) not in shared]
+        planes_at = {s: [] for s in range(first_step, last_step + 1)}
+        for i, plane in enumerate(planes_left):
+            planes_at[first_step + (last_step - first_step) * i // len(planes_left)].append(plane)
+        summed, z_due = list(range(R)), [halves[0]]
 
-        def after(s, fn, *args):
-            behind[s].append((fn, args))
-
-        for u in range(0, wide, 2):
-            after(u + 1 + LAG, rank_sums, u)
-        for i, g in enumerate(halves[:-1]):
-            after(R * (i + 1) + LAG, z_out, g)
-        shared = (pieces[7], PACK - 1)
-        planes_left = [(piece, j) for piece in pieces[4:] for j in range(PACK) if (piece, j) != shared][2:]
-        late_planes = len(planes_left) - EARLY_PLANES
-        late_steps = last_step - TURN - (first_step + 4)
-        for i, (piece, j) in enumerate(planes_left):
-            if i < EARLY_PLANES:
-                after(first_step + 4 * i // EARLY_PLANES, widen, piece, j, True)
-            else:
-                after(first_step + 4 + late_steps * (i - EARLY_PLANES) // late_planes, widen, piece, j, True)
-        turns = [first_step + 1] + list(range(last_step, first_step + 2, -TURN))[::-1]
-        after(first_step, x_turn, 2, 1)
-        after(turns[0], x_quant, 1, 1)
-        after(turns[1], x_quant, 2, 1)
-        for i, s in enumerate(turns[:-EARLY_TURNS]):
-            if pieces[4 + i] == shared[0]:
-                after(s, widen, *shared, False)
-            after(s, w_quant, pieces[3 + i])
-            after(s, w_weave, pieces[4 + i], True)
-        in_middle = {s: len(pieces) - EARLY_TURNS + i for i, s in enumerate(turns[-EARLY_TURNS:])}
-        held_back = [(R, 1), (wide, 2)]
-        after(R - 1, project, R, 1)
-        after(turns[0], x_out, 2, 1, 1, False)
-        after(turns[-2], wo_left_weave, 0)
-        after(last_step - 1, wo_left_weave, 1)
+        def turn(i):
+            if i + 1 in shared:
+                widen(pieces[i + 1], PACK - 1, on_scalar=False)
+            w_quant(i)
+            through = [u for u in p_of if u not in summed]
+            rank_sums(through[0], count=len(through))
+            summed.extend(through)
+            z_due.extend(units[u][0] for u in through if units[u][1] == [R - 1])
+            w_weave(i + 1, on_gpsimd=True)
+            if i + 1 in with_slice:
+                wo_right_weave(with_slice.index(i + 1))
 
         for s in range(first_step, last_step + 1):
             first_factor(s + LEAD)
-            if s >= LAG:
+            for g in z_due:
+                z_out(g)
+            z_due.clear()
+            if s == first_step:
+                second_factor(s)
                 third_factor(s - LAG)
-            if s == turns[0]:
-                x_out(2, 1, 0, on_scalar=True)
-            if s in in_middle:
-                w_quant(pieces[in_middle[s]])
-                if s < last_step:
-                    w_weave(pieces[in_middle[s] + 1], on_gpsimd=True)
-                else:
-                    wo_right_weave()
-            second_factor(s)
+            else:
+                third_factor(s - LAG)
+                if 2 * s in turn_at:
+                    turn(turn_at[2 * s])
+                second_factor(s)
             for u, m in ((s + 1 - LAG, 2), (s + 1 + LEAD, 0), (s + 1, 1)):
-                if (u, m) not in h_of and (u, m) not in held_back:
+                if (u, m) not in h_of and (u, m) != (last_step + 1, 1):
                     project(u, m)
-            for fn, args in behind[s]:
-                fn(*args)
+            for piece, j in planes_at[s]:
+                widen(piece, j, on_scalar=True)
+            if s == last_step:
+                project(s + 2 - LAG, 2)
+            if 2 * s + 1 in turn_at:
+                turn(turn_at[2 * s + 1])
 
-        u = list(range(wide, len(units)))
-        project(u[0], 2)
-        project(u[1], 2)
-        z_out(halves[-1])
-        first_factor(u[5])
-        second_factor(u[3])
-        project(u[2], 2)
-        project(u[3], 2)
-        third_factor(u[0])
-        project(u[4], 1)
-        third_factor(u[1])
-        project(u[6], 0)
-        rank_sums(u[0])
-        third_factor(u[2])
-        project(u[5], 1)
+        project(24, 1)
+        first_factor(26)
+        project(27, 0)
+        project(25, 1)
+        project(28, 0)
+        third_factor(21)
+        project(23, 2)
+        z_out(halves[4])
+        project(28, 1)
+        third_factor(22)
+        project(26, 1)
+        first_factor(27)
+        project(29, 0)
+        second_factor(24)
+        project(29, 1)
+        first_factor(28)
+        project(30, 0)
+        second_factor(25)
+        second_out(28)
+        third_factor(23)
+        first_factor(29)
+        w_quant(11, 0, 2 * P)
+        w_quant(11, 2 * P, 2 * P)
+        project(24, 2)
+        project(25, 2)
+        project(30, 1)
+        project(27, 1)
+        second_times(28, "grouped3")
+        second_out(29)
+        project(26, 2)
+        second_times(29, "grouped1")
+        second_factor(26)
+        project(27, 2)
+        first_factor(30)
+        third_factor(24)
+        second_out(30)
+        second_times(30, "second_30")
+        third_factor(25)
+        rank_sums(24)
+        project(28, 2)
+        project(31, 0)
+        project(31, 1)
+        wo_left_weave(0)
+        second_factor(27)
+        project(29, 2)
         z_out(quarters[0])
-        first_factor(u[6])
-        third_factor(u[3])
-        project(u[7], 0)
-        project(u[4], 2)
         z_turn(0)
-        rank_sums(u[2])
-        second_factor(u[4])
-        for side in range(2):
-            wo_quant(side)
+        third_factor(26)
+        wo_left_weave(1)
+        third_factor(27)
+        rank_sums(26)
+        rank_sums(21, count=3)
         z_turn_out(0)
+        third_factor(28)
         z_out(quarters[1])
-        first_factor(u[7])
-        project(u[5], 2)
-        second_factor(u[5])
-        project(u[6], 1)
-        z_quant(0)
-        third_factor(u[4])
-        out_product(0, 0, z_bank)
         z_turn(1)
-        project(u[7], 1)
+        wo_quant(1)
+        first_factor(31)
+        z_quant(0)
+        out_product(0, 2)
+        out_product(0, 3)
+        project(30, 2)
+        second_out(31)
+        second_times(31, "z_grouped0")
+        wo_quant(0)
+        z_out(halves[5])
+        third_factor(29)
+        rank_sums(28)
+        out_product(0, 0)
         out_product(0, 1)
-        y_out(0, 0)
-        add_bo(0, 0, "first_add")
+        project(31, 2)
         z_turn_out(1)
-        third_factor(u[5])
-        project(u[6], 2)
-        out_product(0, 2, z_bank)
-        second_factor(u[6])
-        rank_sums(u[4])
-        project(u[7], 2)
-        y_out(0, 2)
+        finish(0, 2)
+        y_out(0, 0)
+        finish(0, 3)
         z_out(quarters[2])
-        second_factor(u[7])
-        finish(0, 1)
+        third_factor(30)
         z_quant(1)
-        add_bo(0, 2, "z_grouped1")
-        store(0, 0)
-        out_product(0, 3, z_bank)
-        third_factor(u[6])
-        z_turn(2)
         out_product(1, 0)
         out_product(1, 1)
-        third_factor(u[7])
+        z_turn(2)
+        add_bo(0, 0, "z_grouped1")
         z_turn_out(2)
-        y_out(1, 1)
-        rank_sums(u[6])
-        finish(0, 3)
-        out_product(1, 2, z_bank)
+        finish(0, 1)
+        third_factor(31)
+        rank_sums(30, split=True)
+        out_product(1, 2)
         out_product(1, 3)
+        z_out(last_tiles[0])
         finish(1, 0)
-        z_out(quarters[3])
-        store(0, 2)
+        store(0, 0)
+        z_out(last_tiles[1])
+        finish(1, 1)
         z_quant(2)
-        add_bo(1, 1, "z_grouped2")
         out_product(2, 0)
-        out_product(2, 1)
-        z_turn(3)
-        finish(1, 2)
-        y_out(2, 1)
-        z_turn_out(3)
-        finish(1, 3)
+        z_turn(3, 0, 1)
+        z_turn(3, 1, 1)
         out_product(2, 2)
-        out_product(2, 3, z_bank)
+        out_product(2, 1)
+        out_product(2, 3)
+        z_turn_out(3, 0, 1)
+        finish(1, 2)
+        z_turn_out(3, 1, 1)
+        finish(1, 3)
+        y_out(2, 1)
         finish(2, 0)
-        store(1, 1)
+        z_quant(3, 0)
+        out_product(3, 0)
+        out_product(3, 2)
         finish(2, 2)
-        z_quant(3)
-        add_bo(2, 1, "z_grouped3")
-        for i in range(4):
-            out_product(3, i)
+        z_quant(3, 1)
+        out_product(3, 1)
+        out_product(3, 3)
+        add_bo(2, 1, "z_grouped4")
         finish(2, 3)
         finish(3, 0)
-        finish(3, 1)
-        store(2, 1)
         finish(3, 2)
+        store(2, 1)
+        finish(3, 1)
         finish(3, 3)

from contextlib import ExitStack

import concourse.mybir as mybir
from concourse.masks import make_identity

F32 = mybir.dt.float32
BF16 = mybir.dt.bfloat16
U32 = mybir.dt.uint32
U8 = mybir.dt.uint8
FP8 = mybir.dt.float8_e4m3fn
FP8X4 = mybir.dt.float8_e4m3fn_x4
ACT = mybir.ActivationFunctionType
ALU = mybir.AluOpType

M, N, D, R, F, H = 3, 1024, 512, 4, 512, 1024
FLOPS = 2 * M * N * D * R * F + 2 * N * F * H

P = 128
PACK = 4
HALF = 512
TILES = F // P
BANK = 512
BANKS = 8
LEAD = 2
LAG = 3
RUN = 4


def tile_lowranktrimodalfusion_kernel(tc, x, w_bytes, w_scale, b, omega, wo, bo, out):
    nc = tc.nc
    with ExitStack() as ctx:
        keep = ctx.enter_context(tc.tile_pool(name="keep", bufs=1))
        stage = ctx.enter_context(tc.tile_pool(name="stage", bufs=1))
        psum = ctx.enter_context(tc.psum_pool(name="psum", bufs=1))
        ctx.enter_context(tc.manual_schedule())

        free_banks = list(range(BANKS))
        bank_of = {}

        def bank(key, shape):
            bank_of[key] = free_banks.pop(0)
            t = psum.tile(shape, F32, name="bank%d" % bank_of[key])
            return t

        def release(key):
            free_banks.append(bank_of[key])

        ws = keep.tile([P, PACK], F32, name="ws")
        vec = keep.tile([P, P], BF16, name="vec")
        vec32 = keep.tile([P, P], F32, name="vec32")
        ident = keep.tile([P, P], F32, name="ident")
        nc.scalar.dma_start(out=ws[:], in_=w_scale.rearrange("a (p j) o -> p (a j o)", j=PACK))
        nc.scalar.dma_start(out=vec[48:64, :], in_=omega.rearrange("r (c f) -> (r c) f", f=P))
        nc.scalar.dma_start(out=vec[0:48, :], in_=b.rearrange("m (q f) -> (m q) f", f=P))
        make_identity(nc, ident[:])
        nc.scalar.activation(out=vec32[64:128, :], in_=ident[64:128, :], func=ACT.Copy, scale=0.0)

        pieces = [(c, m) for c in range(TILES) for m in range(M)]
        first_raw, w_raw, x_raw, planes = {}, {}, {}, {}
        for part in range(2):
            t = keep.tile([P, 2, R * P], U8, name="first_raw%d" % part)
            first_raw[part] = t
        for m in range(M):
            for half in range(2):
                t = keep.tile([P, 4, D], BF16, name="x_raw%d%d" % (m, half))
                x_raw[m, half] = t
        wo_raw = keep.tile([P, PACK, H], BF16, name="wo_raw")
        bo_sb = keep.tile([P, H], BF16, name="bo_sb")

        def load_w(i):
            c, m = pieces[i]
            src = w_bytes[m].rearrange("(p j) (r f) -> p (j r) f", j=PACK, r=R)[:, :, c * P : (c + 1) * P]
            if i == 0:
                for part in range(2):
                    rows = slice(2 * R * part, 2 * R * (part + 1))
                    nc.sync.dma_start(out=first_raw[part][:].rearrange("p j (r f) -> p (j r) f", r=R), in_=src[:, rows, :])
            else:
                t = keep.tile([P, PACK, R * P], U8, name="w_raw%d%d" % (c, m))
                w_raw[c, m] = t
                nc.sync.dma_start(out=t[:].rearrange("p j (r f) -> p (j r) f", r=R), in_=src)

        def load_x(m, half):
            src = x[m].rearrange("(p a) k -> p a k", a=8)
            nc.sync.dma_start(out=x_raw[m, half][:], in_=src[:, 4 * half : 4 * half + 4, :])

        def planes_of(piece):
            if piece not in planes:
                t = stage.tile([P, PACK, R * P], BF16, name="planes", align_bytes=64, bufs=5)
                planes[piece] = t
            return planes[piece]

        for i in range(2 * M):
            load_w(i)
            load_x(i % M, i // M)
        for i in range(2 * M, len(pieces)):
            load_w(i)
            if i == 7:
                nc.sync.dma_start(out=wo_raw[:], in_=wo.rearrange("(p j) n -> p j n", j=PACK))
        nc.sync.dma_start(out=bo_sb[:], in_=bo.partition_broadcast(P))

        def mx_operand(name, width):
            codes = keep.tile([P, width], U32, name=name + "_codes", align_bytes=64)
            scales = keep.tile([P, width], U8, name=name + "_scales", align_bytes=64)
            return codes, scales

        def quantize(operand, src, first=0):
            cols = slice(first, first + src.shape[1])
            nc.vector.quantize_mx(
                out=operand[0][:, cols].bitcast(FP8X4), scales=operand[1][:, cols], in_=src.rearrange("p n j -> p (n j)")
            )

        def grouped(slot):
            t = stage.tile([P, BANK, PACK], BF16, name="grouped%d" % slot, align_bytes=64, bufs=1)
            return t

        def product(dst, lhs, lhs_from, rhs, rhs_from, width):
            lcols, rcols = slice(lhs_from, lhs_from + P), slice(rhs_from, rhs_from + width)
            nc.tensor.matmul_mx(
                out=dst,
                lhsT=lhs[0][:, lcols].bitcast(FP8X4),
                lhsT_scale=lhs[1][:, lcols],
                rhs=rhs[0][:, rcols].bitcast(FP8X4),
                rhs_scale=rhs[1][:, rcols],
                start=True,
                stop=True,
            )

        xq = {(m, half): mx_operand("x%d%d" % (m, half), HALF) for m in range(M) for half in range(2)}
        x_turned, x_grouped = {}, {}
        x_slot = ((0, 1, 2), (0, 2, 3))

        def x_turn(m, half):
            words = x_raw[m, half][:].rearrange("p a k -> p (a k)").bitcast(F32)
            for pair in range(2):
                t = bank(("x", m, half, pair), [P, 2, 2, P])
                for i in range(2):
                    base = (2 * pair + i) * (D // 2)
                    for u in range(2):
                        nc.tensor.transpose(t[:, i, u, :], words[:, base + u : base + D // 2 : 2], ident[:])
                x_turned[m, half, pair] = t

        def x_out(m, half, pair, on_scalar):
            if (m, half) not in x_grouped:
                x_grouped[m, half] = grouped(x_slot[half][m])
            dst = x_grouped[m, half][:].rearrange("p n j -> p (n j)").bitcast(F32)
            dst = dst[:, pair * BANK : (pair + 1) * BANK].rearrange("p (a r u) -> p a r u", a=2, u=2)
            src = x_turned[m, half, pair][:].rearrange("p a u r -> p a r u")
            if on_scalar:
                nc.scalar.copy(out=dst, in_=src)
            else:
                nc.vector.tensor_copy(out=dst, in_=src)
            release(("x", m, half, pair))

        def x_quant(m, half):
            quantize(xq[m, half], x_grouped[m, half][:])

        wq = {piece: mx_operand("w%d%d" % piece, R * P) for piece in pieces}
        woq = mx_operand("wo", H)
        woven = {}
        w_slot = (3, 3, 1, 0) + tuple((1, 3, 0)[i % 3] for i in range(8))

        def widen(piece, j, on_scalar):
            raw = first_raw[j // 2][:, j % 2, :] if piece == pieces[0] else w_raw[piece][:, j, :]
            dst, src = planes_of(piece)[:, j, :], raw.bitcast(FP8)
            if on_scalar:
                nc.scalar.activation(out=dst, in_=src, func=ACT.Copy, scale=ws[:, j : j + 1])
            else:
                nc.vector.tensor_scalar(out=dst, in0=src, scalar1=ws[:, j : j + 1], scalar2=None, op0=ALU.mult)

        def in_runs(dst, src):
            return dst.rearrange("p (c i) j -> p c j i", i=RUN), src.rearrange("p j (c i) -> p c j i", i=RUN)

        def weave(dst, src, on_gpsimd):
            to, of = in_runs(dst, src)
            if on_gpsimd:
                nc.gpsimd.tensor_scalar(out=to, in0=of, scalar1=1.0, scalar2=0.0, op0=ALU.mult, op1=ALU.add)
            else:
                nc.vector.tensor_copy(out=to, in_=of)

        def w_weave(i, on_gpsimd):
            t = grouped(w_slot[i])
            woven[i] = t
            weave(t[:], planes[pieces[i]][:], on_gpsimd)

        def w_quant(i, first=0, width=R * P):
            quantize(wq[pieces[i]], woven[i][:, first : first + width, :], first)

        def wo_right_weave(s):
            if s == 0:
                woven["wo", 1] = grouped(2)
            weave(woven["wo", 1][:, s * P : (s + 1) * P, :], wo_raw[:, :, BANK + s * P : BANK + (s + 1) * P], True)

        def wo_left_weave(part):
            if part == 0:
                woven["wo", 0] = grouped(0)
            cs = slice(part * BANK // 2, (part + 1) * BANK // 2)
            to, of = in_runs(woven["wo", 0][:, cs, :], wo_raw[:, :, cs])
            nc.scalar.copy(out=to, in_=of)

        def wo_quant(side):
            quantize(woq, woven["wo", side][:], side * BANK)

        cols = keep.tile([P, 64], F32, name="cols")
        omega_b0 = keep.tile([P, 16], F32, name="omega_b0")

        vec_turned = {}

        def vec_widen():
            nc.scalar.copy(out=vec32[0:64, :], in_=vec[0:64, :])

        def vec_turn():
            vec_turned[0] = bank("vec", [P, P])
            nc.tensor.transpose(vec_turned[0][:], vec32[:], ident[:])

        def vec_cols():
            nc.scalar.copy(out=cols[:], in_=vec_turned[0][:, 0:64])

        def vec_bias():
            nc.vector.tensor_tensor(out=omega_b0[:], in0=vec_turned[0][:, 48:64], in1=cols[:, 0:16], op=ALU.mult)
            release("vec")

        def warm_up(n):
            t = bank("warm", [P, BANK])
            for i in range(n):
                nc.tensor.matmul(t[:], lhsT=x_raw[0, 0][:, 0, 0:P], rhs=x_raw[0, 0][:, 1, :], start=True, stop=True)
            release("warm")

        def column(tile, row, r, c):
            q = 16 * row + 4 * r + c
            return tile[:, q : q + 1]

        halves = [(c, half, 0, 4) for c in range(TILES - 1) for half in range(2)]
        quarters = [(TILES - 1, q // 2, 2 * (q % 2), 2) for q in range(4)]
        units = [(g, [r]) for g in halves for r in range(R)] + [(g, [r, r + 1]) for g in quarters for r in (0, 2)]
        last_tiles = [(TILES - 1, 1, 2 + a, 1) for a in range(2)]
        h_of, a_of, b_of, ab_of, p_of, z_sum, z_rows = {}, {}, {}, {}, {}, {}, {}
        for half in range(2):
            t = keep.tile([P, 4, F], BF16, name="z_rows%d" % half)
            z_rows[half] = t

        first_step, last_step = 7, 23
        turn_at, reads = {}, 2 * first_step - 1
        with_slice = [5, 6, 9, 10]
        for i in range(5, 11):
            reads = reads + (6 if i in with_slice else 5)
            turn_at[reads] = i
        holds_back = {reads // 2: i + 1 for reads, i in turn_at.items() if reads % 2 == 1}

        def parts(u):
            g, ranks = units[u]
            width = g[3] * P
            return [(r, slice(i * width, (i + 1) * width)) for i, r in enumerate(ranks)]

        def project(u, m):
            c, half, a0, na = units[u][0]
            h = bank((u, m), [P, BANK])
            h_of[u, m] = h
            for r, cs in parts(u):
                product(h[:, cs], wq[c, m], r * P, xq[m, half], a0 * P, na * P)

        def first_factor(u):
            c = units[u][0][0]
            if u in holds_back:
                a = stage.tile([P, BANK], F32, name="grouped%d" % w_slot[holds_back[u]], align_bytes=64, bufs=1)
            else:
                a = stage.tile([P, BANK], F32, name="a", bufs=LEAD + 4)
            a_of[u] = a
            for r, cs in parts(u):
                nc.scalar.activation(
                    out=a[:, cs], in_=h_of[u, 0][:, cs], func=ACT.Identity, scale=column(cols, M, r, c), bias=column(omega_b0, 0, r, c)
                )
            release((u, 0))

        def times_factor(dst, u, m, so_far):
            c = units[u][0][0]
            for r, cs in parts(u):
                nc.vector.scalar_tensor_tensor(
                    out=dst[:, cs], in0=h_of[u, m][:, cs], scalar=column(cols, m, r, c), in1=so_far[:, cs], op0=ALU.add, op1=ALU.mult
                )
            release((u, m))

        def second_factor(u):
            ab = stage.tile([P, BANK], F32, name="ab", bufs=LAG + 2)
            ab_of[u] = ab
            times_factor(ab, u, 1, a_of[u])

        def second_out(u):
            c = units[u][0][0]
            t = stage.tile([P, BANK], F32, name="for_gpsimd", bufs=4)
            b_of[u] = t
            for r, cs in parts(u):
                nc.scalar.activation(out=t[:, cs], in_=h_of[u, 1][:, cs], func=ACT.Identity, bias=column(cols, 1, r, c))
            release((u, 1))

        def second_times(u, buffer):
            ab = stage.tile([P, BANK], F32, name=buffer, align_bytes=64, bufs=1)
            ab_of[u] = ab
            nc.gpsimd.tensor_tensor(out=ab[:], in0=a_of[u][:], in1=b_of[u][:], op=ALU.mult)

        def third_factor(u):
            p = stage.tile([P, BANK], F32, name="p", bufs=10)
            p_of[u] = p
            times_factor(p, u, 2, ab_of[u])

        def rank_sums(first, split=False, count=2):
            for u in range(first, first + count):
                g, ranks = units[u]
                c, half, a0, na = g
                sums = [(c, half, a0 + a, 1) for a in range(na)] if split else [g]
                for s in sums:
                    if ranks[0] == 0:
                        z_sum[s] = bank(s, [P, s[3], P])
                    for i, r in enumerate(ranks):
                        for a in range(s[3]):
                            col = (i * na + s[2] - a0 + a) * P
                            nc.tensor.matmul(
                                z_sum[s][:, a, :], lhsT=p_of[u][:, col : col + P], rhs=ident[:], is_transpose=True,
                                start=r == 0 and a == 0, stop=r == R - 1 and a == s[3] - 1,
                            )

        def z_out(g):
            c, half, a0, na = g
            dst = z_rows[half][:, a0 : a0 + na, :].rearrange("p a (u q) -> p a u q", u=2)[:, :, :, 64 * c : 64 * c + 64]
            nc.scalar.copy(
                out=dst.rearrange("p a u (q e) -> p a u q e", e=2),
                in_=z_sum[g][:].rearrange("p a (q u e) -> p a u q e", u=2, e=2),
            )
            release(g)

        zq = [mx_operand("z%d" % q, 2 * P) for q in range(4)]
        z_turned, z_grouped, y_of, y_sb, o_of = {}, {}, {}, {}, {}
        out_rows = out.rearrange("(p a) h -> p a h", a=8)

        def side_cols(i):
            return slice(i // 2 * BANK, (i // 2 + 1) * BANK)

        def z_turn(q, a=0, n=2):
            t = bank(("z", q, a), [P, n, 2, P])
            words = z_rows[q // 2][:].rearrange("p a k -> p (a k)").bitcast(F32)
            for i in range(2 * n):
                base = (4 * (q % 2) + 2 * a + i) * P
                nc.tensor.transpose(t[:, i // 2, i % 2, :], words[:, base : base + P], ident[:])
            z_turned[q, a] = t

        def z_turn_out(q, a=0, n=2):
            g = stage.tile([P, n * P, PACK], BF16, name="z_grouped%d" % (q + a), align_bytes=64, bufs=1)
            z_grouped[q, a] = g
            dst = g[:].rearrange("p n j -> p (n j)").bitcast(F32).rearrange("p (a r u) -> p a r u", r=P, u=2)
            nc.scalar.copy(out=dst, in_=z_turned[q, a][:].rearrange("p a u r -> p a r u"))
            release(("z", q, a))

        def z_quant(q, a=0):
            quantize(zq[q], z_grouped[q, a][:], a * P)

        def out_product(q, i):
            y = bank(("y", q, i), [P, BANK])
            product(y[:], zq[q], i % 2 * P, woq, i // 2 * BANK, BANK)
            y_of[q, i] = y

        def store(q, i):
            nc.sync.dma_start(out=out_rows[:, 2 * q + i % 2, side_cols(i)], in_=o_of[q, i][:])

        def finish(q, i):
            o = stage.tile([P, BANK], F32, name="o", bufs=8)
            o_of[q, i] = o
            nc.vector.tensor_tensor(out=o[:], in0=y_of[q, i][:], in1=bo_sb[:, side_cols(i)], op=ALU.add)
            release(("y", q, i))
            store(q, i)

        def y_out(q, i):
            y = stage.tile([P, BANK], F32, name="for_gpsimd", bufs=4)
            y_sb[q, i] = y
            nc.scalar.copy(out=y[:], in_=y_of[q, i][:])
            release(("y", q, i))

        def add_bo(q, i, buffer):
            o = stage.tile([P, BANK], F32, name=buffer, align_bytes=64, bufs=1)
            o_of[q, i] = o
            nc.gpsimd.tensor_tensor(out=o[:], in0=y_sb[q, i][:], in1=bo_sb[:, side_cols(i)], op=ALU.add)

        x_turn(0, 0)
        widen(pieces[0], 0, on_scalar=False)
        widen(pieces[0], 1, on_scalar=False)
        widen(pieces[0], 3, on_scalar=True)
        widen(pieces[0], 2, on_scalar=False)
        vec_widen()
        vec_turn()
        warm_up(3)
        x_turn(1, 0)
        w_weave(0, on_gpsimd=False)
        x_out(0, 0, 0, on_scalar=True)
        x_out(0, 0, 1, on_scalar=True)
        w_quant(0)
        widen(pieces[1], 3, on_scalar=True)
        widen(pieces[1], 0, on_scalar=False)
        widen(pieces[1], 1, on_scalar=False)
        vec_cols()
        widen(pieces[1], 2, on_scalar=False)
        x_quant(0, 0)
        project(0, 0)
        project(1, 0)
        warm_up(2)
        x_turn(2, 0)
        project(2, 0)
        vec_bias()
        w_weave(1, on_gpsimd=False)
        x_out(1, 0, 0, on_scalar=True)
        x_out(1, 0, 1, on_scalar=True)
        widen(pieces[2], 0, on_scalar=False)
        widen(pieces[2], 1, on_scalar=False)
        widen(pieces[2], 2, on_scalar=True)
        x_quant(1, 0)
        widen(pieces[2], 3, on_scalar=True)
        w_weave(2, on_gpsimd=True)
        w_quant(1)
        project(0, 1)
        project(1, 1)
        project(2, 1)
        first_factor(0)
        x_out(2, 0, 0, on_scalar=False)
        x_turn(0, 1)
        first_factor(1)
        project(3, 0)
        x_out(2, 0, 1, on_scalar=False)
        project(3, 1)
        first_factor(2)
        second_factor(0)
        x_turn(1, 1)
        widen(pieces[3], 0, on_scalar=True)
        second_factor(1)
        widen(pieces[3], 1, on_scalar=True)
        second_factor(2)
        x_out(0, 1, 0, on_scalar=True)
        x_quant(2, 0)
        x_out(0, 1, 1, on_scalar=True)
        widen(pieces[3], 3, on_scalar=False)
        widen(pieces[3], 2, on_scalar=True)
        x_quant(0, 1)
        project(4, 0)
        w_weave(3, on_gpsimd=True)
        first_factor(3)
        w_quant(2)
        project(0, 2)
        project(1, 2)
        project(2, 2)
        project(5, 0)
        widen(pieces[4], 0, on_scalar=True)
        second_factor(3)
        x_out(1, 1, 0, on_scalar=True)
        x_turn(2, 1)
        x_out(1, 1, 1, on_scalar=False)
        project(3, 2)
        first_factor(4)
        project(6, 0)
        third_factor(0)
        widen(pieces[4], 1, on_scalar=True)
        third_factor(1)
        widen(pieces[4], 2, on_scalar=True)
        third_factor(2)
        first_factor(5)
        x_quant(1, 1)
        project(4, 1)
        project(5, 1)
        rank_sums(0)
        project(7, 0)
        x_out(2, 1, 0, on_scalar=True)
        project(6, 1)
        widen(pieces[4], 3, on_scalar=False)
        w_weave(4, on_gpsimd=True)
        widen(pieces[5], 0, on_scalar=True)
        w_quant(3)
        first_factor(6)
        project(8, 0)
        third_factor(3)
        rank_sums(2)
        project(7, 1)
        widen(pieces[5], 1, on_scalar=True)
        x_out(2, 1, 1, on_scalar=False)
        project(9, 0)
        widen(pieces[5], 2, on_scalar=True)
        second_factor(4)
        first_factor(7)
        second_factor(5)
        widen(pieces[6], 0, on_scalar=True)
        second_factor(6)
        first_factor(8)
        x_quant(2, 1)
        project(4, 2)
        widen(pieces[6], 1, on_scalar=True)
        widen(pieces[5], 3, on_scalar=False)
        w_quant(4)
        w_weave(5, on_gpsimd=True)
        wo_right_weave(0)

        planes_left = [(piece, j) for piece in pieces[6:] for j in range(PACK)][2:]
        shared = (7, 8)
        planes_left = [(piece, j) for piece, j in planes_left if j < PACK - 1 or pieces.index(piece) not in shared]
        planes_at = {s: [] for s in range(first_step, last_step + 1)}
        for i, plane in enumerate(planes_left):
            planes_at[first_step + (last_step - first_step) * i // len(planes_left)].append(plane)
        summed, z_due = list(range(R)), [halves[0]]

        def turn(i):
            if i + 1 in shared:
                widen(pieces[i + 1], PACK - 1, on_scalar=False)
            w_quant(i)
            through = [u for u in p_of if u not in summed]
            rank_sums(through[0], count=len(through))
            summed.extend(through)
            z_due.extend(units[u][0] for u in through if units[u][1] == [R - 1])
            w_weave(i + 1, on_gpsimd=True)
            if i + 1 in with_slice:
                wo_right_weave(with_slice.index(i + 1))

        for s in range(first_step, last_step + 1):
            first_factor(s + LEAD)
            for g in z_due:
                z_out(g)
            z_due.clear()
            if s == first_step:
                second_factor(s)
                third_factor(s - LAG)
            else:
                third_factor(s - LAG)
                if 2 * s in turn_at:
                    turn(turn_at[2 * s])
                second_factor(s)
            for u, m in ((s + 1 - LAG, 2), (s + 1 + LEAD, 0), (s + 1, 1)):
                if (u, m) not in h_of and (u, m) != (last_step + 1, 1):
                    project(u, m)
            for piece, j in planes_at[s]:
                widen(piece, j, on_scalar=True)
            if s == last_step:
                project(s + 2 - LAG, 2)
            if 2 * s + 1 in turn_at:
                turn(turn_at[2 * s + 1])

        project(24, 1)
        first_factor(26)
        project(27, 0)
        project(25, 1)
        project(28, 0)
        third_factor(21)
        project(23, 2)
        z_out(halves[4])
        project(28, 1)
        third_factor(22)
        project(26, 1)
        first_factor(27)
        project(29, 0)
        second_factor(24)
        project(29, 1)
        first_factor(28)
        project(30, 0)
        second_factor(25)
        second_out(28)
        third_factor(23)
        first_factor(29)
        w_quant(11, 0, 2 * P)
        w_quant(11, 2 * P, 2 * P)
        project(24, 2)
        project(25, 2)
        project(30, 1)
        project(27, 1)
        second_times(28, "grouped3")
        second_out(29)
        project(26, 2)
        second_times(29, "grouped1")
        second_factor(26)
        project(27, 2)
        first_factor(30)
        third_factor(24)
        second_out(30)
        second_times(30, "second_30")
        third_factor(25)
        rank_sums(24)
        project(28, 2)
        project(31, 0)
        project(31, 1)
        wo_left_weave(0)
        second_factor(27)
        project(29, 2)
        z_out(quarters[0])
        z_turn(0)
        third_factor(26)
        wo_left_weave(1)
        third_factor(27)
        rank_sums(26)
        rank_sums(21, count=3)
        z_turn_out(0)
        third_factor(28)
        z_out(quarters[1])
        z_turn(1)
        wo_quant(1)
        first_factor(31)
        z_quant(0)
        out_product(0, 2)
        out_product(0, 3)
        project(30, 2)
        second_out(31)
        second_times(31, "z_grouped0")
        wo_quant(0)
        z_out(halves[5])
        third_factor(29)
        rank_sums(28)
        out_product(0, 0)
        out_product(0, 1)
        project(31, 2)
        z_turn_out(1)
        finish(0, 2)
        y_out(0, 0)
        finish(0, 3)
        z_out(quarters[2])
        third_factor(30)
        z_quant(1)
        out_product(1, 0)
        out_product(1, 1)
        z_turn(2)
        add_bo(0, 0, "z_grouped1")
        z_turn_out(2)
        finish(0, 1)
        third_factor(31)
        rank_sums(30, split=True)
        out_product(1, 2)
        out_product(1, 3)
        z_out(last_tiles[0])
        finish(1, 0)
        store(0, 0)
        z_out(last_tiles[1])
        finish(1, 1)
        z_quant(2)
        out_product(2, 0)
        z_turn(3, 0, 1)
        z_turn(3, 1, 1)
        out_product(2, 2)
        out_product(2, 1)
        out_product(2, 3)
        z_turn_out(3, 0, 1)
        finish(1, 2)
        z_turn_out(3, 1, 1)
        finish(1, 3)
        y_out(2, 1)
        finish(2, 0)
        z_quant(3, 0)
        out_product(3, 0)
        out_product(3, 2)
        finish(2, 2)
        z_quant(3, 1)
        out_product(3, 1)
        out_product(3, 3)
        add_bo(2, 1, "z_grouped4")
        finish(2, 3)
        finish(3, 0)
        finish(3, 2)
        store(2, 1)
        finish(3, 1)
        finish(3, 3)
